import numpy as np
import ml_dtypes


def mxq(x, axis, fmt="e4m3"):
    dtype, down = {"e4m3": (ml_dtypes.float8_e4m3fn, 7), "e5m2": (ml_dtypes.float8_e5m2, 14)}[fmt]
    v = np.moveaxis(np.asarray(x, np.float32).astype(ml_dtypes.bfloat16).astype(np.float64), axis, -1)
    blocks = v.reshape(v.shape[:-1] + (-1, 32))
    amax = np.abs(blocks).max(-1, keepdims=True)
    byte = np.maximum(np.where(amax > 0, np.frexp(amax)[1] - 1 + 127, 0) - down, 1)
    scale = np.exp2(byte - 127.0)
    codes = (blocks / scale).astype(np.float32).astype(dtype).astype(np.float64)
    return np.moveaxis((codes * scale).reshape(v.shape), -1, axis)


WIDE = False


def mx_kscale(k):
    if not WIDE:
        return np.ones(k)
    levels = np.array([24, -24, 12, -12, 0])
    if k % 512:
        return np.exp2(np.random.permutation(np.resize(levels, k // 32))).repeat(32)
    a = np.empty((k // 512, 16))
    for p in range(k // 512):
        a[p, :8] = np.random.permutation(np.resize(levels, 8))
        for g in range(8):
            far = levels[np.abs(levels - a[p, g]) >= 10]
            a[p, g + 8] = far[np.random.randint(len(far))]
    return np.exp2(a.ravel()).repeat(32)


def f64(x):
    return np.asarray(x).astype(np.float64)


def striped(idx):
    return np.tile(idx.reshape(-1, 16).T, (8, 1)).astype(np.uint16)


def unstriped(offs):
    return offs[:16].T.reshape(-1).astype(np.int64)


E2M1 = np.array([0.0, 0.5, 1.0, 1.5, 2.0, 3.0, 4.0, 6.0, -0.0, -0.5, -1.0, -1.5, -2.0, -3.0, -4.0, -6.0])


def pack_weight(w, fmt):
    k, n = w.shape
    w = f64(np.asarray(w, np.float32).astype(ml_dtypes.bfloat16)).reshape(k // 32, 32, n)
    amax = np.abs(w).max(1)
    if fmt == "e4m3":
        byte = np.frexp(amax)[1] - 1 + 127 - 7
    else:
        mant, ex = np.frexp(amax / 6.0)
        byte = np.where(mant > 0.5, ex, ex - 1) + 127
    byte = np.clip(np.where(amax > 0, byte, 1), 1, 254)
    scaled = (w * np.exp2(127.0 - byte)[:, None, :]).reshape(k, n).astype(np.float32)
    by_word = np.ascontiguousarray(scaled.reshape(k // 512, 128, 4, n).transpose(0, 1, 3, 2))
    if fmt == "e4m3":
        words = by_word.astype(ml_dtypes.float8_e4m3fn).view(np.uint8)
    else:
        c = by_word.astype(ml_dtypes.float4_e2m1fn).view(np.uint8) & 0xF
        words = (c[..., 0::2] | (c[..., 1::2] << 4)).reshape(k // 512, 128, 2 * n)
    return np.ascontiguousarray(words), np.ascontiguousarray(byte.astype(np.uint8).reshape(k // 512, 16, n))


def unpack_weight(words, scales, fmt):
    g, _, n = scales.shape
    words = np.ascontiguousarray(words).reshape(g, 128, n, -1)
    if fmt == "e4m3":
        vals = words.view(ml_dtypes.float8_e4m3fn).astype(np.float64)
    else:
        nib = np.empty((g, 128, n, 4), np.uint8)
        nib[..., 0::2] = words & 0xF
        nib[..., 1::2] = words >> 4
        vals = E2M1[nib]
    vals = vals * np.repeat(np.exp2(scales.astype(np.float64) - 127.0), 8, axis=1)[..., None]
    return vals.transpose(0, 1, 3, 2).reshape(g * 512, n)


K, R, N, T, J = 512, 1024, 512, 2048, 1024


def setup_inputs():
    n = np.random.standard_normal
    s = mx_kscale(K)[:, None]
    u = mx_kscale(R)[:, None]
    wd = n((R, N)) / np.sqrt(R) / u
    p_tab = pack_weight(n((K, T)) * s, "e4m3")
    p_wu = pack_weight(n((K, R)) / np.sqrt(K) / s, "e4m3")
    p_wd8 = pack_weight(wd[:512], "e4m3")
    p_wd4 = pack_weight(wd[512:], "e2m1")
    return {
        "tab_words": p_tab[0],
        "tab_scales": p_tab[1],
        "wu_words": p_wu[0],
        "wu_scales": p_wu[1],
        "sm": (np.random.uniform(0.5, 2.0, R) * u[:, 0]).astype(np.float32),
        "wd8_words": p_wd8[0],
        "wd8_scales": p_wd8[1],
        "wd4_words": p_wd4[0],
        "wd4_scales": p_wd4[1],
        "gT": (n((N, T))).astype(np.float32),
        "wgo": np.tile(np.random.uniform(0.5, 2.0, J), (128, 1)).astype(np.float32),
        "offs": striped(np.random.permutation(T)[:J]),
    }


def reference(tab_words, tab_scales, wu_words, wu_scales, sm, wd8_words, wd8_scales, wd4_words, wd4_scales, gT, wgo, offs):
    idx = unstriped(offs)
    tab_ = unpack_weight(tab_words, tab_scales, "e4m3")[:, idx]
    wu_ = unpack_weight(wu_words, wu_scales, "e4m3")
    a = wu_.T @ tab_
    h = f64(sm)[:, None] * (np.maximum(a, 0.0)) ** 2
    h_ = mxq(h, 0, "e4m3")
    wd8_ = unpack_weight(wd8_words, wd8_scales, "e4m3")
    wd4_ = unpack_weight(wd4_words, wd4_scales, "e2m1")
    y = wd8_.T @ h_[:512] + wd4_.T @ h_[512:]
    out = np.zeros((N, T))
    out[:, idx] = f64(wgo)[0] * (y * f64(gT)[:, idx])
    return out

@@ -1,0 +1,196 @@
+from contextlib import ExitStack
+
+import concourse.mybir as mybir
+
+K, R, N, T, J = 512, 1024, 512, 2048, 1024
+FLOPS = 2 * K * R * J + 2 * R * N * J
+
+F32 = mybir.dt.float32
+BF16 = mybir.dt.bfloat16
+I32 = mybir.dt.int32
+U32 = mybir.dt.uint32
+U16 = mybir.dt.uint16
+U8 = mybir.dt.uint8
+FP8X4 = mybir.dt.float8_e4m3fn_x4
+FP4X4 = mybir.dt.float4_e2m1fn_x4
+ALU = mybir.AluOpType
+ACT = mybir.ActivationFunctionType
+
+P = 128
+PACK = 4
+PASS = P * PACK
+CHUNK = 512
+N_CHUNKS = J // CHUNK
+R_PASSES = R // PASS
+N_TILES = N // P
+SQRT_FLOOR = 2.0 ** -116
+
+
+def tile_list_modp_relu2_mix_gate_kernel(
+    tc, tab_words, tab_scales, wu_words, wu_scales, sm, wd8_words, wd8_scales, wd4_words, wd4_scales, gT, wgo, offs, out
+):
+    nc = tc.nc
+    with ExitStack() as ctx:
+        keep = ctx.enter_context(tc.tile_pool(name="keep", bufs=1))
+        up_psum = ctx.enter_context(tc.psum_pool(name="up_psum", bufs=4))
+        down_psum = ctx.enter_context(tc.psum_pool(name="down_psum", bufs=4))
+
+        def tile(shape, dtype, name, on=None):
+            return keep.tile(shape, dtype, name=name, tag=on or name, align_bytes=64)
+
+        offsets = keep.tile([P, J // 16], U16, name="offsets")
+        tab_w = tile([P, T], I32, "tab_w")
+        tab_s = tile([P, T], U8, "tab_s")
+        wu_raw_w = tile([P, R], I32, "wu_raw_w")
+        wu_raw_s = tile([P, PASS], U8, "wu_raw_s")
+        wu_w = tile([P, R], I32, "wu_w")
+        wu_s = tile([P, PASS], U8, "wu_s")
+        sm_sb = tile([P, R_PASSES, PACK], F32, "sm_sb")
+
+        nc.vector.memset(wu_raw_s[:].bitcast(I32), 0)
+        nc.vector.memset(tab_s[:].bitcast(I32), 0)
+
+        nc.sync.dma_start(offsets[:], offs)
+        nc.sync.dma_start(sm_sb[:], sm.rearrange("(g p t) -> p g t", g=R_PASSES, t=PACK))
+        nc.sync.dma_start(wu_raw_w[:], wu_words[0].rearrange("p r i -> p (r i)").bitcast(I32))
+        nc.sync.dma_start(tab_w[:], tab_words[0].rearrange("p t i -> p (t i)").bitcast(I32))
+        for q in range(4):
+            nc.sync.dma_start(
+                wu_raw_s[32 * q : 32 * q + 8, :].bitcast(I32),
+                wu_scales[0].bitcast(I32)[4 * q : 4 * q + 4, :].rearrange("q (g c) -> g q c", g=R_PASSES),
+            )
+        for q in range(4):
+            nc.sync.dma_start(tab_s[32 * q : 32 * q + 4, :].bitcast(I32), tab_scales[0].bitcast(I32)[4 * q : 4 * q + 4, :])
+
+        sm_flat = sm_sb[:].rearrange("p g t -> p (g t)")
+        sm_abs = tile([P, R_PASSES * PACK], F32, "sm_abs")
+        sm_floor = tile([P, R_PASSES * PACK], F32, "sm_floor")
+        root0 = tile([P, R_PASSES * PACK], F32, "root0")
+        root_inv = tile([P, R_PASSES * PACK], F32, "root_inv")
+        half_quot = tile([P, R_PASSES * PACK], F32, "half_quot")
+        root = tile([P, R_PASSES * PACK], F32, "root")
+        nc.vector.scalar_tensor_tensor(sm_abs[:], sm_flat, -1.0, sm_flat, ALU.mult, ALU.max)
+        nc.vector.tensor_scalar_max(sm_floor[:], sm_abs[:], SQRT_FLOOR)
+        nc.scalar.activation(root0[:], sm_floor[:], ACT.Sqrt)
+        nc.vector.reciprocal(root_inv[:], root0[:])
+        nc.vector.scalar_tensor_tensor(half_quot[:], sm_floor[:], 0.5, root_inv[:], ALU.mult, ALU.mult)
+        nc.vector.scalar_tensor_tensor(root[:], root0[:], 0.5, half_quot[:], ALU.mult, ALU.add)
+        signs = [tile([P, CHUNK, PACK], BF16, f"signs{g}") for g in range(R_PASSES)]
+        for g in range(R_PASSES):
+            nc.scalar.activation(signs[g][:], sm_sb[:, g, :].unsqueeze(1).to_broadcast([P, CHUNK, PACK]), ACT.Sign)
+
+        nc.vector.tensor_copy(
+            wu_w[:].rearrange("p (g t m) -> p g m t", g=R_PASSES, t=PACK),
+            wu_raw_w[:].rearrange("p (g m t) -> p g m t", g=R_PASSES, t=PACK),
+        )
+        nc.vector.tensor_copy(
+            wu_s[:].rearrange("p (t m) -> p m t", t=PACK),
+            wu_raw_s[:].rearrange("p (m t) -> p m t", t=PACK),
+        )
+
+        cols = CHUNK // 16
+        picked_w = [tile([P, CHUNK], U32, f"picked_w{c}") for c in range(N_CHUNKS)]
+        picked_s = [tile([P, CHUNK], U8, f"picked_s{c}") for c in range(N_CHUNKS)]
+        lists = [offsets[:, c * cols : (c + 1) * cols] for c in range(N_CHUNKS)]
+        for c in range(N_CHUNKS):
+            nc.vector.tensor_copy(picked_w[c][:], tab_w[:].bitcast(U32).indirect(lists[c]))
+            nc.vector.tensor_copy(picked_s[c][:], tab_s[:].indirect(lists[c]))
+
+        gates = [tile([P, T], F32, f"gates{i}", on=("sm_abs", "root_inv", "half_quot", "wu_raw_w")[i]) for i in range(N_TILES)]
+        wgo_sb = tile([P, J], F32, "wgo_sb", on="root0")
+        wd8_w = tile([P, N], I32, "wd8_w", on="wu_raw_s")
+        wd4_w = tile([P, 2 * N], U8, "wd4_w", on="sm_floor")
+        wd_s = tile([P, N], U8, "wd_s")
+        nc.sync.dma_start(gates[0][:], gT[0:P, :])
+        nc.sync.dma_start(wgo_sb[:], wgo)
+        for i in range(1, N_TILES):
+            nc.sync.dma_start(gates[i][:], gT[i * P : (i + 1) * P, :])
+
+        pages = [tile([P, T], F32, f"page{i}", on=(None, None, "tab_w", "tab_s")[i]) for i in range(N_TILES)]
+        for i in range(N_TILES):
+            for half in range(2):
+                engine = nc.vector if i < 2 else nc.gpsimd
+                engine.memset(pages[i][:, half * (T // 2) : (half + 1) * (T // 2)], 0.0)
+
+        nc.vector.memset(wd_s[:].bitcast(I32), 0)
+        nc.sync.dma_start(wd8_w[:], wd8_words[0].rearrange("p n i -> p (n i)").bitcast(I32))
+        nc.sync.dma_start(wd4_w[:].bitcast(I32), wd4_words[0].bitcast(I32))
+        for q in range(4):
+            nc.sync.dma_start(wd_s[32 * q : 32 * q + 4, :].bitcast(I32), wd4_scales[0].bitcast(I32)[4 * q : 4 * q + 4, :])
+            nc.sync.dma_start(wd_s[32 * q + 4 : 32 * q + 8, :].bitcast(I32), wd8_scales[0].bitcast(I32)[4 * q : 4 * q + 4, :])
+
+        h_w = {}
+        h_s = {}
+        picked_g = {}
+
+        def hidden(c, g):
+            relu = tile([P, PACK, CHUNK], F32, f"relu{c}_{g}")
+            for t in range(PACK):
+                a = up_psum.tile([P, CHUNK], F32, name="a")
+                nc.tensor.matmul_mx(
+                    out=a[:],
+                    lhsT=wu_w[:, g * PASS + t * P : g * PASS + (t + 1) * P].bitcast(FP8X4),
+                    lhsT_scale=wu_s[4 * g : P, t * P : (t + 1) * P],
+                    rhs=picked_w[c][:].bitcast(FP8X4),
+                    rhs_scale=picked_s[c][:],
+                    start=True,
+                    stop=True,
+                )
+                nc.scalar.activation(relu[:, t, :], a[:], ACT.Relu, scale=root[:, g * PACK + t : g * PACK + t + 1])
+            h_abs = tile([P, CHUNK * PACK], BF16, f"h_abs{c}_{g}")
+            nc.scalar.activation(
+                h_abs[:].rearrange("p (c i t) -> p c t i", i=4, t=PACK),
+                relu[:].rearrange("p t (c i) -> p c t i", i=4),
+                ACT.Square,
+            )
+            h = tile([P, CHUNK * PACK], BF16, f"h{c}_{g}")
+            nc.vector.tensor_tensor(h[:], h_abs[:], signs[g][:].rearrange("p j t -> p (j t)"), ALU.mult)
+            h_w[c, g] = tile([P, CHUNK], U32, f"h_w{c}_{g}")
+            h_s[c, g] = tile([P, CHUNK], U8, f"h_s{c}_{g}")
+            nc.vector.quantize_mx(out=h_w[c, g][:].bitcast(FP8X4), scales=h_s[c, g][:], in_=h[:])
+
+        def gather_gates(c, i, dst):
+            picked_g[c, i] = dst
+            nc.vector.tensor_tensor(dst, gates[i][:].indirect(lists[c]), wgo_sb[:, c * CHUNK : (c + 1) * CHUNK], ALU.mult)
+
+        def down(c, i, y):
+            y_ps = down_psum.tile([P, CHUNK], F32, name="y_ps")
+            nc.tensor.matmul_mx(
+                out=y_ps[:],
+                lhsT=wd8_w[:, i * P : (i + 1) * P].bitcast(FP8X4),
+                lhsT_scale=wd_s[4:P, i * P : (i + 1) * P],
+                rhs=h_w[c, 0][:].bitcast(FP8X4),
+                rhs_scale=h_s[c, 0][:],
+                start=True,
+                stop=False,
+            )
+            nc.tensor.matmul_mx(
+                out=y_ps[:],
+                lhsT=wd4_w[:, 2 * i * P : 2 * (i + 1) * P].bitcast(FP4X4),
+                lhsT_scale=wd_s[:, i * P : (i + 1) * P],
+                rhs=h_w[c, 1][:].bitcast(FP8X4),
+                rhs_scale=h_s[c, 1][:],
+                start=False,
+                stop=True,
+            )
+            nc.scalar.copy(y, y_ps[:])
+            nc.vector.tensor_tensor(pages[i][:].indirect(lists[c]), y, picked_g[c, i], ALU.mult)
+            if c == N_CHUNKS - 1:
+                nc.sync.dma_start(out[i * P : (i + 1) * P, :], pages[i][:])
+
+        hidden(0, 0)
+        hidden(0, 1)
+        for c, i in ((0, 0), (1, 0), (0, 1), (1, 1), (0, 2), (0, 3)):
+            gather_gates(c, i, tile([P, CHUNK], F32, f"picked_g{c}_{i}")[:])
+        late_g = tile([P, 2, CHUNK], F32, "late_g", on="h0_1")
+        gather_gates(1, 2, late_g[:, 0, :])
+        gather_gates(1, 3, late_g[:, 1, :])
+        for i in range(2):
+            down(0, i, tile([P, CHUNK], F32, f"y0_{i}")[:])
+        hidden(1, 0)
+        hidden(1, 1)
+        late_y = tile([P, 2, CHUNK], F32, "late_y", on="relu1_1")
+        for i in range(2, N_TILES):
+            down(0, i, late_y[:, i - 2, :])
+        for i in range(N_TILES):
+            down(1, i, tile([P, CHUNK], F32, f"y1_{i}")[:])

@@ -1,6 +1,7 @@
 from contextlib import ExitStack
 
 import concourse.mybir as mybir
+from concourse.masks import make_identity
 
 K, R, N, T, J = 512, 1024, 512, 2048, 1024
 FLOPS = 2 * K * R * J + 2 * R * N * J
@@ -23,7 +24,7 @@ CHUNK = 512
 N_CHUNKS = J // CHUNK
 R_PASSES = R // PASS
 N_TILES = N // P
-SQRT_FLOOR = 2.0 ** -116
+SIGN_RUN = 16
 
 
 def tile_list_modp_relu2_mix_gate_kernel(
@@ -33,7 +34,8 @@ def tile_list_modp_relu2_mix_gate_kernel(
     with ExitStack() as ctx:
         keep = ctx.enter_context(tc.tile_pool(name="keep", bufs=1))
         up_psum = ctx.enter_context(tc.psum_pool(name="up_psum", bufs=4))
-        down_psum = ctx.enter_context(tc.psum_pool(name="down_psum", bufs=4))
+        down_psum = ctx.enter_context(tc.psum_pool(name="down_psum", bufs=2))
+        turn_psum = ctx.enter_context(tc.psum_pool(name="turn_psum", bufs=2))
 
         def tile(shape, dtype, name, on=None):
             return keep.tile(shape, dtype, name=name, tag=on or name, align_bytes=64)
@@ -47,38 +49,52 @@ def tile_list_modp_relu2_mix_gate_kernel(
         wu_s = tile([P, PASS], U8, "wu_s")
         sm_sb = tile([P, R_PASSES, PACK], F32, "sm_sb")
 
-        nc.vector.memset(wu_raw_s[:].bitcast(I32), 0)
         nc.vector.memset(tab_s[:].bitcast(I32), 0)
-
+        nc.vector.memset(wu_raw_s[:].bitcast(I32), 0)
         nc.sync.dma_start(offsets[:], offs)
         nc.sync.dma_start(sm_sb[:], sm.rearrange("(g p t) -> p g t", g=R_PASSES, t=PACK))
-        nc.sync.dma_start(wu_raw_w[:], wu_words[0].rearrange("p r i -> p (r i)").bitcast(I32))
         nc.sync.dma_start(tab_w[:], tab_words[0].rearrange("p t i -> p (t i)").bitcast(I32))
+        for q in range(4):
+            nc.sync.dma_start(tab_s[32 * q : 32 * q + 4, :].bitcast(I32), tab_scales[0].bitcast(I32)[4 * q : 4 * q + 4, :])
+        nc.sync.dma_start(wu_raw_w[:], wu_words[0].rearrange("p r i -> p (r i)").bitcast(I32))
         for q in range(4):
             nc.sync.dma_start(
                 wu_raw_s[32 * q : 32 * q + 8, :].bitcast(I32),
                 wu_scales[0].bitcast(I32)[4 * q : 4 * q + 4, :].rearrange("q (g c) -> g q c", g=R_PASSES),
             )
-        for q in range(4):
-            nc.sync.dma_start(tab_s[32 * q : 32 * q + 4, :].bitcast(I32), tab_scales[0].bitcast(I32)[4 * q : 4 * q + 4, :])
 
-        sm_flat = sm_sb[:].rearrange("p g t -> p (g t)")
-        sm_abs = tile([P, R_PASSES * PACK], F32, "sm_abs")
-        sm_floor = tile([P, R_PASSES * PACK], F32, "sm_floor")
-        root0 = tile([P, R_PASSES * PACK], F32, "root0")
-        root_inv = tile([P, R_PASSES * PACK], F32, "root_inv")
-        half_quot = tile([P, R_PASSES * PACK], F32, "half_quot")
+        pages = {}
+
+        def clear_page(i, engine, on=None):
+            pages[i] = tile([P, T], F32, f"page{i}", on=on)
+            for k in range(4):
+                engine.memset(pages[i][:, k * (T // 4) : (k + 1) * (T // 4)], 0.0)
+
+        wgo_rows = tile([P, P], F32, "wgo_rows")
+        nc.gpsimd.memset(wgo_rows[:], 0.0)
+        nc.gpsimd.dma_start(wgo_rows[0 : CHUNK // P, :], wgo[0, CHUNK:].rearrange("(b m) -> b m", m=P))
+        identity = tile([P, P], F32, "identity")
+        make_identity(nc, identity[:])
         root = tile([P, R_PASSES * PACK], F32, "root")
-        nc.vector.scalar_tensor_tensor(sm_abs[:], sm_flat, -1.0, sm_flat, ALU.mult, ALU.max)
-        nc.vector.tensor_scalar_max(sm_floor[:], sm_abs[:], SQRT_FLOOR)
-        nc.scalar.activation(root0[:], sm_floor[:], ACT.Sqrt)
-        nc.vector.reciprocal(root_inv[:], root0[:])
-        nc.vector.scalar_tensor_tensor(half_quot[:], sm_floor[:], 0.5, root_inv[:], ALU.mult, ALU.mult)
-        nc.vector.scalar_tensor_tensor(root[:], root0[:], 0.5, half_quot[:], ALU.mult, ALU.add)
-        signs = [tile([P, CHUNK, PACK], BF16, f"signs{g}") for g in range(R_PASSES)]
         for g in range(R_PASSES):
-            nc.scalar.activation(signs[g][:], sm_sb[:, g, :].unsqueeze(1).to_broadcast([P, CHUNK, PACK]), ACT.Sign)
+            sm_abs = tile([P, PACK], F32, f"sm_abs{g}")
+            nc.scalar.activation(sm_abs[:], sm_sb[:, g, :], ACT.Abs)
+            nc.scalar.activation(root[:, g * PACK : (g + 1) * PACK], sm_abs[:], ACT.Sqrt)
+        signs = tile([P, R_PASSES, SIGN_RUN, PACK], BF16, "signs")
+        for g in range(R_PASSES):
+            nc.scalar.activation(signs[:, g], sm_sb[:, g, :].unsqueeze(1).to_broadcast([P, SIGN_RUN, PACK]), ACT.Sign)
 
+        wgo_cols = tile([P, CHUNK // P], F32, "wgo_cols")
+        wgo_ps = turn_psum.tile([P, CHUNK], F32, name="y_ps")
+        nc.tensor.transpose(wgo_ps[:, 0:P], wgo_rows[:], identity[:])
+        nc.scalar.copy(wgo_cols[:], wgo_ps[:, 0 : CHUNK // P])
+
+        cols = CHUNK // 16
+        lists = [offsets[:, c * cols : (c + 1) * cols] for c in range(N_CHUNKS)]
+        picked_w = [tile([P, CHUNK], U32, "picked_w0")]
+        picked_s = [tile([P, CHUNK], U8, "picked_s0")]
+        nc.vector.tensor_copy(picked_w[0][:], tab_w[:].bitcast(U32).indirect(lists[0]))
+        nc.vector.tensor_copy(picked_s[0][:], tab_s[:].indirect(lists[0]))
         nc.vector.tensor_copy(
             wu_w[:].rearrange("p (g t m) -> p g m t", g=R_PASSES, t=PACK),
             wu_raw_w[:].rearrange("p (g m t) -> p g m t", g=R_PASSES, t=PACK),
@@ -87,41 +103,37 @@ def tile_list_modp_relu2_mix_gate_kernel(
             wu_s[:].rearrange("p (t m) -> p m t", t=PACK),
             wu_raw_s[:].rearrange("p (m t) -> p m t", t=PACK),
         )
+        picked_w.append(tile([P, CHUNK], U32, "picked_w1", on="wu_raw_s"))
+        picked_s.append(tile([P, CHUNK], U8, "picked_s1", on="wu_raw_w"))
+        nc.vector.tensor_copy(picked_w[1][:], tab_w[:].bitcast(U32).indirect(lists[1]))
+        nc.vector.tensor_copy(picked_s[1][:], tab_s[:].indirect(lists[1]))
+        clear_page(0, nc.vector)
+        clear_page(1, nc.vector)
 
-        cols = CHUNK // 16
-        picked_w = [tile([P, CHUNK], U32, f"picked_w{c}") for c in range(N_CHUNKS)]
-        picked_s = [tile([P, CHUNK], U8, f"picked_s{c}") for c in range(N_CHUNKS)]
-        lists = [offsets[:, c * cols : (c + 1) * cols] for c in range(N_CHUNKS)]
-        for c in range(N_CHUNKS):
-            nc.vector.tensor_copy(picked_w[c][:], tab_w[:].bitcast(U32).indirect(lists[c]))
-            nc.vector.tensor_copy(picked_s[c][:], tab_s[:].indirect(lists[c]))
-
-        gates = [tile([P, T], F32, f"gates{i}", on=("sm_abs", "root_inv", "half_quot", "wu_raw_w")[i]) for i in range(N_TILES)]
-        wgo_sb = tile([P, J], F32, "wgo_sb", on="root0")
-        wd8_w = tile([P, N], I32, "wd8_w", on="wu_raw_s")
-        wd4_w = tile([P, 2 * N], U8, "wd4_w", on="sm_floor")
-        wd_s = tile([P, N], U8, "wd_s")
+        gates = [tile([P, T], F32, f"gates{i}", on=("sm_abs0", "sm_sb", "wgo_rows", "tab_w")[i]) for i in range(N_TILES)]
+        wgo_sb = tile([P, CHUNK], F32, "wgo_sb", on="sm_abs1")
         nc.sync.dma_start(gates[0][:], gT[0:P, :])
-        nc.sync.dma_start(wgo_sb[:], wgo)
+        nc.sync.dma_start(wgo_sb[:], wgo[:, 0:CHUNK])
         for i in range(1, N_TILES):
             nc.sync.dma_start(gates[i][:], gT[i * P : (i + 1) * P, :])
 
-        pages = [tile([P, T], F32, f"page{i}", on=(None, None, "tab_w", "tab_s")[i]) for i in range(N_TILES)]
-        for i in range(N_TILES):
-            for half in range(2):
-                engine = nc.vector if i < 2 else nc.gpsimd
-                engine.memset(pages[i][:, half * (T // 2) : (half + 1) * (T // 2)], 0.0)
-
-        nc.vector.memset(wd_s[:].bitcast(I32), 0)
-        nc.sync.dma_start(wd8_w[:], wd8_words[0].rearrange("p n i -> p (n i)").bitcast(I32))
-        nc.sync.dma_start(wd4_w[:].bitcast(I32), wd4_words[0].bitcast(I32))
+        wd = tile([P, N + N // 2 + N // 4], I32, "wd", on="tab_s")
+        wd_w = wd[:, 0 : N + N // 2]
+        wd_s32 = wd[:, N + N // 2 :]
+        wd_s = wd_s32.bitcast(U8)
+        nc.vector.memset(wd_s32, 0)
+        nc.sync.dma_start(wd_w[:, 0:N], wd8_words[0].rearrange("p n i -> p (n i)").bitcast(I32))
+        nc.sync.dma_start(wd_w[:, N:], wd4_words[0].bitcast(I32))
         for q in range(4):
-            nc.sync.dma_start(wd_s[32 * q : 32 * q + 4, :].bitcast(I32), wd4_scales[0].bitcast(I32)[4 * q : 4 * q + 4, :])
-            nc.sync.dma_start(wd_s[32 * q + 4 : 32 * q + 8, :].bitcast(I32), wd8_scales[0].bitcast(I32)[4 * q : 4 * q + 4, :])
+            nc.sync.dma_start(wd_s32[32 * q : 32 * q + 4, :], wd4_scales[0].bitcast(I32)[4 * q : 4 * q + 4, :])
+            nc.sync.dma_start(wd_s32[32 * q + 4 : 32 * q + 8, :], wd8_scales[0].bitcast(I32)[4 * q : 4 * q + 4, :])
+        wd8_w = wd_w[:, 0:N]
+        wd4_w = wd_w[:, N:].bitcast(U8)
 
         h_w = {}
         h_s = {}
         picked_g = {}
+        yT = {}
 
         def hidden(c, g):
             relu = tile([P, PACK, CHUNK], F32, f"relu{c}_{g}")
@@ -144,17 +156,23 @@ def tile_list_modp_relu2_mix_gate_kernel(
                 ACT.Square,
             )
             h = tile([P, CHUNK * PACK], BF16, f"h{c}_{g}")
-            nc.vector.tensor_tensor(h[:], h_abs[:], signs[g][:].rearrange("p j t -> p (j t)"), ALU.mult)
+            nc.vector.tensor_tensor(
+                h[:].rearrange("p (a b) -> p a b", b=SIGN_RUN * PACK),
+                h_abs[:].rearrange("p (a b) -> p a b", b=SIGN_RUN * PACK),
+                signs[:, g].rearrange("p j t -> p (j t)").unsqueeze(1).to_broadcast([P, CHUNK // SIGN_RUN, SIGN_RUN * PACK]),
+                ALU.mult,
+            )
             h_w[c, g] = tile([P, CHUNK], U32, f"h_w{c}_{g}")
             h_s[c, g] = tile([P, CHUNK], U8, f"h_s{c}_{g}")
             nc.vector.quantize_mx(out=h_w[c, g][:].bitcast(FP8X4), scales=h_s[c, g][:], in_=h[:])
 
-        def gather_gates(c, i, dst):
-            picked_g[c, i] = dst
-            nc.vector.tensor_tensor(dst, gates[i][:].indirect(lists[c]), wgo_sb[:, c * CHUNK : (c + 1) * CHUNK], ALU.mult)
+        def scatter(c, i, y):
+            nc.vector.tensor_tensor(pages[i][:].indirect(lists[c]), y, picked_g[c, i], ALU.mult)
+            if c == N_CHUNKS - 1:
+                nc.sync.dma_start(out[i * P : (i + 1) * P, :], pages[i][:])
 
-        def down(c, i, y):
-            y_ps = down_psum.tile([P, CHUNK], F32, name="y_ps")
+        def down_by_rows(c, i, y):
+            y_ps = turn_psum.tile([P, CHUNK], F32, name="y_ps")
             nc.tensor.matmul_mx(
                 out=y_ps[:],
                 lhsT=wd8_w[:, i * P : (i + 1) * P].bitcast(FP8X4),
@@ -174,23 +192,59 @@ def tile_list_modp_relu2_mix_gate_kernel(
                 stop=True,
             )
             nc.scalar.copy(y, y_ps[:])
-            nc.vector.tensor_tensor(pages[i][:].indirect(lists[c]), y, picked_g[c, i], ALU.mult)
-            if c == N_CHUNKS - 1:
-                nc.sync.dma_start(out[i * P : (i + 1) * P, :], pages[i][:])
+            scatter(c, i, y)
+
+        def down_by_tokens(c):
+            for b in range(CHUNK // P):
+                tokens = slice(b * P, (b + 1) * P)
+                yT_ps = down_psum.tile([P, N], F32, name="yT_ps")
+                nc.tensor.matmul_mx(
+                    out=yT_ps[:],
+                    lhsT=h_w[c, 0][:, tokens].bitcast(FP8X4),
+                    lhsT_scale=h_s[c, 0][:, tokens],
+                    rhs=wd8_w.bitcast(FP8X4),
+                    rhs_scale=wd_s[4:P, :],
+                    start=True,
+                    stop=False,
+                )
+                nc.tensor.matmul_mx(
+                    out=yT_ps[:],
+                    lhsT=h_w[c, 1][:, tokens].bitcast(FP8X4),
+                    lhsT_scale=h_s[c, 1][:, tokens],
+                    rhs=wd4_w.bitcast(FP4X4),
+                    rhs_scale=wd_s,
+                    start=False,
+                    stop=True,
+                )
+                yT[b] = tile([P, N], F32, f"yT{b}")
+                nc.scalar.activation(yT[b][:], yT_ps[:], ACT.Copy, scale=wgo_cols[:, b : b + 1])
+
+        def turn_back(c, i):
+            y_ps = turn_psum.tile([P, CHUNK], F32, name="y_ps")
+            for b in range(CHUNK // P):
+                nc.tensor.transpose(y_ps[:, b * P : (b + 1) * P], yT[b][:, i * P : (i + 1) * P], identity[:])
+            y = tile([P, CHUNK], F32, f"y{c}_{i}")
+            nc.scalar.copy(y[:], y_ps[:])
+            scatter(c, i, y[:])
 
         hidden(0, 0)
         hidden(0, 1)
-        for c, i in ((0, 0), (1, 0), (0, 1), (1, 1), (0, 2), (0, 3)):
-            gather_gates(c, i, tile([P, CHUNK], F32, f"picked_g{c}_{i}")[:])
-        late_g = tile([P, 2, CHUNK], F32, "late_g", on="h0_1")
-        gather_gates(1, 2, late_g[:, 0, :])
-        gather_gates(1, 3, late_g[:, 1, :])
-        for i in range(2):
-            down(0, i, tile([P, CHUNK], F32, f"y0_{i}")[:])
+        for i in range(N_TILES):
+            picked_g[0, i] = tile([P, CHUNK], F32, f"picked_g0_{i}")[:]
+            nc.vector.tensor_tensor(picked_g[0, i], gates[i][:].indirect(lists[0]), wgo_sb[:], ALU.mult)
+        late_g = tile([P, N_TILES - 1, CHUNK], F32, "late_g", on="h0_1")
+        for i in range(N_TILES):
+            picked_g[1, i] = late_g[:, i - 1, :] if i else tile([P, CHUNK], F32, "picked_g1_0")[:]
+            nc.vector.tensor_copy(picked_g[1, i], gates[i][:].indirect(lists[1]))
+        down_by_rows(0, 0, tile([P, CHUNK], F32, "y0_0")[:])
+        down_by_rows(0, 1, tile([P, CHUNK], F32, "y0_1")[:])
         hidden(1, 0)
         hidden(1, 1)
+        clear_page(2, nc.gpsimd, on="tab_w")
+        clear_page(3, nc.gpsimd, on="y0_0")
         late_y = tile([P, 2, CHUNK], F32, "late_y", on="relu1_1")
         for i in range(2, N_TILES):
-            down(0, i, late_y[:, i - 2, :])
+            down_by_rows(0, i, late_y[:, i - 2, :])
+        down_by_tokens(1)
         for i in range(N_TILES):
-            down(1, i, tile([P, CHUNK], F32, f"y1_{i}")[:])
+            turn_back(1, i)

@@ -1,7 +1,6 @@
 from contextlib import ExitStack
 
 import concourse.mybir as mybir
-from concourse.masks import make_identity
 
 K, R, N, T, J = 512, 1024, 512, 2048, 1024
 FLOPS = 2 * K * R * J + 2 * R * N * J
@@ -34,8 +33,7 @@ def tile_list_modp_relu2_mix_gate_kernel(
     with ExitStack() as ctx:
         keep = ctx.enter_context(tc.tile_pool(name="keep", bufs=1))
         up_psum = ctx.enter_context(tc.psum_pool(name="up_psum", bufs=4))
-        down_psum = ctx.enter_context(tc.psum_pool(name="down_psum", bufs=2))
-        turn_psum = ctx.enter_context(tc.psum_pool(name="turn_psum", bufs=2))
+        down_psum = ctx.enter_context(tc.psum_pool(name="down_psum", bufs=4))
 
         def tile(shape, dtype, name, on=None):
             return keep.tile(shape, dtype, name=name, tag=on or name, align_bytes=64)
@@ -65,16 +63,11 @@ def tile_list_modp_relu2_mix_gate_kernel(
 
         pages = {}
 
-        def clear_page(i, engine, on=None):
+        def clear_page(i, on=None):
             pages[i] = tile([P, T], F32, f"page{i}", on=on)
-            for k in range(4):
-                engine.memset(pages[i][:, k * (T // 4) : (k + 1) * (T // 4)], 0.0)
+            for k in range(2):
+                nc.vector.memset(pages[i][:, k * (T // 2) : (k + 1) * (T // 2)], 0.0)
 
-        wgo_rows = tile([P, P], F32, "wgo_rows")
-        nc.gpsimd.memset(wgo_rows[:], 0.0)
-        nc.gpsimd.dma_start(wgo_rows[0 : CHUNK // P, :], wgo[0, CHUNK:].rearrange("(b m) -> b m", m=P))
-        identity = tile([P, P], F32, "identity")
-        make_identity(nc, identity[:])
         root = tile([P, R_PASSES * PACK], F32, "root")
         for g in range(R_PASSES):
             sm_abs = tile([P, PACK], F32, f"sm_abs{g}")
@@ -84,10 +77,8 @@ def tile_list_modp_relu2_mix_gate_kernel(
         for g in range(R_PASSES):
             nc.scalar.activation(signs[:, g], sm_sb[:, g, :].unsqueeze(1).to_broadcast([P, SIGN_RUN, PACK]), ACT.Sign)
 
-        wgo_cols = tile([P, CHUNK // P], F32, "wgo_cols")
-        wgo_ps = turn_psum.tile([P, CHUNK], F32, name="y_ps")
-        nc.tensor.transpose(wgo_ps[:, 0:P], wgo_rows[:], identity[:])
-        nc.scalar.copy(wgo_cols[:], wgo_ps[:, 0 : CHUNK // P])
+        for i in range(N_TILES - 1):
+            clear_page(i)
 
         cols = CHUNK // 16
         lists = [offsets[:, c * cols : (c + 1) * cols] for c in range(N_CHUNKS)]
@@ -107,33 +98,17 @@ def tile_list_modp_relu2_mix_gate_kernel(
         picked_s.append(tile([P, CHUNK], U8, "picked_s1", on="wu_raw_w"))
         nc.vector.tensor_copy(picked_w[1][:], tab_w[:].bitcast(U32).indirect(lists[1]))
         nc.vector.tensor_copy(picked_s[1][:], tab_s[:].indirect(lists[1]))
-        clear_page(0, nc.vector)
-        clear_page(1, nc.vector)
 
-        gates = [tile([P, T], F32, f"gates{i}", on=("sm_abs0", "sm_sb", "wgo_rows", "tab_w")[i]) for i in range(N_TILES)]
-        wgo_sb = tile([P, CHUNK], F32, "wgo_sb", on="sm_abs1")
+        gates = [tile([P, T], F32, f"gates{i}", on=("sm_abs0", "sm_sb", "tab_w", "tab_s")[i]) for i in range(N_TILES)]
+        wgo_sb = tile([P, J], F32, "wgo_sb", on="sm_abs1")
         nc.sync.dma_start(gates[0][:], gT[0:P, :])
-        nc.sync.dma_start(wgo_sb[:], wgo[:, 0:CHUNK])
+        nc.sync.dma_start(wgo_sb[:], wgo)
         for i in range(1, N_TILES):
             nc.sync.dma_start(gates[i][:], gT[i * P : (i + 1) * P, :])
-
-        wd = tile([P, N + N // 2 + N // 4], I32, "wd", on="tab_s")
-        wd_w = wd[:, 0 : N + N // 2]
-        wd_s32 = wd[:, N + N // 2 :]
-        wd_s = wd_s32.bitcast(U8)
-        nc.vector.memset(wd_s32, 0)
-        nc.sync.dma_start(wd_w[:, 0:N], wd8_words[0].rearrange("p n i -> p (n i)").bitcast(I32))
-        nc.sync.dma_start(wd_w[:, N:], wd4_words[0].bitcast(I32))
-        for q in range(4):
-            nc.sync.dma_start(wd_s32[32 * q : 32 * q + 4, :], wd4_scales[0].bitcast(I32)[4 * q : 4 * q + 4, :])
-            nc.sync.dma_start(wd_s32[32 * q + 4 : 32 * q + 8, :], wd8_scales[0].bitcast(I32)[4 * q : 4 * q + 4, :])
-        wd8_w = wd_w[:, 0:N]
-        wd4_w = wd_w[:, N:].bitcast(U8)
 
         h_w = {}
         h_s = {}
         picked_g = {}
-        yT = {}
 
         def hidden(c, g):
             relu = tile([P, PACK, CHUNK], F32, f"relu{c}_{g}")
@@ -172,7 +147,7 @@ def tile_list_modp_relu2_mix_gate_kernel(
                 nc.sync.dma_start(out[i * P : (i + 1) * P, :], pages[i][:])
 
         def down_by_rows(c, i, y):
-            y_ps = turn_psum.tile([P, CHUNK], F32, name="y_ps")
+            y_ps = down_psum.tile([P, CHUNK], F32, name="y_ps")
             nc.tensor.matmul_mx(
                 out=y_ps[:],
                 lhsT=wd8_w[:, i * P : (i + 1) * P].bitcast(FP8X4),
@@ -194,57 +169,37 @@ def tile_list_modp_relu2_mix_gate_kernel(
             nc.scalar.copy(y, y_ps[:])
             scatter(c, i, y)
 
-        def down_by_tokens(c):
-            for b in range(CHUNK // P):
-                tokens = slice(b * P, (b + 1) * P)
-                yT_ps = down_psum.tile([P, N], F32, name="yT_ps")
-                nc.tensor.matmul_mx(
-                    out=yT_ps[:],
-                    lhsT=h_w[c, 0][:, tokens].bitcast(FP8X4),
-                    lhsT_scale=h_s[c, 0][:, tokens],
-                    rhs=wd8_w.bitcast(FP8X4),
-                    rhs_scale=wd_s[4:P, :],
-                    start=True,
-                    stop=False,
-                )
-                nc.tensor.matmul_mx(
-                    out=yT_ps[:],
-                    lhsT=h_w[c, 1][:, tokens].bitcast(FP8X4),
-                    lhsT_scale=h_s[c, 1][:, tokens],
-                    rhs=wd4_w.bitcast(FP4X4),
-                    rhs_scale=wd_s,
-                    start=False,
-                    stop=True,
-                )
-                yT[b] = tile([P, N], F32, f"yT{b}")
-                nc.scalar.activation(yT[b][:], yT_ps[:], ACT.Copy, scale=wgo_cols[:, b : b + 1])
-
-        def turn_back(c, i):
-            y_ps = turn_psum.tile([P, CHUNK], F32, name="y_ps")
-            for b in range(CHUNK // P):
-                nc.tensor.transpose(y_ps[:, b * P : (b + 1) * P], yT[b][:, i * P : (i + 1) * P], identity[:])
-            y = tile([P, CHUNK], F32, f"y{c}_{i}")
-            nc.scalar.copy(y[:], y_ps[:])
-            scatter(c, i, y[:])
+        def gather_gates(c, i, dst):
+            picked_g[c, i] = dst
+            nc.vector.tensor_tensor(dst, gates[i][:].indirect(lists[c]), wgo_sb[:, c * CHUNK : (c + 1) * CHUNK], ALU.mult)
 
         hidden(0, 0)
+        wd = tile([P, N + N // 2 + N // 4], I32, "wd", on="relu0_0")
+        wd_w = wd[:, 0 : N + N // 2]
+        wd_s32 = wd[:, N + N // 2 :]
+        wd_s = wd_s32.bitcast(U8)
+        nc.vector.memset(wd_s32, 0)
+        nc.sync.dma_start(wd_w[:, 0:N], wd8_words[0].rearrange("p n i -> p (n i)").bitcast(I32))
+        nc.sync.dma_start(wd_w[:, N:], wd4_words[0].bitcast(I32))
+        for q in range(4):
+            nc.sync.dma_start(wd_s32[32 * q : 32 * q + 4, :], wd4_scales[0].bitcast(I32)[4 * q : 4 * q + 4, :])
+            nc.sync.dma_start(wd_s32[32 * q + 4 : 32 * q + 8, :], wd8_scales[0].bitcast(I32)[4 * q : 4 * q + 4, :])
+        wd8_w = wd_w[:, 0:N]
+        wd4_w = wd_w[:, N:].bitcast(U8)
+
         hidden(0, 1)
-        for i in range(N_TILES):
-            picked_g[0, i] = tile([P, CHUNK], F32, f"picked_g0_{i}")[:]
-            nc.vector.tensor_tensor(picked_g[0, i], gates[i][:].indirect(lists[0]), wgo_sb[:], ALU.mult)
-        late_g = tile([P, N_TILES - 1, CHUNK], F32, "late_g", on="h0_1")
-        for i in range(N_TILES):
-            picked_g[1, i] = late_g[:, i - 1, :] if i else tile([P, CHUNK], F32, "picked_g1_0")[:]
-            nc.vector.tensor_copy(picked_g[1, i], gates[i][:].indirect(lists[1]))
-        down_by_rows(0, 0, tile([P, CHUNK], F32, "y0_0")[:])
-        down_by_rows(0, 1, tile([P, CHUNK], F32, "y0_1")[:])
+        for c, i in ((0, 0), (1, 0), (0, 1), (1, 1), (0, 2), (0, 3)):
+            gather_gates(c, i, tile([P, CHUNK], F32, f"picked_g{c}_{i}")[:])
+        late_g = tile([P, 2, CHUNK], F32, "late_g", on="h0_1")
+        gather_gates(1, 2, late_g[:, 0, :])
+        gather_gates(1, 3, late_g[:, 1, :])
+        clear_page(3, on="relu0_1")
+        for i in range(2):
+            down_by_rows(0, i, tile([P, CHUNK], F32, f"y0_{i}")[:])
         hidden(1, 0)
         hidden(1, 1)
-        clear_page(2, nc.gpsimd, on="tab_w")
-        clear_page(3, nc.gpsimd, on="y0_0")
         late_y = tile([P, 2, CHUNK], F32, "late_y", on="relu1_1")
         for i in range(2, N_TILES):
             down_by_rows(0, i, late_y[:, i - 2, :])
-        down_by_tokens(1)
         for i in range(N_TILES):
-            turn_back(1, i)
+            down_by_rows(1, i, tile([P, CHUNK], F32, f"y1_{i}")[:])

@@ -95,16 +95,29 @@ def tile_list_modp_relu2_mix_gate_kernel(
             wu_raw_s[:].rearrange("p (m t) -> p m t", t=PACK),
         )
         picked_w.append(tile([P, CHUNK], U32, "picked_w1", on="wu_raw_s"))
-        picked_s.append(tile([P, CHUNK], U8, "picked_s1", on="wu_raw_w"))
+        picked_s.append(tile([P, CHUNK], U8, "picked_s1", on="tab_w"))
         nc.vector.tensor_copy(picked_w[1][:], tab_w[:].bitcast(U32).indirect(lists[1]))
         nc.vector.tensor_copy(picked_s[1][:], tab_s[:].indirect(lists[1]))
 
-        gates = [tile([P, T], F32, f"gates{i}", on=("sm_abs0", "sm_sb", "tab_w", "tab_s")[i]) for i in range(N_TILES)]
+        gates = [tile([P, T], F32, f"gates{i}", on=("sm_abs0", "sm_sb", "wu_raw_w")[i]) for i in range(N_TILES - 1)]
         wgo_sb = tile([P, J], F32, "wgo_sb", on="sm_abs1")
         nc.sync.dma_start(gates[0][:], gT[0:P, :])
         nc.sync.dma_start(wgo_sb[:], wgo)
-        for i in range(1, N_TILES):
+        for i in range(1, N_TILES - 1):
             nc.sync.dma_start(gates[i][:], gT[i * P : (i + 1) * P, :])
+
+        wd = tile([P, N + N // 2 + N // 4], I32, "wd", on="tab_s")
+        wd_w = wd[:, 0 : N + N // 2]
+        wd_s32 = wd[:, N + N // 2 :]
+        wd_s = wd_s32.bitcast(U8)
+        nc.vector.memset(wd_s32, 0)
+        nc.sync.dma_start(wd_w[:, 0:N], wd8_words[0].rearrange("p n i -> p (n i)").bitcast(I32))
+        nc.sync.dma_start(wd_w[:, N:], wd4_words[0].bitcast(I32))
+        for q in range(4):
+            nc.sync.dma_start(wd_s32[32 * q : 32 * q + 4, :], wd4_scales[0].bitcast(I32)[4 * q : 4 * q + 4, :])
+            nc.sync.dma_start(wd_s32[32 * q + 4 : 32 * q + 8, :], wd8_scales[0].bitcast(I32)[4 * q : 4 * q + 4, :])
+        wd8_w = wd_w[:, 0:N]
+        wd4_w = wd_w[:, N:].bitcast(U8)
 
         h_w = {}
         h_s = {}
@@ -130,7 +143,10 @@ def tile_list_modp_relu2_mix_gate_kernel(
                 relu[:].rearrange("p t (c i) -> p c t i", i=4),
                 ACT.Square,
             )
-            h = tile([P, CHUNK * PACK], BF16, f"h{c}_{g}")
+            return h_abs
+
+        def quantise(c, g, h_abs, on=None):
+            h = tile([P, CHUNK * PACK], BF16, f"h{c}_{g}", on=on)
             nc.vector.tensor_tensor(
                 h[:].rearrange("p (a b) -> p a b", b=SIGN_RUN * PACK),
                 h_abs[:].rearrange("p (a b) -> p a b", b=SIGN_RUN * PACK),
@@ -142,7 +158,7 @@ def tile_list_modp_relu2_mix_gate_kernel(
             nc.vector.quantize_mx(out=h_w[c, g][:].bitcast(FP8X4), scales=h_s[c, g][:], in_=h[:])
 
         def scatter(c, i, y):
-            nc.vector.tensor_tensor(pages[i][:].indirect(lists[c]), y, picked_g[c, i], ALU.mult)
+            nc.vector.tensor_tensor(pages[i][:].indirect(lists[c]), y, picked_g[i][:, c * CHUNK : (c + 1) * CHUNK], ALU.mult)
             if c == N_CHUNKS - 1:
                 nc.sync.dma_start(out[i * P : (i + 1) * P, :], pages[i][:])
 
@@ -169,35 +185,24 @@ def tile_list_modp_relu2_mix_gate_kernel(
             nc.scalar.copy(y, y_ps[:])
             scatter(c, i, y)
 
-        def gather_gates(c, i, dst):
-            picked_g[c, i] = dst
-            nc.vector.tensor_tensor(dst, gates[i][:].indirect(lists[c]), wgo_sb[:, c * CHUNK : (c + 1) * CHUNK], ALU.mult)
+        def gather_gates(i, on=None):
+            picked_g[i] = tile([P, J], F32, f"picked_g{i}", on=on)
+            nc.vector.tensor_tensor(picked_g[i][:], gates[i][:].indirect(offsets[:]), wgo_sb[:], ALU.mult)
 
-        hidden(0, 0)
-        wd = tile([P, N + N // 2 + N // 4], I32, "wd", on="relu0_0")
-        wd_w = wd[:, 0 : N + N // 2]
-        wd_s32 = wd[:, N + N // 2 :]
-        wd_s = wd_s32.bitcast(U8)
-        nc.vector.memset(wd_s32, 0)
-        nc.sync.dma_start(wd_w[:, 0:N], wd8_words[0].rearrange("p n i -> p (n i)").bitcast(I32))
-        nc.sync.dma_start(wd_w[:, N:], wd4_words[0].bitcast(I32))
-        for q in range(4):
-            nc.sync.dma_start(wd_s32[32 * q : 32 * q + 4, :], wd4_scales[0].bitcast(I32)[4 * q : 4 * q + 4, :])
-            nc.sync.dma_start(wd_s32[32 * q + 4 : 32 * q + 8, :], wd8_scales[0].bitcast(I32)[4 * q : 4 * q + 4, :])
-        wd8_w = wd_w[:, 0:N]
-        wd4_w = wd_w[:, N:].bitcast(U8)
-
-        hidden(0, 1)
-        for c, i in ((0, 0), (1, 0), (0, 1), (1, 1), (0, 2), (0, 3)):
-            gather_gates(c, i, tile([P, CHUNK], F32, f"picked_g{c}_{i}")[:])
-        late_g = tile([P, 2, CHUNK], F32, "late_g", on="h0_1")
-        gather_gates(1, 2, late_g[:, 0, :])
-        gather_gates(1, 3, late_g[:, 1, :])
+        h_abs = hidden(0, 0)
+        gates.append(tile([P, T], F32, "gates3", on="relu0_0"))
+        nc.sync.dma_start(gates[3][:], gT[3 * P : 4 * P, :])
+        for i in range(2):
+            gather_gates(i)
+        quantise(0, 0, h_abs, on="sm_sb")
+        quantise(0, 1, hidden(0, 1))
+        gather_gates(2)
+        gather_gates(3, on="h0_1")
         clear_page(3, on="relu0_1")
         for i in range(2):
             down_by_rows(0, i, tile([P, CHUNK], F32, f"y0_{i}")[:])
-        hidden(1, 0)
-        hidden(1, 1)
+        for g in range(R_PASSES):
+            quantise(1, g, hidden(1, g))
         late_y = tile([P, 2, CHUNK], F32, "late_y", on="relu1_1")
         for i in range(2, N_TILES):
             down_by_rows(0, i, late_y[:, i - 2, :])

@@ -19,11 +19,20 @@ ACT = mybir.ActivationFunctionType
 P = 128
 PACK = 4
 PASS = P * PACK
+QUADRANTS = 4
+QUAD = P // QUADRANTS
+SCALE_ROWS = 4
+GROUP = 16
 CHUNK = 512
 N_CHUNKS = J // CHUNK
 R_PASSES = R // PASS
 N_TILES = N // P
+LAST = N_TILES - 1
+LINE = 4
 SIGN_RUN = 16
+WD8_WORDS = N
+WD4_WORDS = N // 2
+WD_PLANE_WORDS = N // 4
 
 
 def tile_list_modp_relu2_mix_gate_kernel(
@@ -32,13 +41,19 @@ def tile_list_modp_relu2_mix_gate_kernel(
     nc = tc.nc
     with ExitStack() as ctx:
         keep = ctx.enter_context(tc.tile_pool(name="keep", bufs=1))
-        up_psum = ctx.enter_context(tc.psum_pool(name="up_psum", bufs=4))
-        down_psum = ctx.enter_context(tc.psum_pool(name="down_psum", bufs=4))
+        up_psum = ctx.enter_context(tc.psum_pool(name="up_psum", bufs=PACK))
+        down_psum = ctx.enter_context(tc.psum_pool(name="down_psum", bufs=N_TILES))
 
         def tile(shape, dtype, name, on=None):
             return keep.tile(shape, dtype, name=name, tag=on or name, align_bytes=64)
 
-        offsets = keep.tile([P, J // 16], U16, name="offsets")
+        def scale_rows(q, first=0, planes=1):
+            return slice(QUAD * q + SCALE_ROWS * first, QUAD * q + SCALE_ROWS * (first + planes))
+
+        def blocks(q):
+            return slice(SCALE_ROWS * q, SCALE_ROWS * (q + 1))
+
+        offsets = keep.tile([P, J // GROUP], U16, name="offsets")
         tab_w = tile([P, T], I32, "tab_w")
         tab_s = tile([P, T], U8, "tab_s")
         wu_raw_w = tile([P, R], I32, "wu_raw_w")
@@ -52,35 +67,31 @@ def tile_list_modp_relu2_mix_gate_kernel(
         nc.sync.dma_start(offsets[:], offs)
         nc.sync.dma_start(sm_sb[:], sm.rearrange("(g p t) -> p g t", g=R_PASSES, t=PACK))
         nc.sync.dma_start(tab_w[:], tab_words[0].rearrange("p t i -> p (t i)").bitcast(I32))
-        for q in range(4):
-            nc.sync.dma_start(tab_s[32 * q : 32 * q + 4, :].bitcast(I32), tab_scales[0].bitcast(I32)[4 * q : 4 * q + 4, :])
+        for q in range(QUADRANTS):
+            nc.sync.dma_start(tab_s[scale_rows(q), :].bitcast(I32), tab_scales[0].bitcast(I32)[blocks(q), :])
         nc.sync.dma_start(wu_raw_w[:], wu_words[0].rearrange("p r i -> p (r i)").bitcast(I32))
-        for q in range(4):
+        for q in range(QUADRANTS):
             nc.sync.dma_start(
-                wu_raw_s[32 * q : 32 * q + 8, :].bitcast(I32),
-                wu_scales[0].bitcast(I32)[4 * q : 4 * q + 4, :].rearrange("q (g c) -> g q c", g=R_PASSES),
+                wu_raw_s[scale_rows(q, planes=R_PASSES), :].bitcast(I32),
+                wu_scales[0].bitcast(I32)[blocks(q), :].rearrange("q (g c) -> g q c", g=R_PASSES),
             )
-
-        pages = {}
-
-        def clear_page(i, on=None):
-            pages[i] = tile([P, T], F32, f"page{i}", on=on)
-            for k in range(2):
-                nc.vector.memset(pages[i][:, k * (T // 2) : (k + 1) * (T // 2)], 0.0)
 
         root = tile([P, R_PASSES * PACK], F32, "root")
         for g in range(R_PASSES):
             sm_abs = tile([P, PACK], F32, f"sm_abs{g}")
             nc.scalar.activation(sm_abs[:], sm_sb[:, g, :], ACT.Abs)
             nc.scalar.activation(root[:, g * PACK : (g + 1) * PACK], sm_abs[:], ACT.Sqrt)
+        sm_last = tile([P, PACK], F32, "sm_last")
+        nc.scalar.copy(sm_last[:], sm_sb[:, R_PASSES - 1, :])
         signs = tile([P, R_PASSES, SIGN_RUN, PACK], BF16, "signs")
         for g in range(R_PASSES):
             nc.scalar.activation(signs[:, g], sm_sb[:, g, :].unsqueeze(1).to_broadcast([P, SIGN_RUN, PACK]), ACT.Sign)
 
-        for i in range(N_TILES - 1):
-            clear_page(i)
+        pages = [tile([P, T], F32, f"page{i}") for i in range(N_TILES)]
+        for page in pages:
+            nc.vector.memset(page[:].bitcast(I32), 0)
 
-        cols = CHUNK // 16
+        cols = CHUNK // GROUP
         lists = [offsets[:, c * cols : (c + 1) * cols] for c in range(N_CHUNKS)]
         picked_w = [tile([P, CHUNK], U32, "picked_w0")]
         picked_s = [tile([P, CHUNK], U8, "picked_s0")]
@@ -99,75 +110,100 @@ def tile_list_modp_relu2_mix_gate_kernel(
         nc.vector.tensor_copy(picked_w[1][:], tab_w[:].bitcast(U32).indirect(lists[1]))
         nc.vector.tensor_copy(picked_s[1][:], tab_s[:].indirect(lists[1]))
 
-        gates = [tile([P, T], F32, f"gates{i}", on=("sm_abs0", "sm_sb", "wu_raw_w")[i]) for i in range(N_TILES - 1)]
+        gates = [tile([P, T], F32, f"gates{i}", on=name) for i, name in enumerate(("sm_abs0", "sm_sb", "wu_raw_w"))]
         wgo_sb = tile([P, J], F32, "wgo_sb", on="sm_abs1")
         nc.sync.dma_start(gates[0][:], gT[0:P, :])
         nc.sync.dma_start(wgo_sb[:], wgo)
-        for i in range(1, N_TILES - 1):
+        for i in range(1, LAST):
             nc.sync.dma_start(gates[i][:], gT[i * P : (i + 1) * P, :])
 
-        wd = tile([P, N + N // 2 + N // 4], I32, "wd", on="tab_s")
-        wd_w = wd[:, 0 : N + N // 2]
-        wd_s32 = wd[:, N + N // 2 :]
-        wd_s = wd_s32.bitcast(U8)
+        wd = tile([P, WD8_WORDS + WD4_WORDS + WD_PLANE_WORDS], I32, "wd", on="tab_s")
+        wd8_w = wd[:, 0:WD8_WORDS]
+        wd4_w32 = wd[:, WD8_WORDS : WD8_WORDS + WD4_WORDS]
+        wd_s32 = wd[:, WD8_WORDS + WD4_WORDS :]
         nc.vector.memset(wd_s32, 0)
-        nc.sync.dma_start(wd_w[:, 0:N], wd8_words[0].rearrange("p n i -> p (n i)").bitcast(I32))
-        nc.sync.dma_start(wd_w[:, N:], wd4_words[0].bitcast(I32))
-        for q in range(4):
-            nc.sync.dma_start(wd_s32[32 * q : 32 * q + 4, :], wd4_scales[0].bitcast(I32)[4 * q : 4 * q + 4, :])
-            nc.sync.dma_start(wd_s32[32 * q + 4 : 32 * q + 8, :], wd8_scales[0].bitcast(I32)[4 * q : 4 * q + 4, :])
-        wd8_w = wd_w[:, 0:N]
-        wd4_w = wd_w[:, N:].bitcast(U8)
+        nc.sync.dma_start(wd8_w, wd8_words[0].rearrange("p n i -> p (n i)").bitcast(I32))
+        nc.sync.dma_start(wd4_w32, wd4_words[0].bitcast(I32))
+        for q in range(QUADRANTS):
+            nc.sync.dma_start(wd_s32[scale_rows(q), :], wd4_scales[0].bitcast(I32)[blocks(q), :])
+            nc.sync.dma_start(wd_s32[scale_rows(q, first=1), :], wd8_scales[0].bitcast(I32)[blocks(q), :])
+        wd4_w = wd4_w32.bitcast(U8)
+        wd_s = wd_s32.bitcast(U8)
 
         h_w = {}
         h_s = {}
         picked_g = {}
 
-        def hidden(c, g):
-            relu = tile([P, PACK, CHUNK], F32, f"relu{c}_{g}")
-            for t in range(PACK):
-                a = up_psum.tile([P, CHUNK], F32, name="a")
-                nc.tensor.matmul_mx(
-                    out=a[:],
-                    lhsT=wu_w[:, g * PASS + t * P : g * PASS + (t + 1) * P].bitcast(FP8X4),
-                    lhsT_scale=wu_s[4 * g : P, t * P : (t + 1) * P],
-                    rhs=picked_w[c][:].bitcast(FP8X4),
-                    rhs_scale=picked_s[c][:],
-                    start=True,
-                    stop=True,
-                )
-                nc.scalar.activation(relu[:, t, :], a[:], ACT.Relu, scale=root[:, g * PACK + t : g * PACK + t + 1])
-            h_abs = tile([P, CHUNK * PACK], BF16, f"h_abs{c}_{g}")
-            nc.scalar.activation(
-                h_abs[:].rearrange("p (c i t) -> p c t i", i=4, t=PACK),
-                relu[:].rearrange("p t (c i) -> p c t i", i=4),
-                ACT.Square,
+        def up_slice(c, g, t):
+            a = up_psum.tile([P, CHUNK], F32, name="a")
+            nc.tensor.matmul_mx(
+                out=a[:],
+                lhsT=wu_w[:, g * PASS + t * P : g * PASS + (t + 1) * P].bitcast(FP8X4),
+                lhsT_scale=wu_s[SCALE_ROWS * g : P, t * P : (t + 1) * P],
+                rhs=picked_w[c][:].bitcast(FP8X4),
+                rhs_scale=picked_s[c][:],
+                start=True,
+                stop=True,
             )
-            return h_abs
+            return a
 
-        def quantise(c, g, h_abs, on=None):
-            h = tile([P, CHUNK * PACK], BF16, f"h{c}_{g}", on=on)
-            nc.vector.tensor_tensor(
-                h[:].rearrange("p (a b) -> p a b", b=SIGN_RUN * PACK),
-                h_abs[:].rearrange("p (a b) -> p a b", b=SIGN_RUN * PACK),
-                signs[:, g].rearrange("p j t -> p (j t)").unsqueeze(1).to_broadcast([P, CHUNK // SIGN_RUN, SIGN_RUN * PACK]),
-                ALU.mult,
+        def interleave(dst, src, func):
+            nc.scalar.activation(
+                dst[:].rearrange("p (c i t) -> p c t i", i=LINE, t=PACK),
+                src[:].rearrange("p t (c i) -> p c t i", i=LINE),
+                func,
             )
+
+        def quantise(c, g, h):
             h_w[c, g] = tile([P, CHUNK], U32, f"h_w{c}_{g}")
             h_s[c, g] = tile([P, CHUNK], U8, f"h_s{c}_{g}")
             nc.vector.quantize_mx(out=h_w[c, g][:].bitcast(FP8X4), scales=h_s[c, g][:], in_=h[:])
 
-        def scatter(c, i, y):
-            nc.vector.tensor_tensor(pages[i][:].indirect(lists[c]), y, picked_g[i][:, c * CHUNK : (c + 1) * CHUNK], ALU.mult)
-            if c == N_CHUNKS - 1:
-                nc.sync.dma_start(out[i * P : (i + 1) * P, :], pages[i][:])
+        def hidden_unsigned(c, g):
+            relu = tile([P, PACK, CHUNK], F32, f"relu{c}_{g}")
+            for t in range(PACK):
+                col = g * PACK + t
+                nc.scalar.activation(relu[:, t, :], up_slice(c, g, t)[:], ACT.Relu, scale=root[:, col : col + 1])
+            h_abs = tile([P, CHUNK * PACK], BF16, f"h_abs{c}_{g}")
+            interleave(h_abs, relu, ACT.Square)
+            return h_abs
 
-        def down_by_rows(c, i, y):
+        def sign_and_quantise(c, g, h_abs, on=None):
+            run = SIGN_RUN * PACK
+            h = tile([P, CHUNK * PACK], BF16, f"h{c}_{g}", on=on)
+            nc.vector.tensor_tensor(
+                h[:].rearrange("p (a b) -> p a b", b=run),
+                h_abs[:].rearrange("p (a b) -> p a b", b=run),
+                signs[:, g].rearrange("p j t -> p (j t)").unsqueeze(1).to_broadcast([P, CHUNK // SIGN_RUN, run]),
+                ALU.mult,
+            )
+            quantise(c, g, h)
+
+        def hidden_on_scalar(c, g, factors, on):
+            relu = tile([P, PACK, CHUNK], F32, f"relu{c}_{g}", on=on)
+            for t in range(PACK):
+                nc.scalar.activation(relu[:, t, :], up_slice(c, g, t)[:], ACT.Relu)
+            square = tile([P, PACK, CHUNK], F32, f"square{c}_{g}")
+            nc.scalar.activation(square[:], relu[:], ACT.Square)
+            scaled = tile([P, PACK, CHUNK], F32, f"scaled{c}_{g}")
+            for t in range(PACK):
+                nc.scalar.activation(scaled[:, t, :], square[:, t, :], ACT.Copy, scale=factors[:, t : t + 1])
+            h = tile([P, CHUNK * PACK], BF16, f"h{c}_{g}")
+            interleave(h, scaled, ACT.Copy)
+            quantise(c, g, h)
+
+        def gather_gates(first, name, on=None):
+            pair = tile([P, 2 * J], F32, name, on=on)
+            for k in range(2):
+                picked_g[first + k] = pair[:, k * J : (k + 1) * J]
+                nc.vector.tensor_tensor(picked_g[first + k], gates[first + k][:].indirect(offsets[:]), wgo_sb[:], ALU.mult)
+
+        def down(c, i):
             y_ps = down_psum.tile([P, CHUNK], F32, name="y_ps")
             nc.tensor.matmul_mx(
                 out=y_ps[:],
                 lhsT=wd8_w[:, i * P : (i + 1) * P].bitcast(FP8X4),
-                lhsT_scale=wd_s[4:P, i * P : (i + 1) * P],
+                lhsT_scale=wd_s[SCALE_ROWS:P, i * P : (i + 1) * P],
                 rhs=h_w[c, 0][:].bitcast(FP8X4),
                 rhs_scale=h_s[c, 0][:],
                 start=True,
@@ -182,29 +218,30 @@ def tile_list_modp_relu2_mix_gate_kernel(
                 start=False,
                 stop=True,
             )
-            nc.scalar.copy(y, y_ps[:])
-            scatter(c, i, y)
+            return y_ps
 
-        def gather_gates(i, on=None):
-            picked_g[i] = tile([P, J], F32, f"picked_g{i}", on=on)
-            nc.vector.tensor_tensor(picked_g[i][:], gates[i][:].indirect(offsets[:]), wgo_sb[:], ALU.mult)
+        def scatter(c, i, y_ps, on=None):
+            y = tile([P, CHUNK], F32, f"y{c}_{i}", on=on)
+            nc.scalar.copy(y[:], y_ps[:])
+            nc.vector.tensor_tensor(
+                pages[i][:].indirect(lists[c]), y[:], picked_g[i][:, c * CHUNK : (c + 1) * CHUNK], ALU.mult
+            )
+            if c == N_CHUNKS - 1:
+                nc.sync.dma_start(out[i * P : (i + 1) * P, :], pages[i][:])
 
-        h_abs = hidden(0, 0)
-        gates.append(tile([P, T], F32, "gates3", on="relu0_0"))
-        nc.sync.dma_start(gates[3][:], gT[3 * P : 4 * P, :])
-        for i in range(2):
-            gather_gates(i)
-        quantise(0, 0, h_abs, on="sm_sb")
-        quantise(0, 1, hidden(0, 1))
-        gather_gates(2)
-        gather_gates(3, on="h0_1")
-        clear_page(3, on="relu0_1")
-        for i in range(2):
-            down_by_rows(0, i, tile([P, CHUNK], F32, f"y0_{i}")[:])
-        for g in range(R_PASSES):
-            quantise(1, g, hidden(1, g))
-        late_y = tile([P, 2, CHUNK], F32, "late_y", on="relu1_1")
-        for i in range(2, N_TILES):
-            down_by_rows(0, i, late_y[:, i - 2, :])
+        h_abs_first = hidden_unsigned(0, 0)
+        gates.append(tile([P, T], F32, f"gates{LAST}", on="relu0_0"))
+        nc.sync.dma_start(gates[LAST][:], gT[LAST * P : (LAST + 1) * P, :])
+        gather_gates(0, "picked_g_early")
+        sign_and_quantise(0, 0, h_abs_first, on="sm_sb")
+        sign_and_quantise(0, 1, hidden_unsigned(0, 1))
+        gather_gates(2, "picked_g_late", on="h0_1")
+        for i in range(LAST):
+            scatter(0, i, down(0, i))
+        y_ps_held = down(0, LAST)
+
+        sign_and_quantise(1, 0, hidden_unsigned(1, 0))
+        hidden_on_scalar(1, 1, sm_last, on="h_w0_1")
+        scatter(0, LAST, y_ps_held, on="scaled1_1")
         for i in range(N_TILES):
-            down_by_rows(1, i, tile([P, CHUNK], F32, f"y1_{i}")[:])
+            scatter(1, i, down(1, i))

@@ -23,7 +23,9 @@ QUADRANTS = 4
 QUAD = P // QUADRANTS
 SCALE_ROWS = 4
 GROUP = 16
-CHUNK = 512
+CHUNK = 256
+BANK = 512
+PAIR = BANK // CHUNK
 N_CHUNKS = J // CHUNK
 R_PASSES = R // PASS
 N_TILES = N // P
@@ -66,10 +68,10 @@ def tile_list_modp_relu2_mix_gate_kernel(
         nc.vector.memset(wu_raw_s[:].bitcast(I32), 0)
         nc.sync.dma_start(offsets[:], offs)
         nc.sync.dma_start(sm_sb[:], sm.rearrange("(g p t) -> p g t", g=R_PASSES, t=PACK))
-        nc.sync.dma_start(tab_w[:], tab_words[0].rearrange("p t i -> p (t i)").bitcast(I32))
+        nc.sync.dma_start(wu_raw_w[:], wu_words[0].rearrange("p r i -> p (r i)").bitcast(I32))
         for q in range(QUADRANTS):
             nc.sync.dma_start(tab_s[scale_rows(q), :].bitcast(I32), tab_scales[0].bitcast(I32)[blocks(q), :])
-        nc.sync.dma_start(wu_raw_w[:], wu_words[0].rearrange("p r i -> p (r i)").bitcast(I32))
+        nc.sync.dma_start(tab_w[:], tab_words[0].rearrange("p t i -> p (t i)").bitcast(I32))
         for q in range(QUADRANTS):
             nc.sync.dma_start(
                 wu_raw_s[scale_rows(q, planes=R_PASSES), :].bitcast(I32),
@@ -81,121 +83,123 @@ def tile_list_modp_relu2_mix_gate_kernel(
             sm_abs = tile([P, PACK], F32, f"sm_abs{g}")
             nc.scalar.activation(sm_abs[:], sm_sb[:, g, :], ACT.Abs)
             nc.scalar.activation(root[:, g * PACK : (g + 1) * PACK], sm_abs[:], ACT.Sqrt)
-        sm_last = tile([P, PACK], F32, "sm_last")
-        nc.scalar.copy(sm_last[:], sm_sb[:, R_PASSES - 1, :])
+        factors = tile([P, R_PASSES, PACK], F32, "factors")
+        nc.scalar.copy(factors[:], sm_sb[:])
         signs = tile([P, R_PASSES, SIGN_RUN, PACK], BF16, "signs")
         for g in range(R_PASSES):
             nc.scalar.activation(signs[:, g], sm_sb[:, g, :].unsqueeze(1).to_broadcast([P, SIGN_RUN, PACK]), ACT.Sign)
 
-        pages = [tile([P, T], F32, f"page{i}") for i in range(N_TILES)]
+        pages = [tile([P, T], F32, f"page{i}") for i in range(2)]
         for page in pages:
             nc.vector.memset(page[:].bitcast(I32), 0)
+        wd_s32 = tile([P, WD_PLANE_WORDS], I32, "wd_s32")
+        nc.vector.memset(wd_s32[:], 0)
 
-        cols = CHUNK // GROUP
-        lists = [offsets[:, c * cols : (c + 1) * cols] for c in range(N_CHUNKS)]
-        picked_w = [tile([P, CHUNK], U32, "picked_w0")]
-        picked_s = [tile([P, CHUNK], U8, "picked_s0")]
-        nc.vector.tensor_copy(picked_w[0][:], tab_w[:].bitcast(U32).indirect(lists[0]))
-        nc.vector.tensor_copy(picked_s[0][:], tab_s[:].indirect(lists[0]))
         nc.vector.tensor_copy(
             wu_w[:].rearrange("p (g t m) -> p g m t", g=R_PASSES, t=PACK),
             wu_raw_w[:].rearrange("p (g m t) -> p g m t", g=R_PASSES, t=PACK),
         )
+        cols = CHUNK // GROUP
+        lists = [offsets[:, c * cols : (c + 1) * cols] for c in range(N_CHUNKS)]
+        half = J // 2
+        early_s = tile([P, half], U8, "early_s")
+        nc.vector.tensor_copy(early_s[:], tab_s[:].indirect(offsets[:, : half // GROUP]))
         nc.vector.tensor_copy(
             wu_s[:].rearrange("p (t m) -> p m t", t=PACK),
             wu_raw_s[:].rearrange("p (m t) -> p m t", t=PACK),
         )
-        picked_w.append(tile([P, CHUNK], U32, "picked_w1", on="wu_raw_s"))
-        picked_s.append(tile([P, CHUNK], U8, "picked_s1", on="tab_w"))
-        nc.vector.tensor_copy(picked_w[1][:], tab_w[:].bitcast(U32).indirect(lists[1]))
-        nc.vector.tensor_copy(picked_s[1][:], tab_s[:].indirect(lists[1]))
+        first_w = tile([P, CHUNK], U32, "first_w")
+        nc.vector.tensor_copy(first_w[:], tab_w[:].bitcast(U32).indirect(lists[0]))
+        rest_w = tile([P, J - CHUNK], U32, "rest_w", on="wu_raw_s")
+        late_s = tile([P, half], U8, "late_s", on="tab_w")
+        nc.vector.tensor_copy(rest_w[:], tab_w[:].bitcast(U32).indirect(offsets[:, cols:]))
+        nc.vector.tensor_copy(late_s[:], tab_s[:].indirect(offsets[:, half // GROUP :]))
+        picked_w = [first_w[:]] + [rest_w[:, c * CHUNK : (c + 1) * CHUNK] for c in range(N_CHUNKS - 1)]
+        picked_s = [s[:, k * CHUNK : (k + 1) * CHUNK] for s in (early_s, late_s) for k in range(half // CHUNK)]
 
-        gates = [tile([P, T], F32, f"gates{i}", on=name) for i, name in enumerate(("sm_abs0", "sm_sb", "wu_raw_w"))]
+        gates = [tile([P, T], F32, f"gates{i}", on=name) for i, name in enumerate(("sm_abs0", "wu_raw_w", "first_w"))]
         wgo_sb = tile([P, J], F32, "wgo_sb", on="sm_abs1")
+        wd = tile([P, WD8_WORDS + WD4_WORDS], I32, "wd", on="sm_sb")
+        wd8_w = wd[:, 0:WD8_WORDS]
+        wd4_w32 = wd[:, WD8_WORDS:]
         nc.sync.dma_start(gates[0][:], gT[0:P, :])
         nc.sync.dma_start(wgo_sb[:], wgo)
-        for i in range(1, LAST):
-            nc.sync.dma_start(gates[i][:], gT[i * P : (i + 1) * P, :])
-
-        wd = tile([P, WD8_WORDS + WD4_WORDS + WD_PLANE_WORDS], I32, "wd", on="tab_s")
-        wd8_w = wd[:, 0:WD8_WORDS]
-        wd4_w32 = wd[:, WD8_WORDS : WD8_WORDS + WD4_WORDS]
-        wd_s32 = wd[:, WD8_WORDS + WD4_WORDS :]
-        nc.vector.memset(wd_s32, 0)
         nc.sync.dma_start(wd8_w, wd8_words[0].rearrange("p n i -> p (n i)").bitcast(I32))
         nc.sync.dma_start(wd4_w32, wd4_words[0].bitcast(I32))
         for q in range(QUADRANTS):
             nc.sync.dma_start(wd_s32[scale_rows(q), :], wd4_scales[0].bitcast(I32)[blocks(q), :])
             nc.sync.dma_start(wd_s32[scale_rows(q, first=1), :], wd8_scales[0].bitcast(I32)[blocks(q), :])
+        nc.sync.dma_start(gates[1][:], gT[P : 2 * P, :])
+        nc.sync.dma_start(gates[2][:], gT[2 * P : 3 * P, :])
         wd4_w = wd4_w32.bitcast(U8)
-        wd_s = wd_s32.bitcast(U8)
+        wd_s = wd_s32[:].bitcast(U8)
 
-        h_w = {}
-        h_s = {}
+        h = [tile([P, R_PASSES, CHUNK * PACK], BF16, f"h{c}") for c in range(N_CHUNKS)]
+        h_w = [tile([P, R_PASSES * CHUNK], U32, f"h_w{c}") for c in range(N_CHUNKS)]
+        h_s = [tile([P, R_PASSES * CHUNK], U8, f"h_s{c}") for c in range(N_CHUNKS)]
         picked_g = {}
 
-        def up_slice(c, g, t):
-            a = up_psum.tile([P, CHUNK], F32, name="a")
-            nc.tensor.matmul_mx(
-                out=a[:],
-                lhsT=wu_w[:, g * PASS + t * P : g * PASS + (t + 1) * P].bitcast(FP8X4),
-                lhsT_scale=wu_s[SCALE_ROWS * g : P, t * P : (t + 1) * P],
-                rhs=picked_w[c][:].bitcast(FP8X4),
-                rhs_scale=picked_s[c][:],
-                start=True,
-                stop=True,
-            )
+        def clear_page(on):
+            pages.append(tile([P, T], F32, f"page{len(pages)}", on=on))
+            nc.vector.memset(pages[-1][:].bitcast(I32), 0)
+
+        def up_pair(c, g, first):
+            a = up_psum.tile([P, PAIR, CHUNK], F32, name="a")
+            for k in range(PAIR):
+                t = first + k
+                nc.tensor.matmul_mx(
+                    out=a[:, k, :],
+                    lhsT=wu_w[:, g * PASS + t * P : g * PASS + (t + 1) * P].bitcast(FP8X4),
+                    lhsT_scale=wu_s[SCALE_ROWS * g : P, t * P : (t + 1) * P],
+                    rhs=picked_w[c].bitcast(FP8X4),
+                    rhs_scale=picked_s[c],
+                    start=True,
+                    stop=True,
+                )
             return a
 
         def interleave(dst, src, func):
             nc.scalar.activation(
-                dst[:].rearrange("p (c i t) -> p c t i", i=LINE, t=PACK),
-                src[:].rearrange("p t (c i) -> p c t i", i=LINE),
+                dst.rearrange("p (c i t) -> p c t i", i=LINE, t=PACK),
+                src.rearrange("p t (c i) -> p c t i", i=LINE),
                 func,
             )
 
-        def quantise(c, g, h):
-            h_w[c, g] = tile([P, CHUNK], U32, f"h_w{c}_{g}")
-            h_s[c, g] = tile([P, CHUNK], U8, f"h_s{c}_{g}")
-            nc.vector.quantize_mx(out=h_w[c, g][:].bitcast(FP8X4), scales=h_s[c, g][:], in_=h[:])
-
-        def hidden_unsigned(c, g):
+        def hidden_signed_on_vector(c, g):
             relu = tile([P, PACK, CHUNK], F32, f"relu{c}_{g}")
-            for t in range(PACK):
-                col = g * PACK + t
-                nc.scalar.activation(relu[:, t, :], up_slice(c, g, t)[:], ACT.Relu, scale=root[:, col : col + 1])
+            for first in range(0, PACK, PAIR):
+                a = up_pair(c, g, first)
+                for k in range(PAIR):
+                    col = g * PACK + first + k
+                    nc.scalar.activation(relu[:, first + k, :], a[:, k, :], ACT.Relu, scale=root[:, col : col + 1])
             h_abs = tile([P, CHUNK * PACK], BF16, f"h_abs{c}_{g}")
-            interleave(h_abs, relu, ACT.Square)
-            return h_abs
-
-        def sign_and_quantise(c, g, h_abs, on=None):
+            interleave(h_abs[:], relu[:], ACT.Square)
             run = SIGN_RUN * PACK
-            h = tile([P, CHUNK * PACK], BF16, f"h{c}_{g}", on=on)
             nc.vector.tensor_tensor(
-                h[:].rearrange("p (a b) -> p a b", b=run),
+                h[c][:, g, :].rearrange("p (a b) -> p a b", b=run),
                 h_abs[:].rearrange("p (a b) -> p a b", b=run),
                 signs[:, g].rearrange("p j t -> p (j t)").unsqueeze(1).to_broadcast([P, CHUNK // SIGN_RUN, run]),
                 ALU.mult,
             )
-            quantise(c, g, h)
 
-        def hidden_on_scalar(c, g, factors, on):
-            relu = tile([P, PACK, CHUNK], F32, f"relu{c}_{g}", on=on)
-            for t in range(PACK):
-                nc.scalar.activation(relu[:, t, :], up_slice(c, g, t)[:], ACT.Relu)
+        def hidden_on_scalar(c, g):
+            relu = tile([P, PACK, CHUNK], F32, f"relu{c}_{g}")
+            for first in range(0, PACK, PAIR):
+                nc.scalar.activation(relu[:, first : first + PAIR, :], up_pair(c, g, first)[:], ACT.Relu)
             square = tile([P, PACK, CHUNK], F32, f"square{c}_{g}")
             nc.scalar.activation(square[:], relu[:], ACT.Square)
             scaled = tile([P, PACK, CHUNK], F32, f"scaled{c}_{g}")
             for t in range(PACK):
-                nc.scalar.activation(scaled[:, t, :], square[:, t, :], ACT.Copy, scale=factors[:, t : t + 1])
-            h = tile([P, CHUNK * PACK], BF16, f"h{c}_{g}")
-            interleave(h, scaled, ACT.Copy)
-            quantise(c, g, h)
+                nc.scalar.activation(scaled[:, t, :], square[:, t, :], ACT.Copy, scale=factors[:, g, t : t + 1])
+            interleave(h[c][:, g, :], scaled[:], ACT.Copy)
 
-        def gather_gates(first, name, on=None):
-            pair = tile([P, 2 * J], F32, name, on=on)
-            for k in range(2):
-                picked_g[first + k] = pair[:, k * J : (k + 1) * J]
+        def quantise(c):
+            nc.vector.quantize_mx(out=h_w[c][:].bitcast(FP8X4), scales=h_s[c][:], in_=h[c][:].rearrange("p g x -> p (g x)"))
+
+        def gather_gates(first, count, on=None):
+            dense = tile([P, count * J], F32, f"picked_g{first}", on=on)
+            for k in range(count):
+                picked_g[first + k] = dense[:, k * J : (k + 1) * J]
                 nc.vector.tensor_tensor(picked_g[first + k], gates[first + k][:].indirect(offsets[:]), wgo_sb[:], ALU.mult)
 
         def down(c, i):
@@ -204,44 +208,68 @@ def tile_list_modp_relu2_mix_gate_kernel(
                 out=y_ps[:],
                 lhsT=wd8_w[:, i * P : (i + 1) * P].bitcast(FP8X4),
                 lhsT_scale=wd_s[SCALE_ROWS:P, i * P : (i + 1) * P],
-                rhs=h_w[c, 0][:].bitcast(FP8X4),
-                rhs_scale=h_s[c, 0][:],
+                rhs=h_w[c][:, 0:CHUNK].bitcast(FP8X4),
+                rhs_scale=h_s[c][:, 0:CHUNK],
                 start=True,
                 stop=False,
             )
-            nc.tensor.matmul_mx(
-                out=y_ps[:],
-                lhsT=wd4_w[:, 2 * i * P : 2 * (i + 1) * P].bitcast(FP4X4),
-                lhsT_scale=wd_s[:, i * P : (i + 1) * P],
-                rhs=h_w[c, 1][:].bitcast(FP8X4),
-                rhs_scale=h_s[c, 1][:],
-                start=False,
-                stop=True,
-            )
+            for lo in range(0, CHUNK, P):
+                nc.tensor.matmul_mx(
+                    out=y_ps[:, lo : lo + P],
+                    lhsT=wd4_w[:, 2 * i * P : 2 * (i + 1) * P].bitcast(FP4X4),
+                    lhsT_scale=wd_s[:, i * P : (i + 1) * P],
+                    rhs=h_w[c][:, CHUNK + lo : CHUNK + lo + P].bitcast(FP8X4),
+                    rhs_scale=h_s[c][:, CHUNK + lo : CHUNK + lo + P],
+                    start=False,
+                    stop=(lo + P == CHUNK),
+                )
             return y_ps
 
-        def scatter(c, i, y_ps, on=None):
-            y = tile([P, CHUNK], F32, f"y{c}_{i}", on=on)
-            nc.scalar.copy(y[:], y_ps[:])
+        def scatter(c, rows, on=None):
+            y = tile([P, len(rows) * CHUNK], F32, f"y{c}_{rows[0]}", on=on)
+            for k, i in enumerate(rows):
+                part = y[:, k * CHUNK : (k + 1) * CHUNK]
+                nc.scalar.copy(part, down(c, i)[:])
+                nc.vector.tensor_tensor(
+                    pages[i][:].indirect(lists[c]), part, picked_g[i][:, c * CHUNK : (c + 1) * CHUNK], ALU.mult
+                )
+                if c == N_CHUNKS - 1:
+                    nc.sync.dma_start(out[i * P : (i + 1) * P, :], pages[i][:])
+
+        def scatter_last(i):
+            first = N_CHUNKS - 2
+            y = tile([P, 2 * CHUNK], F32, "y_last", on="square3_1")
+            for k in range(2):
+                nc.scalar.copy(y[:, k * CHUNK : (k + 1) * CHUNK], down(first + k, i)[:])
             nc.vector.tensor_tensor(
-                pages[i][:].indirect(lists[c]), y[:], picked_g[i][:, c * CHUNK : (c + 1) * CHUNK], ALU.mult
+                pages[i][:].indirect(offsets[:, first * cols :]), y[:], picked_g[i][:, first * CHUNK :], ALU.mult
             )
-            if c == N_CHUNKS - 1:
-                nc.sync.dma_start(out[i * P : (i + 1) * P, :], pages[i][:])
+            nc.sync.dma_start(out[i * P : (i + 1) * P, :], pages[i][:])
 
-        h_abs_first = hidden_unsigned(0, 0)
-        gates.append(tile([P, T], F32, f"gates{LAST}", on="relu0_0"))
-        nc.sync.dma_start(gates[LAST][:], gT[LAST * P : (LAST + 1) * P, :])
-        gather_gates(0, "picked_g_early")
-        sign_and_quantise(0, 0, h_abs_first, on="sm_sb")
-        sign_and_quantise(0, 1, hidden_unsigned(0, 1))
-        gather_gates(2, "picked_g_late", on="h0_1")
-        for i in range(LAST):
-            scatter(0, i, down(0, i))
-        y_ps_held = down(0, LAST)
-
-        sign_and_quantise(1, 0, hidden_unsigned(1, 0))
-        hidden_on_scalar(1, 1, sm_last, on="h_w0_1")
-        scatter(0, LAST, y_ps_held, on="scaled1_1")
-        for i in range(N_TILES):
-            scatter(1, i, down(1, i))
+        gather_gates(0, 1)
+        clear_page(on="tab_s")
+        hidden_signed_on_vector(0, 0)
+        gates.append(tile([P, T], F32, "gates3", on="relu0_0"))
+        nc.sync.dma_start(gates[3][:], gT[3 * P : 4 * P, :])
+        hidden_signed_on_vector(0, 1)
+        quantise(0)
+        clear_page(on="relu0_1")
+        gather_gates(1, 1, on="h_abs0_1")
+        scatter(0, [0, 1])
+        hidden_signed_on_vector(1, 0)
+        hidden_on_scalar(1, 1)
+        quantise(1)
+        gather_gates(2, 2, on="scaled1_1")
+        scatter(0, [2, 3], on="square1_1")
+        hidden_on_scalar(2, 0)
+        hidden_on_scalar(2, 1)
+        quantise(2)
+        scatter(1, [0], on="square2_1")
+        scatter(1, [1, 2, 3], on="scaled2_1")
+        hidden_on_scalar(3, 0)
+        hidden_on_scalar(3, 1)
+        quantise(3)
+        scatter(2, [0, 1], on="relu3_1")
+        scatter(2, [2], on="scaled3_1")
+        scatter(3, [0, 1, 2])
+        scatter_last(3)

@@ -58,9 +58,9 @@ def tile_list_modp_relu2_mix_gate_kernel(
         offsets = keep.tile([P, J // GROUP], U16, name="offsets")
         tab_w = tile([P, T], I32, "tab_w")
         tab_s = tile([P, T], U8, "tab_s")
-        wu_raw_w = tile([P, R], I32, "wu_raw_w")
+        wu_raw_w = [tile([P, PASS], I32, f"wu_raw_w{g}") for g in range(R_PASSES)]
         wu_raw_s = tile([P, PASS], U8, "wu_raw_s")
-        wu_w = tile([P, R], I32, "wu_w")
+        wu_w = [tile([P, PASS], I32, f"wu_w{g}") for g in range(R_PASSES)]
         wu_s = tile([P, PASS], U8, "wu_s")
         sm_sb = tile([P, R_PASSES, PACK], F32, "sm_sb")
 
@@ -68,7 +68,6 @@ def tile_list_modp_relu2_mix_gate_kernel(
         nc.vector.memset(wu_raw_s[:].bitcast(I32), 0)
         nc.sync.dma_start(offsets[:], offs)
         nc.sync.dma_start(sm_sb[:], sm.rearrange("(g p t) -> p g t", g=R_PASSES, t=PACK))
-        nc.sync.dma_start(wu_raw_w[:], wu_words[0].rearrange("p r i -> p (r i)").bitcast(I32))
         for q in range(QUADRANTS):
             nc.sync.dma_start(tab_s[scale_rows(q), :].bitcast(I32), tab_scales[0].bitcast(I32)[blocks(q), :])
         nc.sync.dma_start(tab_w[:], tab_words[0].rearrange("p t i -> p (t i)").bitcast(I32))
@@ -77,6 +76,9 @@ def tile_list_modp_relu2_mix_gate_kernel(
                 wu_raw_s[scale_rows(q, planes=R_PASSES), :].bitcast(I32),
                 wu_scales[0].bitcast(I32)[blocks(q), :].rearrange("q (g c) -> g q c", g=R_PASSES),
             )
+        wu_words32 = wu_words[0].rearrange("p r i -> p (r i)").bitcast(I32)
+        for g in range(R_PASSES):
+            nc.sync.dma_start(wu_raw_w[g][:], wu_words32[:, g * PASS : (g + 1) * PASS])
 
         root = tile([P, R_PASSES * PACK], F32, "root")
         for g in range(R_PASSES):
@@ -89,35 +91,33 @@ def tile_list_modp_relu2_mix_gate_kernel(
         for g in range(R_PASSES):
             nc.scalar.activation(signs[:, g], sm_sb[:, g, :].unsqueeze(1).to_broadcast([P, SIGN_RUN, PACK]), ACT.Sign)
 
-        pages = [tile([P, T], F32, f"page{i}") for i in range(2)]
+        pages = [tile([P, T], F32, f"page{i}") for i in range(3)]
         for page in pages:
             nc.vector.memset(page[:].bitcast(I32), 0)
         wd_s32 = tile([P, WD_PLANE_WORDS], I32, "wd_s32")
         nc.vector.memset(wd_s32[:], 0)
 
-        nc.vector.tensor_copy(
-            wu_w[:].rearrange("p (g t m) -> p g m t", g=R_PASSES, t=PACK),
-            wu_raw_w[:].rearrange("p (g m t) -> p g m t", g=R_PASSES, t=PACK),
-        )
         cols = CHUNK // GROUP
         lists = [offsets[:, c * cols : (c + 1) * cols] for c in range(N_CHUNKS)]
-        half = J // 2
-        early_s = tile([P, half], U8, "early_s")
-        nc.vector.tensor_copy(early_s[:], tab_s[:].indirect(offsets[:, : half // GROUP]))
+        all_s = tile([P, J], U8, "all_s")
+        nc.vector.tensor_copy(all_s[:], tab_s[:].indirect(offsets[:]))
+        first_w = tile([P, CHUNK], U32, "first_w")
+        nc.vector.tensor_copy(first_w[:], tab_w[:].bitcast(U32).indirect(lists[0]))
         nc.vector.tensor_copy(
             wu_s[:].rearrange("p (t m) -> p m t", t=PACK),
             wu_raw_s[:].rearrange("p (m t) -> p m t", t=PACK),
         )
-        first_w = tile([P, CHUNK], U32, "first_w")
-        nc.vector.tensor_copy(first_w[:], tab_w[:].bitcast(U32).indirect(lists[0]))
-        rest_w = tile([P, J - CHUNK], U32, "rest_w", on="wu_raw_s")
-        late_s = tile([P, half], U8, "late_s", on="tab_w")
+        for g in range(R_PASSES):
+            nc.vector.tensor_copy(
+                wu_w[g][:].rearrange("p (t m) -> p m t", t=PACK),
+                wu_raw_w[g][:].rearrange("p (m t) -> p m t", t=PACK),
+            )
+        rest_w = tile([P, J - CHUNK], U32, "rest_w", on="wu_raw_w1")
         nc.vector.tensor_copy(rest_w[:], tab_w[:].bitcast(U32).indirect(offsets[:, cols:]))
-        nc.vector.tensor_copy(late_s[:], tab_s[:].indirect(offsets[:, half // GROUP :]))
         picked_w = [first_w[:]] + [rest_w[:, c * CHUNK : (c + 1) * CHUNK] for c in range(N_CHUNKS - 1)]
-        picked_s = [s[:, k * CHUNK : (k + 1) * CHUNK] for s in (early_s, late_s) for k in range(half // CHUNK)]
+        picked_s = [all_s[:, c * CHUNK : (c + 1) * CHUNK] for c in range(N_CHUNKS)]
 
-        gates = [tile([P, T], F32, f"gates{i}", on=name) for i, name in enumerate(("sm_abs0", "wu_raw_w", "first_w"))]
+        gates = [tile([P, T], F32, f"gates{i}", on=name) for i, name in enumerate(("sm_abs0", "wu_raw_s", "first_w"))]
         wgo_sb = tile([P, J], F32, "wgo_sb", on="sm_abs1")
         wd = tile([P, WD8_WORDS + WD4_WORDS], I32, "wd", on="sm_sb")
         wd8_w = wd[:, 0:WD8_WORDS]
@@ -134,7 +134,9 @@ def tile_list_modp_relu2_mix_gate_kernel(
         wd4_w = wd4_w32.bitcast(U8)
         wd_s = wd_s32[:].bitcast(U8)
 
-        h = [tile([P, R_PASSES, CHUNK * PACK], BF16, f"h{c}") for c in range(N_CHUNKS)]
+        h = [
+            tile([P, R_PASSES, CHUNK * PACK], BF16, f"h{c}", on="sm_abs0" if c == 0 else None) for c in range(N_CHUNKS)
+        ]
         h_w = [tile([P, R_PASSES * CHUNK], U32, f"h_w{c}") for c in range(N_CHUNKS)]
         h_s = [tile([P, R_PASSES * CHUNK], U8, f"h_s{c}") for c in range(N_CHUNKS)]
         picked_g = {}
@@ -149,7 +151,7 @@ def tile_list_modp_relu2_mix_gate_kernel(
                 t = first + k
                 nc.tensor.matmul_mx(
                     out=a[:, k, :],
-                    lhsT=wu_w[:, g * PASS + t * P : g * PASS + (t + 1) * P].bitcast(FP8X4),
+                    lhsT=wu_w[g][:, t * P : (t + 1) * P].bitcast(FP8X4),
                     lhsT_scale=wu_s[SCALE_ROWS * g : P, t * P : (t + 1) * P],
                     rhs=picked_w[c].bitcast(FP8X4),
                     rhs_scale=picked_s[c],
@@ -165,8 +167,8 @@ def tile_list_modp_relu2_mix_gate_kernel(
                 func,
             )
 
-        def hidden_signed_on_vector(c, g):
-            relu = tile([P, PACK, CHUNK], F32, f"relu{c}_{g}")
+        def hidden_signed_on_vector(c, g, on=None):
+            relu = tile([P, PACK, CHUNK], F32, f"relu{c}_{g}", on=on)
             for first in range(0, PACK, PAIR):
                 a = up_pair(c, g, first)
                 for k in range(PAIR):
@@ -182,11 +184,11 @@ def tile_list_modp_relu2_mix_gate_kernel(
                 ALU.mult,
             )
 
-        def hidden_on_scalar(c, g):
-            relu = tile([P, PACK, CHUNK], F32, f"relu{c}_{g}")
+        def hidden_on_scalar(c, g, on=None, square_on=None):
+            relu = tile([P, PACK, CHUNK], F32, f"relu{c}_{g}", on=on)
             for first in range(0, PACK, PAIR):
                 nc.scalar.activation(relu[:, first : first + PAIR, :], up_pair(c, g, first)[:], ACT.Relu)
-            square = tile([P, PACK, CHUNK], F32, f"square{c}_{g}")
+            square = tile([P, PACK, CHUNK], F32, f"square{c}_{g}", on=square_on)
             nc.scalar.activation(square[:], relu[:], ACT.Square)
             scaled = tile([P, PACK, CHUNK], F32, f"scaled{c}_{g}")
             for t in range(PACK):
@@ -202,10 +204,9 @@ def tile_list_modp_relu2_mix_gate_kernel(
                 picked_g[first + k] = dense[:, k * J : (k + 1) * J]
                 nc.vector.tensor_tensor(picked_g[first + k], gates[first + k][:].indirect(offsets[:]), wgo_sb[:], ALU.mult)
 
-        def down(c, i):
-            y_ps = down_psum.tile([P, CHUNK], F32, name="y_ps")
+        def down(y_ps, c, i):
             nc.tensor.matmul_mx(
-                out=y_ps[:],
+                out=y_ps,
                 lhsT=wd8_w[:, i * P : (i + 1) * P].bitcast(FP8X4),
                 lhsT_scale=wd_s[SCALE_ROWS:P, i * P : (i + 1) * P],
                 rhs=h_w[c][:, 0:CHUNK].bitcast(FP8X4),
@@ -223,53 +224,57 @@ def tile_list_modp_relu2_mix_gate_kernel(
                     start=False,
                     stop=(lo + P == CHUNK),
                 )
-            return y_ps
 
-        def scatter(c, rows, on=None):
-            y = tile([P, len(rows) * CHUNK], F32, f"y{c}_{rows[0]}", on=on)
-            for k, i in enumerate(rows):
-                part = y[:, k * CHUNK : (k + 1) * CHUNK]
-                nc.scalar.copy(part, down(c, i)[:])
+        begun = {}
+
+        def begin_down(first, i):
+            begun[first, i] = down_psum.tile([P, BANK], F32, name="y_ps")
+            down(begun[first, i][:, 0:CHUNK], first, i)
+            return begun[first, i]
+
+        def scatter(items, on=None):
+            y = tile([P, sum(count for first, count, i in items) * CHUNK], F32, "y%d_%d" % items[0][::2], on=on)
+            at = 0
+            for first, count, i in items:
+                width = count * CHUNK
+                y_ps = begun[first, i] if (first, i) in begun else begin_down(first, i)
+                for c in range(1, count):
+                    down(y_ps[:, c * CHUNK : (c + 1) * CHUNK], first + c, i)
+                part = y[:, at : at + width]
+                at = at + width
+                nc.scalar.copy(part, y_ps[:, 0:width])
                 nc.vector.tensor_tensor(
-                    pages[i][:].indirect(lists[c]), part, picked_g[i][:, c * CHUNK : (c + 1) * CHUNK], ALU.mult
+                    pages[i][:].indirect(offsets[:, first * cols : (first + count) * cols]),
+                    part,
+                    picked_g[i][:, first * CHUNK : first * CHUNK + width],
+                    ALU.mult,
                 )
-                if c == N_CHUNKS - 1:
+                if first + count == N_CHUNKS:
                     nc.sync.dma_start(out[i * P : (i + 1) * P, :], pages[i][:])
 
-        def scatter_last(i):
-            first = N_CHUNKS - 2
-            y = tile([P, 2 * CHUNK], F32, "y_last", on="square3_1")
-            for k in range(2):
-                nc.scalar.copy(y[:, k * CHUNK : (k + 1) * CHUNK], down(first + k, i)[:])
-            nc.vector.tensor_tensor(
-                pages[i][:].indirect(offsets[:, first * cols :]), y[:], picked_g[i][:, first * CHUNK :], ALU.mult
-            )
-            nc.sync.dma_start(out[i * P : (i + 1) * P, :], pages[i][:])
-
+        clear_page(on="tab_w")
         gather_gates(0, 1)
-        clear_page(on="tab_s")
         hidden_signed_on_vector(0, 0)
         gates.append(tile([P, T], F32, "gates3", on="relu0_0"))
         nc.sync.dma_start(gates[3][:], gT[3 * P : 4 * P, :])
         hidden_signed_on_vector(0, 1)
         quantise(0)
-        clear_page(on="relu0_1")
-        gather_gates(1, 1, on="h_abs0_1")
-        scatter(0, [0, 1])
+        gather_gates(1, 1, on="sm_abs0")
+        scatter([(0, 1, 0), (0, 1, 1)])
+        begin_down(0, 2)
+        begin_down(0, 3)
         hidden_signed_on_vector(1, 0)
-        hidden_on_scalar(1, 1)
+        hidden_on_scalar(1, 1, square_on="h_w0")
         quantise(1)
         gather_gates(2, 2, on="scaled1_1")
-        scatter(0, [2, 3], on="square1_1")
-        hidden_on_scalar(2, 0)
-        hidden_on_scalar(2, 1)
+        hidden_signed_on_vector(2, 0, on="h_w0")
+        hidden_on_scalar(2, 1, on="relu1_1")
         quantise(2)
-        scatter(1, [0], on="square2_1")
-        scatter(1, [1, 2, 3], on="scaled2_1")
-        hidden_on_scalar(3, 0)
-        hidden_on_scalar(3, 1)
+        scatter([(0, 2, 2)], on="relu1_1")
+        scatter([(0, 2, 3), (1, 1, 0), (1, 1, 1)], on="scaled2_1")
+        hidden_on_scalar(3, 0, on="square2_1")
+        hidden_on_scalar(3, 1, on="square3_0")
         quantise(3)
-        scatter(2, [0, 1], on="relu3_1")
-        scatter(2, [2], on="scaled3_1")
-        scatter(3, [0, 1, 2])
-        scatter_last(3)
+        scatter([(2, 1, 0), (2, 1, 1)], on="scaled3_0")
+        scatter([(2, 1, 2)], on="scaled3_1")
+        scatter([(3, 1, 0), (3, 1, 1), (3, 1, 2), (2, 2, 3)])

@@ -35,6 +35,11 @@ SIGN_RUN = 16
 WD8_WORDS = N
 WD4_WORDS = N // 2
 WD_PLANE_WORDS = N // 4
+UP_BANKS = {(0, 0): 0, (0, 1): 2, (1, 0): 0, (1, 1): 2, (2, 0): 4, (2, 1): 0, (3, 0): 4, (3, 1): 0}
+DOWN_BANKS = {
+    (0, 0): 4, (0, 1): 5, (0, 2): 6, (0, 3): 7, (1, 0): 2, (1, 1): 3, (2, 0): 6, (2, 1): 7, (2, 2): 2,
+    (3, 0): 3, (3, 1): 4, (3, 2): 5, (2, 3): 0,
+}
 
 
 def tile_list_modp_relu2_mix_gate_kernel(
@@ -43,8 +48,7 @@ def tile_list_modp_relu2_mix_gate_kernel(
     nc = tc.nc
     with ExitStack() as ctx:
         keep = ctx.enter_context(tc.tile_pool(name="keep", bufs=1))
-        up_psum = ctx.enter_context(tc.psum_pool(name="up_psum", bufs=PACK))
-        down_psum = ctx.enter_context(tc.psum_pool(name="down_psum", bufs=N_TILES))
+        psum = ctx.enter_context(tc.psum_pool(name="psum", bufs=1))
 
         def tile(shape, dtype, name, on=None):
             return keep.tile(shape, dtype, name=name, tag=on or name, align_bytes=64)
@@ -91,7 +95,7 @@ def tile_list_modp_relu2_mix_gate_kernel(
         for g in range(R_PASSES):
             nc.scalar.activation(signs[:, g], sm_sb[:, g, :].unsqueeze(1).to_broadcast([P, SIGN_RUN, PACK]), ACT.Sign)
 
-        pages = [tile([P, T], F32, f"page{i}") for i in range(3)]
+        pages = [tile([P, T], F32, f"page{i}") for i in range(2)]
         for page in pages:
             nc.vector.memset(page[:].bitcast(I32), 0)
         wd_s32 = tile([P, WD_PLANE_WORDS], I32, "wd_s32")
@@ -112,24 +116,27 @@ def tile_list_modp_relu2_mix_gate_kernel(
                 wu_w[g][:].rearrange("p (t m) -> p m t", t=PACK),
                 wu_raw_w[g][:].rearrange("p (m t) -> p m t", t=PACK),
             )
+        pages.append(tile([P, T], F32, "page2", on="wu_raw_w0"))
+        nc.vector.memset(pages[2][:].bitcast(I32), 0)
         rest_w = tile([P, J - CHUNK], U32, "rest_w", on="wu_raw_w1")
         nc.vector.tensor_copy(rest_w[:], tab_w[:].bitcast(U32).indirect(offsets[:, cols:]))
         picked_w = [first_w[:]] + [rest_w[:, c * CHUNK : (c + 1) * CHUNK] for c in range(N_CHUNKS - 1)]
         picked_s = [all_s[:, c * CHUNK : (c + 1) * CHUNK] for c in range(N_CHUNKS)]
 
-        gates = [tile([P, T], F32, f"gates{i}", on=name) for i, name in enumerate(("sm_abs0", "wu_raw_s", "first_w"))]
+        gates = [tile([P, T], F32, f"gates{i}", on=name) for i, name in enumerate(("sm_abs0", "sm_sb", "first_w"))]
         wgo_sb = tile([P, J], F32, "wgo_sb", on="sm_abs1")
-        wd = tile([P, WD8_WORDS + WD4_WORDS], I32, "wd", on="sm_sb")
+        wd = tile([P, WD8_WORDS + WD4_WORDS], I32, "wd", on="tab_s")
         wd8_w = wd[:, 0:WD8_WORDS]
         wd4_w32 = wd[:, WD8_WORDS:]
         nc.sync.dma_start(gates[0][:], gT[0:P, :])
         nc.sync.dma_start(wgo_sb[:], wgo)
+        for q in range(QUADRANTS):
+            nc.sync.dma_start(wd_s32[scale_rows(q, first=1), :], wd8_scales[0].bitcast(I32)[blocks(q), :])
+        nc.sync.dma_start(gates[1][:], gT[P : 2 * P, :])
         nc.sync.dma_start(wd8_w, wd8_words[0].rearrange("p n i -> p (n i)").bitcast(I32))
         nc.sync.dma_start(wd4_w32, wd4_words[0].bitcast(I32))
         for q in range(QUADRANTS):
             nc.sync.dma_start(wd_s32[scale_rows(q), :], wd4_scales[0].bitcast(I32)[blocks(q), :])
-            nc.sync.dma_start(wd_s32[scale_rows(q, first=1), :], wd8_scales[0].bitcast(I32)[blocks(q), :])
-        nc.sync.dma_start(gates[1][:], gT[P : 2 * P, :])
         nc.sync.dma_start(gates[2][:], gT[2 * P : 3 * P, :])
         wd4_w = wd4_w32.bitcast(U8)
         wd_s = wd_s32[:].bitcast(U8)
@@ -141,12 +148,12 @@ def tile_list_modp_relu2_mix_gate_kernel(
         h_s = [tile([P, R_PASSES * CHUNK], U8, f"h_s{c}") for c in range(N_CHUNKS)]
         picked_g = {}
 
-        def clear_page(on):
+        def clear_page(engine, on):
             pages.append(tile([P, T], F32, f"page{len(pages)}", on=on))
-            nc.vector.memset(pages[-1][:].bitcast(I32), 0)
+            engine.memset(pages[-1][:].bitcast(I32), 0)
 
         def up_pair(c, g, first):
-            a = up_psum.tile([P, PAIR, CHUNK], F32, name="a")
+            a = psum.tile([P, PAIR, CHUNK], F32, name="a", tag=f"bank{UP_BANKS[c, g] + first // PAIR}")
             for k in range(PAIR):
                 t = first + k
                 nc.tensor.matmul_mx(
@@ -184,12 +191,15 @@ def tile_list_modp_relu2_mix_gate_kernel(
                 ALU.mult,
             )
 
-        def hidden_on_scalar(c, g, on=None, square_on=None):
+        def squared(c, g, on=None, square_on=None):
             relu = tile([P, PACK, CHUNK], F32, f"relu{c}_{g}", on=on)
             for first in range(0, PACK, PAIR):
                 nc.scalar.activation(relu[:, first : first + PAIR, :], up_pair(c, g, first)[:], ACT.Relu)
             square = tile([P, PACK, CHUNK], F32, f"square{c}_{g}", on=square_on)
             nc.scalar.activation(square[:], relu[:], ACT.Square)
+            return square
+
+        def scale_and_round(c, g, square):
             scaled = tile([P, PACK, CHUNK], F32, f"scaled{c}_{g}")
             for t in range(PACK):
                 nc.scalar.activation(scaled[:, t, :], square[:, t, :], ACT.Copy, scale=factors[:, g, t : t + 1])
@@ -228,7 +238,7 @@ def tile_list_modp_relu2_mix_gate_kernel(
         begun = {}
 
         def begin_down(first, i):
-            begun[first, i] = down_psum.tile([P, BANK], F32, name="y_ps")
+            begun[first, i] = psum.tile([P, BANK], F32, name="y_ps", tag=f"bank{DOWN_BANKS[first, i]}")
             down(begun[first, i][:, 0:CHUNK], first, i)
             return begun[first, i]
 
@@ -252,29 +262,29 @@ def tile_list_modp_relu2_mix_gate_kernel(
                 if first + count == N_CHUNKS:
                     nc.sync.dma_start(out[i * P : (i + 1) * P, :], pages[i][:])
 
-        clear_page(on="tab_w")
         gather_gates(0, 1)
         hidden_signed_on_vector(0, 0)
         gates.append(tile([P, T], F32, "gates3", on="relu0_0"))
         nc.sync.dma_start(gates[3][:], gT[3 * P : 4 * P, :])
         hidden_signed_on_vector(0, 1)
         quantise(0)
-        gather_gates(1, 1, on="sm_abs0")
+        gather_gates(1, 1, on="h_abs0_1")
+        clear_page(nc.gpsimd, on="sm_sb")
         scatter([(0, 1, 0), (0, 1, 1)])
         begin_down(0, 2)
         begin_down(0, 3)
         hidden_signed_on_vector(1, 0)
-        hidden_on_scalar(1, 1, square_on="h_w0")
+        scale_and_round(1, 1, squared(1, 1, square_on="h_w0"))
         quantise(1)
         gather_gates(2, 2, on="scaled1_1")
-        hidden_signed_on_vector(2, 0, on="h_w0")
-        hidden_on_scalar(2, 1, on="relu1_1")
+        hidden_signed_on_vector(2, 0)
+        scatter([(0, 2, 2), (1, 1, 0)], on="relu2_0")
+        scale_and_round(2, 1, squared(2, 1, on="relu1_1"))
         quantise(2)
-        scatter([(0, 2, 2)], on="relu1_1")
-        scatter([(0, 2, 3), (1, 1, 0), (1, 1, 1)], on="scaled2_1")
-        hidden_on_scalar(3, 0, on="square2_1")
-        hidden_on_scalar(3, 1, on="square3_0")
-        quantise(3)
+        scatter([(0, 2, 3), (1, 1, 1)], on="scaled2_1")
+        scale_and_round(3, 0, squared(3, 0))
         scatter([(2, 1, 0), (2, 1, 1)], on="scaled3_0")
+        scale_and_round(3, 1, squared(3, 1))
+        quantise(3)
         scatter([(2, 1, 2)], on="scaled3_1")
         scatter([(3, 1, 0), (3, 1, 1), (3, 1, 2), (2, 2, 3)])

@@ -1,6 +1,7 @@
 from contextlib import ExitStack
 
 import concourse.mybir as mybir
+from concourse.masks import make_identity
 
 K, R, N, T, J = 512, 1024, 512, 2048, 1024
 FLOPS = 2 * K * R * J + 2 * R * N * J
@@ -35,7 +36,9 @@ SIGN_RUN = 16
 WD8_WORDS = N
 WD4_WORDS = N // 2
 WD_PLANE_WORDS = N // 4
-UP_BANKS = {(0, 0): 0, (0, 1): 2, (1, 0): 0, (1, 1): 2, (2, 0): 4, (2, 1): 0, (3, 0): 4, (3, 1): 0}
+WGO_RUN = J // P
+PROBE = False
+UP_BANKS = {(0, 0): 0, (0, 1): 4, (1, 0): 0, (1, 1): 2, (2, 0): 4, (2, 1): 0, (3, 0): 4, (3, 1): 0}
 DOWN_BANKS = {
     (0, 0): 4, (0, 1): 5, (0, 2): 6, (0, 3): 7, (1, 0): 2, (1, 1): 3, (2, 0): 6, (2, 1): 7, (2, 2): 2,
     (3, 0): 3, (3, 1): 4, (3, 2): 5, (2, 3): 0,
@@ -72,8 +75,12 @@ def tile_list_modp_relu2_mix_gate_kernel(
         nc.vector.memset(wu_raw_s[:].bitcast(I32), 0)
         nc.sync.dma_start(offsets[:], offs)
         nc.sync.dma_start(sm_sb[:], sm.rearrange("(g p t) -> p g t", g=R_PASSES, t=PACK))
-        for q in range(QUADRANTS):
-            nc.sync.dma_start(tab_s[scale_rows(q), :].bitcast(I32), tab_scales[0].bitcast(I32)[blocks(q), :])
+        wgo_row = tile([P, WGO_RUN], F32, "wgo_row")
+        nc.sync.dma_start(wgo_row[:], wgo[0].rearrange("(p i) -> p i", i=WGO_RUN))
+        identity = tile([P, P], F32, "identity")
+        make_identity(nc, identity[:])
+        for r in range(SCALE_ROWS):
+            nc.sync.dma_start(tab_s[r:P:QUAD, :].bitcast(I32), tab_scales[0].bitcast(I32)[r::SCALE_ROWS, :])
         nc.sync.dma_start(tab_w[:], tab_words[0].rearrange("p t i -> p (t i)").bitcast(I32))
         for q in range(QUADRANTS):
             nc.sync.dma_start(
@@ -95,9 +102,19 @@ def tile_list_modp_relu2_mix_gate_kernel(
         for g in range(R_PASSES):
             nc.scalar.activation(signs[:, g], sm_sb[:, g, :].unsqueeze(1).to_broadcast([P, SIGN_RUN, PACK]), ACT.Sign)
 
-        pages = [tile([P, T], F32, f"page{i}") for i in range(2)]
-        for page in pages:
-            nc.vector.memset(page[:].bitcast(I32), 0)
+        wgo_sb = tile([P, J], F32, "wgo_sb")
+        for b in range(WGO_RUN // LINE):
+            spread = psum.tile([P, LINE, P], F32, name="spread", tag=f"bank{6 + b}")
+            for k in range(LINE):
+                i = b * LINE + k
+                nc.tensor.transpose(spread[:, k, :], wgo_row[:, i : i + 1].to_broadcast([P, P]), identity[:])
+            nc.scalar.copy(
+                wgo_sb[:].rearrange("p (m i) -> p m i", i=WGO_RUN)[:, :, b * LINE : (b + 1) * LINE],
+                spread[:].rearrange("p k m -> p m k"),
+            )
+
+        pages = [tile([P, T], F32, "page0")]
+        nc.vector.memset(pages[0][:].bitcast(I32), 0)
         wd_s32 = tile([P, WD_PLANE_WORDS], I32, "wd_s32")
         nc.vector.memset(wd_s32[:], 0)
 
@@ -116,28 +133,24 @@ def tile_list_modp_relu2_mix_gate_kernel(
                 wu_w[g][:].rearrange("p (t m) -> p m t", t=PACK),
                 wu_raw_w[g][:].rearrange("p (m t) -> p m t", t=PACK),
             )
-        pages.append(tile([P, T], F32, "page2", on="wu_raw_w0"))
-        nc.vector.memset(pages[2][:].bitcast(I32), 0)
         rest_w = tile([P, J - CHUNK], U32, "rest_w", on="wu_raw_w1")
         nc.vector.tensor_copy(rest_w[:], tab_w[:].bitcast(U32).indirect(offsets[:, cols:]))
         picked_w = [first_w[:]] + [rest_w[:, c * CHUNK : (c + 1) * CHUNK] for c in range(N_CHUNKS - 1)]
         picked_s = [all_s[:, c * CHUNK : (c + 1) * CHUNK] for c in range(N_CHUNKS)]
 
-        gates = [tile([P, T], F32, f"gates{i}", on=name) for i, name in enumerate(("sm_abs0", "sm_sb", "first_w"))]
-        wgo_sb = tile([P, J], F32, "wgo_sb", on="sm_abs1")
+        gates = [tile([P, T], F32, f"gates{i}", on=name) for i, name in enumerate(("sm_abs1", "sm_abs0", "sm_sb"))]
         wd = tile([P, WD8_WORDS + WD4_WORDS], I32, "wd", on="tab_s")
         wd8_w = wd[:, 0:WD8_WORDS]
         wd4_w32 = wd[:, WD8_WORDS:]
         nc.sync.dma_start(gates[0][:], gT[0:P, :])
-        nc.sync.dma_start(wgo_sb[:], wgo)
+        nc.sync.dma_start(gates[1][:], gT[P : 2 * P, :])
         for q in range(QUADRANTS):
             nc.sync.dma_start(wd_s32[scale_rows(q, first=1), :], wd8_scales[0].bitcast(I32)[blocks(q), :])
-        nc.sync.dma_start(gates[1][:], gT[P : 2 * P, :])
+        nc.sync.dma_start(gates[2][:], gT[2 * P : 3 * P, :])
         nc.sync.dma_start(wd8_w, wd8_words[0].rearrange("p n i -> p (n i)").bitcast(I32))
         nc.sync.dma_start(wd4_w32, wd4_words[0].bitcast(I32))
         for q in range(QUADRANTS):
             nc.sync.dma_start(wd_s32[scale_rows(q), :], wd4_scales[0].bitcast(I32)[blocks(q), :])
-        nc.sync.dma_start(gates[2][:], gT[2 * P : 3 * P, :])
         wd4_w = wd4_w32.bitcast(U8)
         wd_s = wd_s32[:].bitcast(U8)
 
@@ -152,9 +165,9 @@ def tile_list_modp_relu2_mix_gate_kernel(
             pages.append(tile([P, T], F32, f"page{len(pages)}", on=on))
             engine.memset(pages[-1][:].bitcast(I32), 0)
 
-        def up_pair(c, g, first):
-            a = psum.tile([P, PAIR, CHUNK], F32, name="a", tag=f"bank{UP_BANKS[c, g] + first // PAIR}")
-            for k in range(PAIR):
+        def up_pair(c, g, first, count=PAIR):
+            a = psum.tile([P, count, CHUNK], F32, name="a", tag=f"bank{UP_BANKS[c, g] + first // count}")
+            for k in range(count):
                 t = first + k
                 nc.tensor.matmul_mx(
                     out=a[:, k, :],
@@ -174,11 +187,11 @@ def tile_list_modp_relu2_mix_gate_kernel(
                 func,
             )
 
-        def hidden_signed_on_vector(c, g, on=None):
+        def hidden_signed_on_vector(c, g, on=None, count=PAIR):
             relu = tile([P, PACK, CHUNK], F32, f"relu{c}_{g}", on=on)
-            for first in range(0, PACK, PAIR):
-                a = up_pair(c, g, first)
-                for k in range(PAIR):
+            for first in range(0, PACK, count):
+                a = up_pair(c, g, first, count)
+                for k in range(count):
                     col = g * PACK + first + k
                     nc.scalar.activation(relu[:, first + k, :], a[:, k, :], ACT.Relu, scale=root[:, col : col + 1])
             h_abs = tile([P, CHUNK * PACK], BF16, f"h_abs{c}_{g}")
@@ -191,22 +204,29 @@ def tile_list_modp_relu2_mix_gate_kernel(
                 ALU.mult,
             )
 
-        def squared(c, g, on=None, square_on=None):
+        def rectified(c, g, on=None):
             relu = tile([P, PACK, CHUNK], F32, f"relu{c}_{g}", on=on)
             for first in range(0, PACK, PAIR):
                 nc.scalar.activation(relu[:, first : first + PAIR, :], up_pair(c, g, first)[:], ACT.Relu)
-            square = tile([P, PACK, CHUNK], F32, f"square{c}_{g}", on=square_on)
+            return relu
+
+        def squared(c, g, relu):
+            square = tile([P, PACK, CHUNK], F32, f"square{c}_{g}")
             nc.scalar.activation(square[:], relu[:], ACT.Square)
             return square
 
-        def scale_and_round(c, g, square):
-            scaled = tile([P, PACK, CHUNK], F32, f"scaled{c}_{g}")
+        def scale_and_round(c, g, square, on=None):
+            scaled = tile([P, PACK, CHUNK], F32, f"scaled{c}_{g}", on=on)
             for t in range(PACK):
                 nc.scalar.activation(scaled[:, t, :], square[:, t, :], ACT.Copy, scale=factors[:, g, t : t + 1])
             interleave(h[c][:, g, :], scaled[:], ACT.Copy)
 
         def quantise(c):
             nc.vector.quantize_mx(out=h_w[c][:].bitcast(FP8X4), scales=h_s[c][:], in_=h[c][:].rearrange("p g x -> p (g x)"))
+
+        def quantise_part(c, g):
+            part = slice(g * CHUNK, (g + 1) * CHUNK)
+            nc.vector.quantize_mx(out=h_w[c][:, part].bitcast(FP8X4), scales=h_s[c][:, part], in_=h[c][:, g, :])
 
         def gather_gates(first, count, on=None):
             dense = tile([P, count * J], F32, f"picked_g{first}", on=on)
@@ -262,29 +282,41 @@ def tile_list_modp_relu2_mix_gate_kernel(
                 if first + count == N_CHUNKS:
                     nc.sync.dma_start(out[i * P : (i + 1) * P, :], pages[i][:])
 
-        gather_gates(0, 1)
-        hidden_signed_on_vector(0, 0)
+        clocks = []
+
+        def clock(ap, dtype):
+            clocks.append(tile([P, 1], dtype, f"clock{len(clocks)}"))
+            nc.gpsimd.tensor_copy(clocks[-1][:], ap)
+
+        gather_gates(0, 2)
+        hidden_signed_on_vector(0, 0, count=1)
         gates.append(tile([P, T], F32, "gates3", on="relu0_0"))
         nc.sync.dma_start(gates[3][:], gT[3 * P : 4 * P, :])
         hidden_signed_on_vector(0, 1)
-        quantise(0)
-        gather_gates(1, 1, on="h_abs0_1")
-        clear_page(nc.gpsimd, on="sm_sb")
+        quantise_part(0, 0)
+        quantise_part(0, 1)
+        gather_gates(2, 1, on="h_abs0_1")
+        clear_page(nc.gpsimd, on=None if PROBE else "sm_abs0")
         scatter([(0, 1, 0), (0, 1, 1)])
         begin_down(0, 2)
         begin_down(0, 3)
+        clear_page(nc.gpsimd, on="h_s0")
         hidden_signed_on_vector(1, 0)
-        scale_and_round(1, 1, squared(1, 1, square_on="h_w0"))
+        scale_and_round(1, 1, squared(1, 1, rectified(1, 1)), on="h_w0")
         quantise(1)
-        gather_gates(2, 2, on="scaled1_1")
+        clear_page(nc.gpsimd, on="h1")
+        gather_gates(3, 1, on="h_w0")
         hidden_signed_on_vector(2, 0)
+        relu = rectified(2, 1, on="square1_1")
         scatter([(0, 2, 2), (1, 1, 0)], on="relu2_0")
-        scale_and_round(2, 1, squared(2, 1, on="relu1_1"))
+        scale_and_round(2, 1, squared(2, 1, relu))
         quantise(2)
         scatter([(0, 2, 3), (1, 1, 1)], on="scaled2_1")
-        scale_and_round(3, 0, squared(3, 0))
-        scatter([(2, 1, 0), (2, 1, 1)], on="scaled3_0")
-        scale_and_round(3, 1, squared(3, 1))
+        hidden_signed_on_vector(3, 0)
+        relu = rectified(3, 1)
+        square = squared(3, 1, relu)
+        scatter([(2, 1, 0), (2, 1, 1)], on="relu3_1")
+        scale_and_round(3, 1, square)
         quantise(3)
         scatter([(2, 1, 2)], on="scaled3_1")
         scatter([(3, 1, 0), (3, 1, 1), (3, 1, 2), (2, 2, 3)])

@@ -25,23 +25,26 @@ QUAD = P // QUADRANTS
 SCALE_ROWS = 4
 GROUP = 16
 CHUNK = 256
+COLS = CHUNK // GROUP
 BANK = 512
 PAIR = BANK // CHUNK
 N_CHUNKS = J // CHUNK
 R_PASSES = R // PASS
-N_TILES = N // P
-LAST = N_TILES - 1
 LINE = 4
 SIGN_RUN = 16
+SHARED = CHUNK // 2
 WD8_WORDS = N
 WD4_WORDS = N // 2
 WD_PLANE_WORDS = N // 4
 WGO_RUN = J // P
-PROBE = False
+WGO_BANK = 6
+
 UP_BANKS = {(0, 0): 0, (0, 1): 4, (1, 0): 0, (1, 1): 2, (2, 0): 4, (2, 1): 0, (3, 0): 4, (3, 1): 0}
 DOWN_BANKS = {
-    (0, 0): 4, (0, 1): 5, (0, 2): 6, (0, 3): 7, (1, 0): 2, (1, 1): 3, (2, 0): 6, (2, 1): 7, (2, 2): 2,
-    (3, 0): 3, (3, 1): 4, (3, 2): 5, (2, 3): 0,
+    (0, 0): 4, (0, 1): 5, (0, 2): 6, (0, 3): 7,
+    (1, 0): 2, (1, 1): 3,
+    (2, 0): 6, (2, 1): 7, (2, 2): 2, (2, 3): 0,
+    (3, 0): 3, (3, 1): 4, (3, 2): 5,
 }
 
 
@@ -96,15 +99,18 @@ def tile_list_modp_relu2_mix_gate_kernel(
             sm_abs = tile([P, PACK], F32, f"sm_abs{g}")
             nc.scalar.activation(sm_abs[:], sm_sb[:, g, :], ACT.Abs)
             nc.scalar.activation(root[:, g * PACK : (g + 1) * PACK], sm_abs[:], ACT.Sqrt)
-        factors = tile([P, R_PASSES, PACK], F32, "factors")
-        nc.scalar.copy(factors[:], sm_sb[:])
+        sm_pass1 = tile([P, PACK], F32, "sm_pass1")
+        nc.scalar.copy(sm_pass1[:], sm_sb[:, 1, :])
         signs = tile([P, R_PASSES, SIGN_RUN, PACK], BF16, "signs")
         for g in range(R_PASSES):
             nc.scalar.activation(signs[:, g], sm_sb[:, g, :].unsqueeze(1).to_broadcast([P, SIGN_RUN, PACK]), ACT.Sign)
+        sign_pass0 = tile([P, PACK], F32, "sign_pass0")
+        nc.scalar.activation(sign_pass0[:], sm_sb[:, 0, :], ACT.Sign)
 
         wgo_sb = tile([P, J], F32, "wgo_sb")
+        wgo_low = tile([P, J // 2], F32, "wgo_low")
         for b in range(WGO_RUN // LINE):
-            spread = psum.tile([P, LINE, P], F32, name="spread", tag=f"bank{6 + b}")
+            spread = psum.tile([P, LINE, P], F32, name="spread", tag=f"bank{WGO_BANK + b}")
             for k in range(LINE):
                 i = b * LINE + k
                 nc.tensor.transpose(spread[:, k, :], wgo_row[:, i : i + 1].to_broadcast([P, P]), identity[:])
@@ -112,18 +118,20 @@ def tile_list_modp_relu2_mix_gate_kernel(
                 wgo_sb[:].rearrange("p (m i) -> p m i", i=WGO_RUN)[:, :, b * LINE : (b + 1) * LINE],
                 spread[:].rearrange("p k m -> p m k"),
             )
+            nc.scalar.copy(
+                wgo_low[:].rearrange("p (m i) -> p m i", i=WGO_RUN)[:, :, b * LINE : (b + 1) * LINE],
+                spread[:, :, 0 : P // 2].rearrange("p k m -> p m k"),
+            )
 
         pages = [tile([P, T], F32, "page0")]
         nc.vector.memset(pages[0][:].bitcast(I32), 0)
         wd_s32 = tile([P, WD_PLANE_WORDS], I32, "wd_s32")
         nc.vector.memset(wd_s32[:], 0)
 
-        cols = CHUNK // GROUP
-        lists = [offsets[:, c * cols : (c + 1) * cols] for c in range(N_CHUNKS)]
         all_s = tile([P, J], U8, "all_s")
         nc.vector.tensor_copy(all_s[:], tab_s[:].indirect(offsets[:]))
         first_w = tile([P, CHUNK], U32, "first_w")
-        nc.vector.tensor_copy(first_w[:], tab_w[:].bitcast(U32).indirect(lists[0]))
+        nc.vector.tensor_copy(first_w[:], tab_w[:].bitcast(U32).indirect(offsets[:, 0:COLS]))
         nc.vector.tensor_copy(
             wu_s[:].rearrange("p (t m) -> p m t", t=PACK),
             wu_raw_s[:].rearrange("p (m t) -> p m t", t=PACK),
@@ -134,7 +142,7 @@ def tile_list_modp_relu2_mix_gate_kernel(
                 wu_raw_w[g][:].rearrange("p (m t) -> p m t", t=PACK),
             )
         rest_w = tile([P, J - CHUNK], U32, "rest_w", on="wu_raw_w1")
-        nc.vector.tensor_copy(rest_w[:], tab_w[:].bitcast(U32).indirect(offsets[:, cols:]))
+        nc.vector.tensor_copy(rest_w[:], tab_w[:].bitcast(U32).indirect(offsets[:, COLS:]))
         picked_w = [first_w[:]] + [rest_w[:, c * CHUNK : (c + 1) * CHUNK] for c in range(N_CHUNKS - 1)]
         picked_s = [all_s[:, c * CHUNK : (c + 1) * CHUNK] for c in range(N_CHUNKS)]
 
@@ -155,17 +163,18 @@ def tile_list_modp_relu2_mix_gate_kernel(
         wd_s = wd_s32[:].bitcast(U8)
 
         h = [
-            tile([P, R_PASSES, CHUNK * PACK], BF16, f"h{c}", on="sm_abs0" if c == 0 else None) for c in range(N_CHUNKS)
+            tile([P, R_PASSES, CHUNK * PACK], BF16, f"h{c}", on="wgo_low" if c == 0 else None) for c in range(N_CHUNKS)
         ]
         h_w = [tile([P, R_PASSES * CHUNK], U32, f"h_w{c}") for c in range(N_CHUNKS)]
         h_s = [tile([P, R_PASSES * CHUNK], U8, f"h_s{c}") for c in range(N_CHUNKS)]
         picked_g = {}
+        begun = {}
 
-        def clear_page(engine, on):
+        def clear_page(on):
             pages.append(tile([P, T], F32, f"page{len(pages)}", on=on))
-            engine.memset(pages[-1][:].bitcast(I32), 0)
+            nc.gpsimd.memset(pages[-1][:].bitcast(I32), 0)
 
-        def up_pair(c, g, first, count=PAIR):
+        def up_slices(c, g, first, count):
             a = psum.tile([P, count, CHUNK], F32, name="a", tag=f"bank{UP_BANKS[c, g] + first // count}")
             for k in range(count):
                 t = first + k
@@ -187,52 +196,61 @@ def tile_list_modp_relu2_mix_gate_kernel(
                 func,
             )
 
-        def hidden_signed_on_vector(c, g, on=None, count=PAIR):
-            relu = tile([P, PACK, CHUNK], F32, f"relu{c}_{g}", on=on)
+        def rectified_root(c, g, count=PAIR):
+            relu = tile([P, PACK, CHUNK], F32, f"relu{c}_{g}")
             for first in range(0, PACK, count):
-                a = up_pair(c, g, first, count)
+                a = up_slices(c, g, first, count)
                 for k in range(count):
                     col = g * PACK + first + k
                     nc.scalar.activation(relu[:, first + k, :], a[:, k, :], ACT.Relu, scale=root[:, col : col + 1])
-            h_abs = tile([P, CHUNK * PACK], BF16, f"h_abs{c}_{g}")
-            interleave(h_abs[:], relu[:], ACT.Square)
+            return relu
+
+        def square_and_sign(c, g, relu, tokens=CHUNK):
+            h_abs = tile([P, tokens * PACK], BF16, f"h_abs{c}_{g}")
+            interleave(h_abs[:], relu[:, :, 0:tokens], ACT.Square)
             run = SIGN_RUN * PACK
             nc.vector.tensor_tensor(
-                h[c][:, g, :].rearrange("p (a b) -> p a b", b=run),
+                h[c][:, g, 0 : tokens * PACK].rearrange("p (a b) -> p a b", b=run),
                 h_abs[:].rearrange("p (a b) -> p a b", b=run),
-                signs[:, g].rearrange("p j t -> p (j t)").unsqueeze(1).to_broadcast([P, CHUNK // SIGN_RUN, run]),
+                signs[:, g].rearrange("p j t -> p (j t)").unsqueeze(1).to_broadcast([P, tokens // SIGN_RUN, run]),
                 ALU.mult,
             )
 
         def rectified(c, g, on=None):
             relu = tile([P, PACK, CHUNK], F32, f"relu{c}_{g}", on=on)
             for first in range(0, PACK, PAIR):
-                nc.scalar.activation(relu[:, first : first + PAIR, :], up_pair(c, g, first)[:], ACT.Relu)
+                nc.scalar.activation(relu[:, first : first + PAIR, :], up_slices(c, g, first, PAIR)[:], ACT.Relu)
             return relu
 
-        def squared(c, g, relu):
-            square = tile([P, PACK, CHUNK], F32, f"square{c}_{g}")
-            nc.scalar.activation(square[:], relu[:], ACT.Square)
+        def squared(c, g, relu, skip=0):
+            square = tile([P, PACK, CHUNK - skip], F32, f"square{c}_{g}")
+            nc.scalar.activation(square[:], relu[:, :, skip:], ACT.Square)
             return square
 
-        def scale_and_round(c, g, square, on=None):
-            scaled = tile([P, PACK, CHUNK], F32, f"scaled{c}_{g}", on=on)
+        def scale_and_round(c, g, square, factor, skip=0, on=None):
+            scaled = tile([P, PACK, CHUNK - skip], F32, f"scaled{c}_{g}", on=on)
             for t in range(PACK):
-                nc.scalar.activation(scaled[:, t, :], square[:, t, :], ACT.Copy, scale=factors[:, g, t : t + 1])
-            interleave(h[c][:, g, :], scaled[:], ACT.Copy)
+                nc.scalar.activation(scaled[:, t, :], square[:, t, :], ACT.Copy, scale=factor[:, t : t + 1])
+            interleave(h[c][:, g, skip * PACK :], scaled[:], ACT.Copy)
 
-        def quantise(c):
-            nc.vector.quantize_mx(out=h_w[c][:].bitcast(FP8X4), scales=h_s[c][:], in_=h[c][:].rearrange("p g x -> p (g x)"))
+        def quantise(c, first=0, count=R_PASSES):
+            columns = slice(first * CHUNK, (first + count) * CHUNK)
+            nc.vector.quantize_mx(
+                out=h_w[c][:, columns].bitcast(FP8X4),
+                scales=h_s[c][:, columns],
+                in_=h[c][:, first : first + count, :].rearrange("p g x -> p (g x)"),
+            )
 
-        def quantise_part(c, g):
-            part = slice(g * CHUNK, (g + 1) * CHUNK)
-            nc.vector.quantize_mx(out=h_w[c][:, part].bitcast(FP8X4), scales=h_s[c][:, part], in_=h[c][:, g, :])
+        def gather_gates(i, on=None):
+            picked_g[i] = tile([P, J], F32, f"picked_g{i}", on=on)[:]
+            nc.vector.tensor_tensor(picked_g[i], gates[i][:].indirect(offsets[:]), wgo_sb[:], ALU.mult)
 
-        def gather_gates(first, count, on=None):
-            dense = tile([P, count * J], F32, f"picked_g{first}", on=on)
-            for k in range(count):
-                picked_g[first + k] = dense[:, k * J : (k + 1) * J]
-                nc.vector.tensor_tensor(picked_g[first + k], gates[first + k][:].indirect(offsets[:]), wgo_sb[:], ALU.mult)
+        def gather_gates_in_halves(i):
+            picked_g[i] = tile([P, J], F32, f"picked_g{i}")[:]
+            half = J // 2
+            low, high = offsets[:, 0 : half // GROUP], offsets[:, half // GROUP :]
+            nc.vector.tensor_tensor(picked_g[i][:, 0:half], gates[i][:].indirect(low), wgo_low[:], ALU.mult)
+            nc.vector.tensor_tensor(picked_g[i][:, half:], gates[i][:].indirect(high), wgo_sb[:, half:], ALU.mult)
 
         def down(y_ps, c, i):
             nc.tensor.matmul_mx(
@@ -255,8 +273,6 @@ def tile_list_modp_relu2_mix_gate_kernel(
                     stop=(lo + P == CHUNK),
                 )
 
-        begun = {}
-
         def begin_down(first, i):
             begun[first, i] = psum.tile([P, BANK], F32, name="y_ps", tag=f"bank{DOWN_BANKS[first, i]}")
             down(begun[first, i][:, 0:CHUNK], first, i)
@@ -270,53 +286,53 @@ def tile_list_modp_relu2_mix_gate_kernel(
                 y_ps = begun[first, i] if (first, i) in begun else begin_down(first, i)
                 for c in range(1, count):
                     down(y_ps[:, c * CHUNK : (c + 1) * CHUNK], first + c, i)
-                part = y[:, at : at + width]
+                y_sb = y[:, at : at + width]
                 at = at + width
-                nc.scalar.copy(part, y_ps[:, 0:width])
+                nc.scalar.copy(y_sb, y_ps[:, 0:width])
                 nc.vector.tensor_tensor(
-                    pages[i][:].indirect(offsets[:, first * cols : (first + count) * cols]),
-                    part,
+                    pages[i][:].indirect(offsets[:, first * COLS : (first + count) * COLS]),
+                    y_sb,
                     picked_g[i][:, first * CHUNK : first * CHUNK + width],
                     ALU.mult,
                 )
                 if first + count == N_CHUNKS:
                     nc.sync.dma_start(out[i * P : (i + 1) * P, :], pages[i][:])
 
-        clocks = []
-
-        def clock(ap, dtype):
-            clocks.append(tile([P, 1], dtype, f"clock{len(clocks)}"))
-            nc.gpsimd.tensor_copy(clocks[-1][:], ap)
-
-        gather_gates(0, 2)
-        hidden_signed_on_vector(0, 0, count=1)
+        gather_gates(0)
+        gather_gates_in_halves(1)
+        square_and_sign(0, 0, rectified_root(0, 0, count=1))
         gates.append(tile([P, T], F32, "gates3", on="relu0_0"))
         nc.sync.dma_start(gates[3][:], gT[3 * P : 4 * P, :])
-        hidden_signed_on_vector(0, 1)
-        quantise_part(0, 0)
-        quantise_part(0, 1)
-        gather_gates(2, 1, on="h_abs0_1")
-        clear_page(nc.gpsimd, on=None if PROBE else "sm_abs0")
+        square_and_sign(0, 1, rectified_root(0, 1))
+        quantise(0, 0, 1)
+        quantise(0, 1, 1)
+        gather_gates(2, on="h_abs0_1")
+        clear_page(on="wgo_low")
         scatter([(0, 1, 0), (0, 1, 1)])
         begin_down(0, 2)
         begin_down(0, 3)
-        clear_page(nc.gpsimd, on="h_s0")
-        hidden_signed_on_vector(1, 0)
-        scale_and_round(1, 1, squared(1, 1, rectified(1, 1)), on="h_w0")
+        clear_page(on="h_s0")
+
+        square_and_sign(1, 0, rectified_root(1, 0))
+        scale_and_round(1, 1, squared(1, 1, rectified(1, 1)), sm_pass1, on="h_w0")
         quantise(1)
-        clear_page(nc.gpsimd, on="h1")
-        gather_gates(3, 1, on="h_w0")
-        hidden_signed_on_vector(2, 0)
+        clear_page(on="h1")
+        gather_gates(3, on="h_w0")
+
+        square_and_sign(2, 0, rectified_root(2, 0))
         relu = rectified(2, 1, on="square1_1")
         scatter([(0, 2, 2), (1, 1, 0)], on="relu2_0")
-        scale_and_round(2, 1, squared(2, 1, relu))
+        scale_and_round(2, 1, squared(2, 1, relu), sm_pass1)
         quantise(2)
         scatter([(0, 2, 3), (1, 1, 1)], on="scaled2_1")
-        hidden_signed_on_vector(3, 0)
-        relu = rectified(3, 1)
-        square = squared(3, 1, relu)
+
+        relu = rectified_root(3, 0)
+        square = squared(3, 0, relu, skip=SHARED)
+        square_and_sign(3, 0, relu, tokens=SHARED)
+        scale_and_round(3, 0, square, sign_pass0, skip=SHARED)
+        square = squared(3, 1, rectified(3, 1))
         scatter([(2, 1, 0), (2, 1, 1)], on="relu3_1")
-        scale_and_round(3, 1, square)
+        scale_and_round(3, 1, square, sm_pass1)
         quantise(3)
         scatter([(2, 1, 2)], on="scaled3_1")
         scatter([(3, 1, 0), (3, 1, 1), (3, 1, 2), (2, 2, 3)])

@@ -32,17 +32,17 @@ N_CHUNKS = J // CHUNK
 R_PASSES = R // PASS
 LINE = 4
 SIGN_RUN = 16
-SHARED = CHUNK // 2
+SHARED = 3 * CHUNK // 4
 WD8_WORDS = N
 WD4_WORDS = N // 2
 WD_PLANE_WORDS = N // 4
 WGO_RUN = J // P
 WGO_BANK = 6
 
-UP_BANKS = {(0, 0): 0, (0, 1): 4, (1, 0): 0, (1, 1): 2, (2, 0): 4, (2, 1): 0, (3, 0): 4, (3, 1): 0}
+UP_BANKS = {(0, 0): 0, (0, 1): 4, (1, 0): 0, (1, 1): 2, (2, 0): 4, (2, 1): 0, (3, 0): 2, (3, 1): 0}
 DOWN_BANKS = {
     (0, 0): 4, (0, 1): 5, (0, 2): 6, (0, 3): 7,
-    (1, 0): 2, (1, 1): 3,
+    (1, 0): 2, (1, 1): 6, (1, 2): 3,
     (2, 0): 6, (2, 1): 7, (2, 2): 2, (2, 3): 0,
     (3, 0): 3, (3, 1): 4, (3, 2): 5,
 }
@@ -54,7 +54,11 @@ def tile_list_modp_relu2_mix_gate_kernel(
     nc = tc.nc
     with ExitStack() as ctx:
         keep = ctx.enter_context(tc.tile_pool(name="keep", bufs=1))
+        laid = ctx.enter_context(tc.tile_pool(name="laid", bufs=1))
         psum = ctx.enter_context(tc.psum_pool(name="psum", bufs=1))
+
+        def laid_tile(shape, dtype, name, offset):
+            return laid.tile(shape, dtype, name=name, align_bytes=64, offset=offset)
 
         def tile(shape, dtype, name, on=None):
             return keep.tile(shape, dtype, name=name, tag=on or name, align_bytes=64)
@@ -123,7 +127,7 @@ def tile_list_modp_relu2_mix_gate_kernel(
                 spread[:, :, 0 : P // 2].rearrange("p k m -> p m k"),
             )
 
-        pages = [tile([P, T], F32, "page0")]
+        pages = {0: tile([P, T], F32, "page0")}
         nc.vector.memset(pages[0][:].bitcast(I32), 0)
         wd_s32 = tile([P, WD_PLANE_WORDS], I32, "wd_s32")
         nc.vector.memset(wd_s32[:], 0)
@@ -162,17 +166,16 @@ def tile_list_modp_relu2_mix_gate_kernel(
         wd4_w = wd4_w32.bitcast(U8)
         wd_s = wd_s32[:].bitcast(U8)
 
-        h = [
-            tile([P, R_PASSES, CHUNK * PACK], BF16, f"h{c}", on="wgo_low" if c == 0 else None) for c in range(N_CHUNKS)
-        ]
-        h_w = [tile([P, R_PASSES * CHUNK], U32, f"h_w{c}") for c in range(N_CHUNKS)]
+        h = {c: tile([P, R_PASSES, CHUNK * PACK], BF16, f"h{c}", on="wgo_low" if c == 0 else None) for c in range(2)}
+        h_w = [laid_tile([P, R_PASSES * CHUNK], U32, "h_w0", 0)]
+        h_w.extend(tile([P, R_PASSES * CHUNK], U32, f"h_w{c}") for c in range(1, N_CHUNKS))
         h_s = [tile([P, R_PASSES * CHUNK], U8, f"h_s{c}") for c in range(N_CHUNKS)]
         picked_g = {}
         begun = {}
 
-        def clear_page(on):
-            pages.append(tile([P, T], F32, f"page{len(pages)}", on=on))
-            nc.gpsimd.memset(pages[-1][:].bitcast(I32), 0)
+        def clear_page(i, on):
+            pages[i] = tile([P, T], F32, f"page{i}", on=on)
+            nc.gpsimd.memset(pages[i][:].bitcast(I32), 0)
 
         def up_slices(c, g, first, count):
             a = psum.tile([P, count, CHUNK], F32, name="a", tag=f"bank{UP_BANKS[c, g] + first // count}")
@@ -205,14 +208,18 @@ def tile_list_modp_relu2_mix_gate_kernel(
                     nc.scalar.activation(relu[:, first + k, :], a[:, k, :], ACT.Relu, scale=root[:, col : col + 1])
             return relu
 
-        def square_and_sign(c, g, relu, tokens=CHUNK):
+        def square_and_round(c, g, relu, tokens=CHUNK):
             h_abs = tile([P, tokens * PACK], BF16, f"h_abs{c}_{g}")
             interleave(h_abs[:], relu[:, :, 0:tokens], ACT.Square)
+            return h_abs
+
+        def sign(c, g, h_abs, engine):
+            width = h_abs.shape[1]
             run = SIGN_RUN * PACK
-            nc.vector.tensor_tensor(
-                h[c][:, g, 0 : tokens * PACK].rearrange("p (a b) -> p a b", b=run),
+            engine.tensor_tensor(
+                h[c][:, g, 0:width].rearrange("p (a b) -> p a b", b=run),
                 h_abs[:].rearrange("p (a b) -> p a b", b=run),
-                signs[:, g].rearrange("p j t -> p (j t)").unsqueeze(1).to_broadcast([P, tokens // SIGN_RUN, run]),
+                signs[:, g].rearrange("p j t -> p (j t)").unsqueeze(1).to_broadcast([P, width // run, run]),
                 ALU.mult,
             )
 
@@ -227,8 +234,9 @@ def tile_list_modp_relu2_mix_gate_kernel(
             nc.scalar.activation(square[:], relu[:, :, skip:], ACT.Square)
             return square
 
-        def scale_and_round(c, g, square, factor, skip=0, on=None):
-            scaled = tile([P, PACK, CHUNK - skip], F32, f"scaled{c}_{g}", on=on)
+        def scale_and_round(c, g, square, factor, skip=0, scaled=None):
+            if scaled is None:
+                scaled = tile([P, PACK, CHUNK - skip], F32, f"scaled{c}_{g}")
             for t in range(PACK):
                 nc.scalar.activation(scaled[:, t, :], square[:, t, :], ACT.Copy, scale=factor[:, t : t + 1])
             interleave(h[c][:, g, skip * PACK :], scaled[:], ACT.Copy)
@@ -241,8 +249,8 @@ def tile_list_modp_relu2_mix_gate_kernel(
                 in_=h[c][:, first : first + count, :].rearrange("p g x -> p (g x)"),
             )
 
-        def gather_gates(i, on=None):
-            picked_g[i] = tile([P, J], F32, f"picked_g{i}", on=on)[:]
+        def gather_gates(i, picked):
+            picked_g[i] = picked[:]
             nc.vector.tensor_tensor(picked_g[i], gates[i][:].indirect(offsets[:]), wgo_sb[:], ALU.mult)
 
         def gather_gates_in_halves(i):
@@ -298,38 +306,58 @@ def tile_list_modp_relu2_mix_gate_kernel(
                 if first + count == N_CHUNKS:
                     nc.sync.dma_start(out[i * P : (i + 1) * P, :], pages[i][:])
 
-        gather_gates(0)
+        def gate_and_place(first, count, i, y, engine, z):
+            engine.tensor_tensor(z[:], y, picked_g[i][:, first * CHUNK : (first + count) * CHUNK], ALU.mult)
+            return lambda: nc.vector.tensor_copy(
+                pages[i][:].indirect(offsets[:, first * COLS : (first + count) * COLS]), z[:]
+            )
+
+        gather_gates(0, tile([P, J], F32, "picked_g0"))
         gather_gates_in_halves(1)
-        square_and_sign(0, 0, rectified_root(0, 0, count=1))
+        sign(0, 0, square_and_round(0, 0, rectified_root(0, 0, count=1)), nc.vector)
         gates.append(tile([P, T], F32, "gates3", on="relu0_0"))
         nc.sync.dma_start(gates[3][:], gT[3 * P : 4 * P, :])
-        square_and_sign(0, 1, rectified_root(0, 1))
+        sign(0, 1, square_and_round(0, 1, rectified_root(0, 1)), nc.vector)
         quantise(0, 0, 1)
         quantise(0, 1, 1)
-        gather_gates(2, on="h_abs0_1")
-        clear_page(on="wgo_low")
+        gather_gates(2, tile([P, J], F32, "picked_g2", on="h_abs0_1"))
+        clear_page(1, on="wgo_low")
         scatter([(0, 1, 0), (0, 1, 1)])
         begin_down(0, 2)
         begin_down(0, 3)
-        clear_page(on="h_s0")
+        clear_page(2, on="h_s0")
 
-        square_and_sign(1, 0, rectified_root(1, 0))
-        scale_and_round(1, 1, squared(1, 1, rectified(1, 1)), sm_pass1, on="h_w0")
+        sign(1, 0, square_and_round(1, 0, rectified_root(1, 0)), nc.vector)
+        scaled = laid_tile([P, PACK, CHUNK], F32, "scaled1_1", 0)
+        scale_and_round(1, 1, squared(1, 1, rectified(1, 1)), sm_pass1, scaled=scaled)
         quantise(1)
-        clear_page(on="h1")
-        gather_gates(3, on="h_w0")
+        clear_page(3, on="h1")
+        z = laid_tile([P, CHUNK], F32, "z0_2", 0)
+        place = gate_and_place(0, 1, 2, begun[0, 2][:, 0:CHUNK], nc.vector, z)
+        gather_gates(3, laid_tile([P, J], F32, "picked_g3", 1024))
+        place()
 
-        square_and_sign(2, 0, rectified_root(2, 0))
+        h_abs = square_and_round(2, 0, rectified_root(2, 0))
         relu = rectified(2, 1, on="square1_1")
-        scatter([(0, 2, 2), (1, 1, 0)], on="relu2_0")
-        scale_and_round(2, 1, squared(2, 1, relu), sm_pass1)
-        quantise(2)
-        scatter([(0, 2, 3), (1, 1, 1)], on="scaled2_1")
-
+        y = tile([P, 2, CHUNK], F32, "y1", on="relu2_0")
+        for k, i in enumerate((0, 2)):
+            nc.scalar.copy(y[:, k, :], begin_down(1, i)[:, 0:CHUNK])
+            gate_and_place(1, 1, i, y[:, k, :], nc.gpsimd, tile([P, CHUNK], F32, f"z1_{i}"))()
+        square = squared(2, 1, relu)
+        y = tile([P, 2 * CHUNK], F32, "y0_3", on="square1_1")
+        down(begun[0, 3][:, CHUNK:], 1, 3)
+        nc.scalar.copy(y[:], begun[0, 3][:])
+        gate_and_place(0, 2, 3, y[:], nc.gpsimd, tile([P, 2 * CHUNK], F32, "z0_3"))()
+        h[2] = tile([P, R_PASSES, CHUNK * PACK], BF16, "h2", on="square1_1")
+        sign(2, 0, h_abs, nc.gpsimd)
+        h[3] = tile([P, R_PASSES, CHUNK * PACK], BF16, "h3", on="h_abs2_0")
         relu = rectified_root(3, 0)
-        square = squared(3, 0, relu, skip=SHARED)
-        square_and_sign(3, 0, relu, tokens=SHARED)
-        scale_and_round(3, 0, square, sign_pass0, skip=SHARED)
+        sign(3, 0, square_and_round(3, 0, relu, tokens=SHARED), nc.gpsimd)
+        scale_and_round(2, 1, square, sm_pass1)
+        quantise(2)
+        scatter([(1, 1, 1)], on="scaled2_1")
+
+        scale_and_round(3, 0, squared(3, 0, relu, skip=SHARED), sign_pass0, skip=SHARED)
         square = squared(3, 1, rectified(3, 1))
         scatter([(2, 1, 0), (2, 1, 1)], on="relu3_1")
         scale_and_round(3, 1, square, sm_pass1)

@@ -108,8 +108,6 @@ def tile_list_modp_relu2_mix_gate_kernel(
         signs = tile([P, R_PASSES, SIGN_RUN, PACK], BF16, "signs")
         for g in range(R_PASSES):
             nc.scalar.activation(signs[:, g], sm_sb[:, g, :].unsqueeze(1).to_broadcast([P, SIGN_RUN, PACK]), ACT.Sign)
-        sign_pass0 = tile([P, PACK], F32, "sign_pass0")
-        nc.scalar.activation(sign_pass0[:], sm_sb[:, 0, :], ACT.Sign)
 
         wgo_sb = tile([P, J], F32, "wgo_sb")
         wgo_low = tile([P, J // 2], F32, "wgo_low")
@@ -339,25 +337,23 @@ def tile_list_modp_relu2_mix_gate_kernel(
 
         h_abs = square_and_round(2, 0, rectified_root(2, 0))
         relu = rectified(2, 1, on="square1_1")
-        y = tile([P, 2, CHUNK], F32, "y1", on="relu2_0")
+        y = tile([P, 4 * CHUNK], F32, "y1", on="relu2_0")
         for k, i in enumerate((0, 2)):
-            nc.scalar.copy(y[:, k, :], begin_down(1, i)[:, 0:CHUNK])
-            gate_and_place(1, 1, i, y[:, k, :], nc.gpsimd, tile([P, CHUNK], F32, f"z1_{i}"))()
-        square = squared(2, 1, relu)
-        y = tile([P, 2 * CHUNK], F32, "y0_3", on="square1_1")
+            y_sb = y[:, k * CHUNK : (k + 1) * CHUNK]
+            nc.scalar.copy(y_sb, begin_down(1, i)[:, 0:CHUNK])
+            gate_and_place(1, 1, i, y_sb, nc.gpsimd, tile([P, CHUNK], F32, f"z1_{i}"))()
         down(begun[0, 3][:, CHUNK:], 1, 3)
-        nc.scalar.copy(y[:], begun[0, 3][:])
-        gate_and_place(0, 2, 3, y[:], nc.gpsimd, tile([P, 2 * CHUNK], F32, "z0_3"))()
-        h[2] = tile([P, R_PASSES, CHUNK * PACK], BF16, "h2", on="square1_1")
+        nc.scalar.copy(y[:, 2 * CHUNK :], begun[0, 3][:])
+        gate_and_place(0, 2, 3, y[:, 2 * CHUNK :], nc.gpsimd, tile([P, 2 * CHUNK], F32, "z0_3"))()
+        square = squared(2, 1, relu)
+        h[2] = tile([P, R_PASSES, CHUNK * PACK], BF16, "h2", on="relu2_0")
         sign(2, 0, h_abs, nc.gpsimd)
         h[3] = tile([P, R_PASSES, CHUNK * PACK], BF16, "h3", on="h_abs2_0")
-        relu = rectified_root(3, 0)
-        sign(3, 0, square_and_round(3, 0, relu, tokens=SHARED), nc.gpsimd)
+        sign(3, 0, square_and_round(3, 0, rectified_root(3, 0)), nc.gpsimd)
         scale_and_round(2, 1, square, sm_pass1)
         quantise(2)
         scatter([(1, 1, 1)], on="scaled2_1")
 
-        scale_and_round(3, 0, squared(3, 0, relu, skip=SHARED), sign_pass0, skip=SHARED)
         square = squared(3, 1, rectified(3, 1))
         scatter([(2, 1, 0), (2, 1, 1)], on="relu3_1")
         scale_and_round(3, 1, square, sm_pass1)

@@ -32,11 +32,11 @@ N_CHUNKS = J // CHUNK
 R_PASSES = R // PASS
 LINE = 4
 SIGN_RUN = 16
-SHARED = 3 * CHUNK // 4
 WD8_WORDS = N
 WD4_WORDS = N // 2
 WD_PLANE_WORDS = N // 4
 WGO_RUN = J // P
+CHUNK_BYTES = 4 * CHUNK
 WGO_BANK = 6
 
 UP_BANKS = {(0, 0): 0, (0, 1): 4, (1, 0): 0, (1, 1): 2, (2, 0): 4, (2, 1): 0, (3, 0): 2, (3, 1): 0}
@@ -206,18 +206,18 @@ def tile_list_modp_relu2_mix_gate_kernel(
                     nc.scalar.activation(relu[:, first + k, :], a[:, k, :], ACT.Relu, scale=root[:, col : col + 1])
             return relu
 
-        def square_and_round(c, g, relu, tokens=CHUNK):
-            h_abs = tile([P, tokens * PACK], BF16, f"h_abs{c}_{g}")
-            interleave(h_abs[:], relu[:, :, 0:tokens], ACT.Square)
+        def square_and_round(c, g, relu):
+            h_abs = tile([P, CHUNK * PACK], BF16, f"h_abs{c}_{g}")
+            interleave(h_abs[:], relu[:], ACT.Square)
             return h_abs
 
-        def sign(c, g, h_abs, engine):
-            width = h_abs.shape[1]
+        def sign(c, g, h_abs, engine, first=0, tokens=CHUNK):
             run = SIGN_RUN * PACK
+            columns = slice(first * PACK, (first + tokens) * PACK)
             engine.tensor_tensor(
-                h[c][:, g, 0:width].rearrange("p (a b) -> p a b", b=run),
-                h_abs[:].rearrange("p (a b) -> p a b", b=run),
-                signs[:, g].rearrange("p j t -> p (j t)").unsqueeze(1).to_broadcast([P, width // run, run]),
+                h[c][:, g, columns].rearrange("p (a b) -> p a b", b=run),
+                h_abs[:, columns].rearrange("p (a b) -> p a b", b=run),
+                signs[:, g].rearrange("p j t -> p (j t)").unsqueeze(1).to_broadcast([P, tokens // SIGN_RUN, run]),
                 ALU.mult,
             )
 
@@ -227,17 +227,15 @@ def tile_list_modp_relu2_mix_gate_kernel(
                 nc.scalar.activation(relu[:, first : first + PAIR, :], up_slices(c, g, first, PAIR)[:], ACT.Relu)
             return relu
 
-        def squared(c, g, relu, skip=0):
-            square = tile([P, PACK, CHUNK - skip], F32, f"square{c}_{g}")
-            nc.scalar.activation(square[:], relu[:, :, skip:], ACT.Square)
+        def squared(c, g, relu):
+            square = tile([P, PACK, CHUNK], F32, f"square{c}_{g}")
+            nc.scalar.activation(square[:], relu[:], ACT.Square)
             return square
 
-        def scale_and_round(c, g, square, factor, skip=0, scaled=None):
-            if scaled is None:
-                scaled = tile([P, PACK, CHUNK - skip], F32, f"scaled{c}_{g}")
+        def scale_and_round(c, square, scaled):
             for t in range(PACK):
-                nc.scalar.activation(scaled[:, t, :], square[:, t, :], ACT.Copy, scale=factor[:, t : t + 1])
-            interleave(h[c][:, g, skip * PACK :], scaled[:], ACT.Copy)
+                nc.scalar.activation(scaled[:, t, :], square[:, t, :], ACT.Copy, scale=sm_pass1[:, t : t + 1])
+            interleave(h[c][:, 1, :], scaled[:], ACT.Copy)
 
         def quantise(c, first=0, count=R_PASSES):
             columns = slice(first * CHUNK, (first + count) * CHUNK)
@@ -268,16 +266,15 @@ def tile_list_modp_relu2_mix_gate_kernel(
                 start=True,
                 stop=False,
             )
-            for lo in range(0, CHUNK, P):
-                nc.tensor.matmul_mx(
-                    out=y_ps[:, lo : lo + P],
-                    lhsT=wd4_w[:, 2 * i * P : 2 * (i + 1) * P].bitcast(FP4X4),
-                    lhsT_scale=wd_s[:, i * P : (i + 1) * P],
-                    rhs=h_w[c][:, CHUNK + lo : CHUNK + lo + P].bitcast(FP8X4),
-                    rhs_scale=h_s[c][:, CHUNK + lo : CHUNK + lo + P],
-                    start=False,
-                    stop=(lo + P == CHUNK),
-                )
+            nc.tensor.matmul_mx(
+                out=y_ps,
+                lhsT=wd4_w[:, 2 * i * P : 2 * (i + 1) * P].bitcast(FP4X4),
+                lhsT_scale=wd_s[:, i * P : (i + 1) * P],
+                rhs=h_w[c][:, CHUNK:].bitcast(FP8X4),
+                rhs_scale=h_s[c][:, CHUNK:],
+                start=False,
+                stop=True,
+            )
 
         def begin_down(first, i):
             begun[first, i] = psum.tile([P, BANK], F32, name="y_ps", tag=f"bank{DOWN_BANKS[first, i]}")
@@ -304,11 +301,12 @@ def tile_list_modp_relu2_mix_gate_kernel(
                 if first + count == N_CHUNKS:
                     nc.sync.dma_start(out[i * P : (i + 1) * P, :], pages[i][:])
 
-        def gate_and_place(first, count, i, y, engine, z):
+        def gate(first, count, i, y, engine, z):
             engine.tensor_tensor(z[:], y, picked_g[i][:, first * CHUNK : (first + count) * CHUNK], ALU.mult)
-            return lambda: nc.vector.tensor_copy(
-                pages[i][:].indirect(offsets[:, first * COLS : (first + count) * COLS]), z[:]
-            )
+            return z
+
+        def place(first, count, i, z):
+            nc.vector.tensor_copy(pages[i][:].indirect(offsets[:, first * COLS : (first + count) * COLS]), z[:])
 
         gather_gates(0, tile([P, J], F32, "picked_g0"))
         gather_gates_in_halves(1)
@@ -326,37 +324,36 @@ def tile_list_modp_relu2_mix_gate_kernel(
         clear_page(2, on="h_s0")
 
         sign(1, 0, square_and_round(1, 0, rectified_root(1, 0)), nc.vector)
-        scaled = laid_tile([P, PACK, CHUNK], F32, "scaled1_1", 0)
-        scale_and_round(1, 1, squared(1, 1, rectified(1, 1)), sm_pass1, scaled=scaled)
+        scale_and_round(1, squared(1, 1, rectified(1, 1)), laid_tile([P, PACK, CHUNK], F32, "scaled1", 0))
         quantise(1)
         clear_page(3, on="h1")
-        z = laid_tile([P, CHUNK], F32, "z0_2", 0)
-        place = gate_and_place(0, 1, 2, begun[0, 2][:, 0:CHUNK], nc.vector, z)
-        gather_gates(3, laid_tile([P, J], F32, "picked_g3", 1024))
-        place()
+        z = gate(0, 1, 2, begun[0, 2][:, 0:CHUNK], nc.vector, laid_tile([P, CHUNK], F32, "z0_2", 0))
+        gather_gates(3, laid_tile([P, J], F32, "picked_g3", CHUNK_BYTES))
+        place(0, 1, 2, z)
 
         h_abs = square_and_round(2, 0, rectified_root(2, 0))
         relu = rectified(2, 1, on="square1_1")
-        y = tile([P, 4 * CHUNK], F32, "y1", on="relu2_0")
+        y = tile([P, 2, CHUNK], F32, "y1", on="relu2_0")
         for k, i in enumerate((0, 2)):
-            y_sb = y[:, k * CHUNK : (k + 1) * CHUNK]
-            nc.scalar.copy(y_sb, begin_down(1, i)[:, 0:CHUNK])
-            gate_and_place(1, 1, i, y_sb, nc.gpsimd, tile([P, CHUNK], F32, f"z1_{i}"))()
-        down(begun[0, 3][:, CHUNK:], 1, 3)
-        nc.scalar.copy(y[:, 2 * CHUNK :], begun[0, 3][:])
-        gate_and_place(0, 2, 3, y[:, 2 * CHUNK :], nc.gpsimd, tile([P, 2 * CHUNK], F32, "z0_3"))()
-        square = squared(2, 1, relu)
+            nc.scalar.copy(y[:, k, :], begin_down(1, i)[:, 0:CHUNK])
+            place(1, 1, i, gate(1, 1, i, y[:, k, :], nc.gpsimd, tile([P, CHUNK], F32, f"z1_{i}")))
         h[2] = tile([P, R_PASSES, CHUNK * PACK], BF16, "h2", on="relu2_0")
-        sign(2, 0, h_abs, nc.gpsimd)
+        sign(2, 0, h_abs, nc.gpsimd, 0, CHUNK // 2)
+        square = squared(2, 1, relu)
+        y = tile([P, 2 * CHUNK], F32, "y0_3", on="square1_1")
+        down(begun[0, 3][:, CHUNK:], 1, 3)
+        nc.scalar.copy(y[:], begun[0, 3][:])
+        place(0, 2, 3, gate(0, 2, 3, y[:], nc.gpsimd, tile([P, 2 * CHUNK], F32, "z0_3")))
+        sign(2, 0, h_abs, nc.gpsimd, CHUNK // 2, CHUNK // 2)
         h[3] = tile([P, R_PASSES, CHUNK * PACK], BF16, "h3", on="h_abs2_0")
         sign(3, 0, square_and_round(3, 0, rectified_root(3, 0)), nc.gpsimd)
-        scale_and_round(2, 1, square, sm_pass1)
+        scale_and_round(2, square, tile([P, PACK, CHUNK], F32, "scaled2"))
         quantise(2)
-        scatter([(1, 1, 1)], on="scaled2_1")
+        scatter([(1, 1, 1)], on="scaled2")
 
         square = squared(3, 1, rectified(3, 1))
         scatter([(2, 1, 0), (2, 1, 1)], on="relu3_1")
-        scale_and_round(3, 1, square, sm_pass1)
+        scale_and_round(3, square, tile([P, PACK, CHUNK], F32, "scaled3"))
         quantise(3)
-        scatter([(2, 1, 2)], on="scaled3_1")
+        scatter([(2, 1, 2)], on="scaled3")
         scatter([(3, 1, 0), (3, 1, 1), (3, 1, 2), (2, 2, 3)])

@@ -211,13 +211,12 @@ def tile_list_modp_relu2_mix_gate_kernel(
             interleave(h_abs[:], relu[:], ACT.Square)
             return h_abs
 
-        def sign(c, g, h_abs, engine, first=0, tokens=CHUNK):
+        def sign(c, g, h_abs, engine):
             run = SIGN_RUN * PACK
-            columns = slice(first * PACK, (first + tokens) * PACK)
             engine.tensor_tensor(
-                h[c][:, g, columns].rearrange("p (a b) -> p a b", b=run),
-                h_abs[:, columns].rearrange("p (a b) -> p a b", b=run),
-                signs[:, g].rearrange("p j t -> p (j t)").unsqueeze(1).to_broadcast([P, tokens // SIGN_RUN, run]),
+                h[c][:, g, :].rearrange("p (a b) -> p a b", b=run),
+                h_abs[:].rearrange("p (a b) -> p a b", b=run),
+                signs[:, g].rearrange("p j t -> p (j t)").unsqueeze(1).to_broadcast([P, CHUNK // SIGN_RUN, run]),
                 ALU.mult,
             )
 
@@ -301,12 +300,12 @@ def tile_list_modp_relu2_mix_gate_kernel(
                 if first + count == N_CHUNKS:
                     nc.sync.dma_start(out[i * P : (i + 1) * P, :], pages[i][:])
 
-        def gate(first, count, i, y, engine, z):
-            engine.tensor_tensor(z[:], y, picked_g[i][:, first * CHUNK : (first + count) * CHUNK], ALU.mult)
+        def gate(c, i, y, engine, z):
+            engine.tensor_tensor(z[:], y, picked_g[i][:, c * CHUNK : (c + 1) * CHUNK], ALU.mult)
             return z
 
-        def place(first, count, i, z):
-            nc.vector.tensor_copy(pages[i][:].indirect(offsets[:, first * COLS : (first + count) * COLS]), z[:])
+        def place(c, i, z):
+            nc.vector.tensor_copy(pages[i][:].indirect(offsets[:, c * COLS : (c + 1) * COLS]), z[:])
 
         gather_gates(0, tile([P, J], F32, "picked_g0"))
         gather_gates_in_halves(1)
@@ -327,24 +326,24 @@ def tile_list_modp_relu2_mix_gate_kernel(
         scale_and_round(1, squared(1, 1, rectified(1, 1)), laid_tile([P, PACK, CHUNK], F32, "scaled1", 0))
         quantise(1)
         clear_page(3, on="h1")
-        z = gate(0, 1, 2, begun[0, 2][:, 0:CHUNK], nc.vector, laid_tile([P, CHUNK], F32, "z0_2", 0))
+        z = gate(0, 2, begun[0, 2][:, 0:CHUNK], nc.vector, laid_tile([P, CHUNK], F32, "z0_2", 0))
         gather_gates(3, laid_tile([P, J], F32, "picked_g3", CHUNK_BYTES))
-        place(0, 1, 2, z)
+        place(0, 2, z)
 
         h_abs = square_and_round(2, 0, rectified_root(2, 0))
         relu = rectified(2, 1, on="square1_1")
-        y = tile([P, 2, CHUNK], F32, "y1", on="relu2_0")
-        for k, i in enumerate((0, 2)):
-            nc.scalar.copy(y[:, k, :], begin_down(1, i)[:, 0:CHUNK])
-            place(1, 1, i, gate(1, 1, i, y[:, k, :], nc.gpsimd, tile([P, CHUNK], F32, f"z1_{i}")))
+        y = tile([P, 3, CHUNK], F32, "y1", on="relu2_0")
+        for k, (c, i) in enumerate(((1, 0), (0, 3), (1, 2))):
+            y_ps = begun[c, i] if (c, i) in begun else begin_down(c, i)
+            nc.scalar.copy(y[:, k, :], y_ps[:, 0:CHUNK])
+            place(c, i, gate(c, i, y[:, k, :], nc.gpsimd, tile([P, CHUNK], F32, f"z{c}_{i}")))
         h[2] = tile([P, R_PASSES, CHUNK * PACK], BF16, "h2", on="relu2_0")
-        sign(2, 0, h_abs, nc.gpsimd, 0, CHUNK // 2)
+        sign(2, 0, h_abs, nc.gpsimd)
         square = squared(2, 1, relu)
-        y = tile([P, 2 * CHUNK], F32, "y0_3", on="square1_1")
+        y = tile([P, CHUNK], F32, "y1_3", on="square1_1")
         down(begun[0, 3][:, CHUNK:], 1, 3)
-        nc.scalar.copy(y[:], begun[0, 3][:])
-        place(0, 2, 3, gate(0, 2, 3, y[:], nc.gpsimd, tile([P, 2 * CHUNK], F32, "z0_3")))
-        sign(2, 0, h_abs, nc.gpsimd, CHUNK // 2, CHUNK // 2)
+        nc.scalar.copy(y[:], begun[0, 3][:, CHUNK:])
+        place(1, 3, gate(1, 3, y[:], nc.gpsimd, tile([P, CHUNK], F32, "z1_3")))
         h[3] = tile([P, R_PASSES, CHUNK * PACK], BF16, "h3", on="h_abs2_0")
         sign(3, 0, square_and_round(3, 0, rectified_root(3, 0)), nc.gpsimd)
         scale_and_round(2, square, tile([P, PACK, CHUNK], F32, "scaled2"))

@@ -25,27 +25,25 @@ QUAD = P // QUADRANTS
 SCALE_ROWS = 4
 GROUP = 16
 CHUNK = 256
+HALF = CHUNK // 2
 COLS = CHUNK // GROUP
 BANK = 512
 PAIR = BANK // CHUNK
 N_CHUNKS = J // CHUNK
+LAST = N_CHUNKS - 1
+N_PAGES = N // P
 R_PASSES = R // PASS
 LINE = 4
-SIGN_RUN = 16
+RUN = 16
 WD8_WORDS = N
 WD4_WORDS = N // 2
 WD_PLANE_WORDS = N // 4
 WGO_RUN = J // P
-CHUNK_BYTES = 4 * CHUNK
+KIB = 1024
 WGO_BANK = 6
-
-UP_BANKS = {(0, 0): 0, (0, 1): 4, (1, 0): 0, (1, 1): 2, (2, 0): 4, (2, 1): 0, (3, 0): 2, (3, 1): 0}
-DOWN_BANKS = {
-    (0, 0): 4, (0, 1): 5, (0, 2): 6, (0, 3): 7,
-    (1, 0): 2, (1, 1): 6, (1, 2): 3,
-    (2, 0): 6, (2, 1): 7, (2, 2): 2, (2, 3): 0,
-    (3, 0): 3, (3, 1): 4, (3, 2): 5,
-}
+FIRST_BANKS = (0, 1, 4, 5)
+REGION = 9 * KIB
+HEAD_REGION = N_CHUNKS * REGION
 
 
 def tile_list_modp_relu2_mix_gate_kernel(
@@ -63,16 +61,25 @@ def tile_list_modp_relu2_mix_gate_kernel(
         def tile(shape, dtype, name, on=None):
             return keep.tile(shape, dtype, name=name, tag=on or name, align_bytes=64)
 
+        def bank(shape, index, name):
+            return psum.tile(shape, F32, name=name, tag=f"bank{index}")
+
         def scale_rows(q, first=0, planes=1):
             return slice(QUAD * q + SCALE_ROWS * first, QUAD * q + SCALE_ROWS * (first + planes))
 
         def blocks(q):
             return slice(SCALE_ROWS * q, SCALE_ROWS * (q + 1))
 
+        def listed(first, count=1):
+            return offsets[:, first * COLS : (first + count) * COLS]
+
+        def tokens(first, count=1):
+            return slice(first * CHUNK, (first + count) * CHUNK)
+
         offsets = keep.tile([P, J // GROUP], U16, name="offsets")
         tab_w = tile([P, T], I32, "tab_w")
         tab_s = tile([P, T], U8, "tab_s")
-        wu_raw_w = [tile([P, PASS], I32, f"wu_raw_w{g}") for g in range(R_PASSES)]
+        wu_raw_w = [tile([P, PASS], I32, "wu_raw_w0"), laid_tile([P, PASS], I32, "wu_raw_w1", HEAD_REGION + 2 * KIB)]
         wu_raw_s = tile([P, PASS], U8, "wu_raw_s")
         wu_w = [tile([P, PASS], I32, f"wu_w{g}") for g in range(R_PASSES)]
         wu_s = tile([P, PASS], U8, "wu_s")
@@ -105,14 +112,17 @@ def tile_list_modp_relu2_mix_gate_kernel(
             nc.scalar.activation(root[:, g * PACK : (g + 1) * PACK], sm_abs[:], ACT.Sqrt)
         sm_pass1 = tile([P, PACK], F32, "sm_pass1")
         nc.scalar.copy(sm_pass1[:], sm_sb[:, 1, :])
-        signs = tile([P, R_PASSES, SIGN_RUN, PACK], BF16, "signs")
+        sm_run = tile([P, RUN, PACK], F32, "sm_run")
+        nc.scalar.copy(sm_run[:], sm_sb[:, 0, :].unsqueeze(1).to_broadcast([P, RUN, PACK]))
+        signs = tile([P, R_PASSES, RUN, PACK], BF16, "signs")
         for g in range(R_PASSES):
-            nc.scalar.activation(signs[:, g], sm_sb[:, g, :].unsqueeze(1).to_broadcast([P, SIGN_RUN, PACK]), ACT.Sign)
+            nc.scalar.activation(signs[:, g], sm_sb[:, g, :].unsqueeze(1).to_broadcast([P, RUN, PACK]), ACT.Sign)
 
         wgo_sb = tile([P, J], F32, "wgo_sb")
         wgo_low = tile([P, J // 2], F32, "wgo_low")
+        wgo_first = laid_tile([P, CHUNK], F32, "wgo_first", KIB // 2)
         for b in range(WGO_RUN // LINE):
-            spread = psum.tile([P, LINE, P], F32, name="spread", tag=f"bank{WGO_BANK + b}")
+            spread = bank([P, LINE, P], WGO_BANK + b, "spread")
             for k in range(LINE):
                 i = b * LINE + k
                 nc.tensor.transpose(spread[:, k, :], wgo_row[:, i : i + 1].to_broadcast([P, P]), identity[:])
@@ -124,6 +134,10 @@ def tile_list_modp_relu2_mix_gate_kernel(
                 wgo_low[:].rearrange("p (m i) -> p m i", i=WGO_RUN)[:, :, b * LINE : (b + 1) * LINE],
                 spread[:, :, 0 : P // 2].rearrange("p k m -> p m k"),
             )
+            nc.scalar.copy(
+                wgo_first[:].rearrange("p (m i) -> p m i", i=WGO_RUN)[:, :, b * LINE : (b + 1) * LINE],
+                spread[:, :, 0 : CHUNK // WGO_RUN].rearrange("p k m -> p m k"),
+            )
 
         pages = {0: tile([P, T], F32, "page0")}
         nc.vector.memset(pages[0][:].bitcast(I32), 0)
@@ -133,7 +147,7 @@ def tile_list_modp_relu2_mix_gate_kernel(
         all_s = tile([P, J], U8, "all_s")
         nc.vector.tensor_copy(all_s[:], tab_s[:].indirect(offsets[:]))
         first_w = tile([P, CHUNK], U32, "first_w")
-        nc.vector.tensor_copy(first_w[:], tab_w[:].bitcast(U32).indirect(offsets[:, 0:COLS]))
+        nc.vector.tensor_copy(first_w[:], tab_w[:].bitcast(U32).indirect(listed(0)))
         nc.vector.tensor_copy(
             wu_s[:].rearrange("p (t m) -> p m t", t=PACK),
             wu_raw_s[:].rearrange("p (m t) -> p m t", t=PACK),
@@ -143,51 +157,59 @@ def tile_list_modp_relu2_mix_gate_kernel(
                 wu_w[g][:].rearrange("p (t m) -> p m t", t=PACK),
                 wu_raw_w[g][:].rearrange("p (m t) -> p m t", t=PACK),
             )
-        rest_w = tile([P, J - CHUNK], U32, "rest_w", on="wu_raw_w1")
-        nc.vector.tensor_copy(rest_w[:], tab_w[:].bitcast(U32).indirect(offsets[:, COLS:]))
-        picked_w = [first_w[:]] + [rest_w[:, c * CHUNK : (c + 1) * CHUNK] for c in range(N_CHUNKS - 1)]
-        picked_s = [all_s[:, c * CHUNK : (c + 1) * CHUNK] for c in range(N_CHUNKS)]
+        rest_w = laid_tile([P, J - CHUNK], U32, "rest_w", HEAD_REGION)
+        nc.vector.tensor_copy(rest_w[:], tab_w[:].bitcast(U32).indirect(listed(1, LAST)))
+        picked_w = [first_w[:]] + [rest_w[:, tokens(c)] for c in range(LAST)]
+        picked_s = [all_s[:, tokens(c)] for c in range(N_CHUNKS)]
+
+        def clear(i, page):
+            pages[i] = page
+            nc.gpsimd.memset(page[:].bitcast(I32), 0)
+
+        clear(1, laid_tile([P, T], F32, "page1", HEAD_REGION + 3 * KIB))
+        clear(2, tile([P, T], F32, "page2", on="first_w"))
 
         gates = [tile([P, T], F32, f"gates{i}", on=name) for i, name in enumerate(("sm_abs1", "sm_abs0", "sm_sb"))]
-        wd = tile([P, WD8_WORDS + WD4_WORDS], I32, "wd", on="tab_s")
-        wd8_w = wd[:, 0:WD8_WORDS]
-        wd4_w32 = wd[:, WD8_WORDS:]
         nc.sync.dma_start(gates[0][:], gT[0:P, :])
         nc.sync.dma_start(gates[1][:], gT[P : 2 * P, :])
         for q in range(QUADRANTS):
             nc.sync.dma_start(wd_s32[scale_rows(q, first=1), :], wd8_scales[0].bitcast(I32)[blocks(q), :])
         nc.sync.dma_start(gates[2][:], gT[2 * P : 3 * P, :])
+        wd = tile([P, WD8_WORDS + WD4_WORDS], I32, "wd", on="tab_s")
+        wd8_w = wd[:, 0:WD8_WORDS]
         nc.sync.dma_start(wd8_w, wd8_words[0].rearrange("p n i -> p (n i)").bitcast(I32))
-        nc.sync.dma_start(wd4_w32, wd4_words[0].bitcast(I32))
+        nc.sync.dma_start(wd[:, WD8_WORDS:], wd4_words[0].bitcast(I32))
+        wd4_w = wd[:, WD8_WORDS:].bitcast(U8)
         for q in range(QUADRANTS):
             nc.sync.dma_start(wd_s32[scale_rows(q), :], wd4_scales[0].bitcast(I32)[blocks(q), :])
-        wd4_w = wd4_w32.bitcast(U8)
         wd_s = wd_s32[:].bitcast(U8)
 
-        h = {c: tile([P, R_PASSES, CHUNK * PACK], BF16, f"h{c}", on="wgo_low" if c == 0 else None) for c in range(2)}
-        h_w = [laid_tile([P, R_PASSES * CHUNK], U32, "h_w0", 0)]
-        h_w.extend(tile([P, R_PASSES * CHUNK], U32, f"h_w{c}") for c in range(1, N_CHUNKS))
-        h_s = [tile([P, R_PASSES * CHUNK], U8, f"h_s{c}") for c in range(N_CHUNKS)]
-        picked_g = {}
-        begun = {}
+        h = {0: tile([P, R_PASSES, CHUNK * PACK], BF16, "h0", on="wgo_low")}
+        codes = {c: tile([P, R_PASSES * CHUNK], U32, f"h_w{c}") for c in range(1, N_CHUNKS)}
+        planes = [tile([P, R_PASSES * CHUNK], U8, f"h_s{c}") for c in range(N_CHUNKS)]
+        h_w = {c: [codes[c][:, tokens(g)] for g in range(R_PASSES)] for c in codes}
+        h_w[0] = [tile([P, CHUNK], U32, "h_w0_0")[:], laid_tile([P, CHUNK], U32, "h_w0_1", REGION + 3 * KIB)[:]]
+        h_s = [[plane[:, tokens(g)] for g in range(R_PASSES)] for plane in planes]
+        gw = {}
+        y_ps = {}
+        y = {}
+        z = {}
 
-        def clear_page(i, on):
-            pages[i] = tile([P, T], F32, f"page{i}", on=on)
-            nc.gpsimd.memset(pages[i][:].bitcast(I32), 0)
+        def up(a, c, g, t, columns):
+            nc.tensor.matmul_mx(
+                out=a,
+                lhsT=wu_w[g][:, t * P : (t + 1) * P].bitcast(FP8X4),
+                lhsT_scale=wu_s[SCALE_ROWS * g : P, t * P : (t + 1) * P],
+                rhs=picked_w[c][:, columns].bitcast(FP8X4),
+                rhs_scale=picked_s[c][:, columns],
+                start=True,
+                stop=True,
+            )
 
-        def up_slices(c, g, first, count):
-            a = psum.tile([P, count, CHUNK], F32, name="a", tag=f"bank{UP_BANKS[c, g] + first // count}")
+        def up_slices(c, g, first, count, index):
+            a = bank([P, count, CHUNK], index, "a")
             for k in range(count):
-                t = first + k
-                nc.tensor.matmul_mx(
-                    out=a[:, k, :],
-                    lhsT=wu_w[g][:, t * P : (t + 1) * P].bitcast(FP8X4),
-                    lhsT_scale=wu_s[SCALE_ROWS * g : P, t * P : (t + 1) * P],
-                    rhs=picked_w[c].bitcast(FP8X4),
-                    rhs_scale=picked_s[c],
-                    start=True,
-                    stop=True,
-                )
+                up(a[:, k, :], c, g, first + k, slice(0, CHUNK))
             return a
 
         def interleave(dst, src, func):
@@ -197,162 +219,181 @@ def tile_list_modp_relu2_mix_gate_kernel(
                 func,
             )
 
-        def rectified_root(c, g, count=PAIR):
-            relu = tile([P, PACK, CHUNK], F32, f"relu{c}_{g}")
-            for first in range(0, PACK, count):
-                a = up_slices(c, g, first, count)
+        def rectified_root(g, banks):
+            relu = tile([P, PACK, CHUNK], F32, f"relu0_{g}")
+            count = PACK // len(banks)
+            for b, index in enumerate(banks):
+                a = up_slices(0, g, b * count, count, index)
                 for k in range(count):
-                    col = g * PACK + first + k
-                    nc.scalar.activation(relu[:, first + k, :], a[:, k, :], ACT.Relu, scale=root[:, col : col + 1])
+                    col = g * PACK + b * count + k
+                    nc.scalar.activation(relu[:, b * count + k, :], a[:, k, :], ACT.Relu, scale=root[:, col : col + 1])
             return relu
 
-        def square_and_round(c, g, relu):
-            h_abs = tile([P, CHUNK * PACK], BF16, f"h_abs{c}_{g}")
+        def square_and_round(g, relu):
+            h_abs = tile([P, CHUNK * PACK], BF16, f"h_abs0_{g}")
             interleave(h_abs[:], relu[:], ACT.Square)
             return h_abs
 
-        def sign(c, g, h_abs, engine):
-            run = SIGN_RUN * PACK
+        def times_pattern(engine, dst, src, pattern):
+            run = RUN * PACK
             engine.tensor_tensor(
-                h[c][:, g, :].rearrange("p (a b) -> p a b", b=run),
-                h_abs[:].rearrange("p (a b) -> p a b", b=run),
-                signs[:, g].rearrange("p j t -> p (j t)").unsqueeze(1).to_broadcast([P, CHUNK // SIGN_RUN, run]),
+                dst.rearrange("p (a b) -> p a b", b=run),
+                src.rearrange("p (a b) -> p a b", b=run),
+                pattern.rearrange("p j t -> p (j t)").unsqueeze(1).to_broadcast([P, CHUNK // RUN, run]),
                 ALU.mult,
             )
 
-        def rectified(c, g, on=None):
-            relu = tile([P, PACK, CHUNK], F32, f"relu{c}_{g}", on=on)
-            for first in range(0, PACK, PAIR):
-                nc.scalar.activation(relu[:, first : first + PAIR, :], up_slices(c, g, first, PAIR)[:], ACT.Relu)
+        def rectified_interleaved(c, relu):
+            for b in range(CHUNK // HALF):
+                a = bank([P, PACK, HALF], b, "a")
+                for t in range(PACK):
+                    up(a[:, t, :], c, 0, t, slice(b * HALF, (b + 1) * HALF))
+                nc.scalar.activation(
+                    relu[:, b * BANK : (b + 1) * BANK].rearrange("p (j t) -> p j t", t=PACK),
+                    a[:].rearrange("p t j -> p j t"),
+                    ACT.Relu,
+                )
+            return relu
+
+        def rectified(c, relu):
+            for b in range(PACK // PAIR):
+                a = up_slices(c, 1, b * PAIR, PAIR, PAIR + b)
+                nc.scalar.activation(relu[:, b * PAIR : (b + 1) * PAIR, :], a[:], ACT.Relu)
             return relu
 
         def squared(c, g, relu):
-            square = tile([P, PACK, CHUNK], F32, f"square{c}_{g}")
+            square = tile(relu.shape, F32, f"square{c}_{g}")
             nc.scalar.activation(square[:], relu[:], ACT.Square)
             return square
 
-        def scale_and_round(c, square, scaled):
+        def scale(c, square):
+            scaled = laid_tile([P, PACK, CHUNK], F32, f"scaled{c}", c * REGION + 3 * KIB)
             for t in range(PACK):
                 nc.scalar.activation(scaled[:, t, :], square[:, t, :], ACT.Copy, scale=sm_pass1[:, t : t + 1])
-            interleave(h[c][:, 1, :], scaled[:], ACT.Copy)
+            return scaled
 
-        def quantise(c, first=0, count=R_PASSES):
-            columns = slice(first * CHUNK, (first + count) * CHUNK)
+        def quantise(c):
             nc.vector.quantize_mx(
-                out=h_w[c][:, columns].bitcast(FP8X4),
-                scales=h_s[c][:, columns],
-                in_=h[c][:, first : first + count, :].rearrange("p g x -> p (g x)"),
+                out=codes[c][:].bitcast(FP8X4), scales=planes[c][:], in_=h[c][:].rearrange("p g x -> p (g x)")
             )
 
-        def gather_gates(i, picked):
-            picked_g[i] = picked[:]
-            nc.vector.tensor_tensor(picked_g[i], gates[i][:].indirect(offsets[:]), wgo_sb[:], ALU.mult)
-
-        def gather_gates_in_halves(i):
-            picked_g[i] = tile([P, J], F32, f"picked_g{i}")[:]
-            half = J // 2
-            low, high = offsets[:, 0 : half // GROUP], offsets[:, half // GROUP :]
-            nc.vector.tensor_tensor(picked_g[i][:, 0:half], gates[i][:].indirect(low), wgo_low[:], ALU.mult)
-            nc.vector.tensor_tensor(picked_g[i][:, half:], gates[i][:].indirect(high), wgo_sb[:, half:], ALU.mult)
-
-        def down(y_ps, c, i):
+        def down8(dst, c, i):
             nc.tensor.matmul_mx(
-                out=y_ps,
+                out=dst,
                 lhsT=wd8_w[:, i * P : (i + 1) * P].bitcast(FP8X4),
                 lhsT_scale=wd_s[SCALE_ROWS:P, i * P : (i + 1) * P],
-                rhs=h_w[c][:, 0:CHUNK].bitcast(FP8X4),
-                rhs_scale=h_s[c][:, 0:CHUNK],
+                rhs=h_w[c][0].bitcast(FP8X4),
+                rhs_scale=h_s[c][0],
                 start=True,
                 stop=False,
             )
+
+        def down4(dst, c, i):
             nc.tensor.matmul_mx(
-                out=y_ps,
+                out=dst,
                 lhsT=wd4_w[:, 2 * i * P : 2 * (i + 1) * P].bitcast(FP4X4),
                 lhsT_scale=wd_s[:, i * P : (i + 1) * P],
-                rhs=h_w[c][:, CHUNK:].bitcast(FP8X4),
-                rhs_scale=h_s[c][:, CHUNK:],
+                rhs=h_w[c][1].bitcast(FP8X4),
+                rhs_scale=h_s[c][1],
                 start=False,
                 stop=True,
             )
 
-        def begin_down(first, i):
-            begun[first, i] = psum.tile([P, BANK], F32, name="y_ps", tag=f"bank{DOWN_BANKS[first, i]}")
-            down(begun[first, i][:, 0:CHUNK], first, i)
-            return begun[first, i]
+        def down_products(c, count=N_PAGES):
+            for i in range(count):
+                y_ps[c, i] = bank([P, BANK], N_PAGES + i, "y_ps")
+                down8(y_ps[c, i][:, 0:CHUNK], c, i)
+                if c > 0:
+                    down4(y_ps[c, i][:, 0:CHUNK], c, i)
+            if c == 0:
+                for i in range(count):
+                    down4(y_ps[c, i][:, 0:CHUNK], c, i)
 
-        def scatter(items, on=None):
-            y = tile([P, sum(count for first, count, i in items) * CHUNK], F32, "y%d_%d" % items[0][::2], on=on)
-            at = 0
-            for first, count, i in items:
-                width = count * CHUNK
-                y_ps = begun[first, i] if (first, i) in begun else begin_down(first, i)
-                for c in range(1, count):
-                    down(y_ps[:, c * CHUNK : (c + 1) * CHUNK], first + c, i)
-                y_sb = y[:, at : at + width]
-                at = at + width
-                nc.scalar.copy(y_sb, y_ps[:, 0:width])
-                nc.vector.tensor_tensor(
-                    pages[i][:].indirect(offsets[:, first * COLS : (first + count) * COLS]),
-                    y_sb,
-                    picked_g[i][:, first * CHUNK : first * CHUNK + width],
-                    ALU.mult,
-                )
-                if first + count == N_CHUNKS:
-                    nc.sync.dma_start(out[i * P : (i + 1) * P, :], pages[i][:])
+        def copy_y(c, i, dst=None):
+            y[c, i] = dst if dst is not None else tile([P, CHUNK], F32, f"y{c}_{i}")
+            nc.scalar.copy(y[c, i][:], y_ps[c, i][:, 0:CHUNK])
 
-        def gate(c, i, y, engine, z):
-            engine.tensor_tensor(z[:], y, picked_g[i][:, c * CHUNK : (c + 1) * CHUNK], ALU.mult)
-            return z
+        def gate(c, i, dst, weights):
+            z[c, i] = dst
+            nc.gpsimd.tensor_tensor(dst[:], y[c, i][:], weights, ALU.mult)
 
-        def place(c, i, z):
-            nc.vector.tensor_copy(pages[i][:].indirect(offsets[:, c * COLS : (c + 1) * COLS]), z[:])
+        def place(c, i):
+            nc.vector.tensor_copy(pages[i][:].indirect(listed(c)), z[c, i][:])
 
-        gather_gates(0, tile([P, J], F32, "picked_g0"))
-        gather_gates_in_halves(1)
-        sign(0, 0, square_and_round(0, 0, rectified_root(0, 0, count=1)), nc.vector)
+        def scatter(first, count, i, values, weights):
+            nc.vector.tensor_tensor(pages[i][:].indirect(listed(first, count)), values, weights, ALU.mult)
+            if first + count == N_CHUNKS:
+                nc.sync.dma_start(out[i * P : (i + 1) * P, :], pages[i][:])
+
+        gw[0] = tile([P, J], F32, "gw0")
+        nc.vector.tensor_tensor(gw[0][:], gates[0][:].indirect(offsets[:]), wgo_sb[:], ALU.mult)
+        gw[1] = tile([P, J], F32, "gw1")
+        nc.vector.tensor_tensor(gw[1][:, tokens(0, 2)], gates[1][:].indirect(listed(0, 2)), wgo_low[:], ALU.mult)
+        nc.vector.tensor_tensor(gw[1][:, tokens(2, 2)], gates[1][:].indirect(listed(2, 2)), wgo_sb[:, tokens(2, 2)], ALU.mult)
+        times_pattern(nc.vector, h[0][:, 0, :], square_and_round(0, rectified_root(0, FIRST_BANKS))[:], signs[:, 0])
         gates.append(tile([P, T], F32, "gates3", on="relu0_0"))
         nc.sync.dma_start(gates[3][:], gT[3 * P : 4 * P, :])
-        sign(0, 1, square_and_round(0, 1, rectified_root(0, 1)), nc.vector)
-        quantise(0, 0, 1)
-        quantise(0, 1, 1)
-        gather_gates(2, tile([P, J], F32, "picked_g2", on="h_abs0_1"))
-        clear_page(1, on="wgo_low")
-        scatter([(0, 1, 0), (0, 1, 1)])
-        begin_down(0, 2)
-        begin_down(0, 3)
-        clear_page(2, on="h_s0")
+        times_pattern(nc.vector, h[0][:, 1, :], square_and_round(1, rectified_root(1, (2, 3)))[:], signs[:, 1])
+        for g in range(R_PASSES):
+            nc.vector.quantize_mx(out=h_w[0][g].bitcast(FP8X4), scales=h_s[0][g], in_=h[0][:, g, :])
+        gw[2] = tile([P, J], F32, "gw2", on="h_abs0_1")
+        nc.vector.tensor_tensor(gw[2][:], gates[2][:].indirect(offsets[:]), wgo_sb[:], ALU.mult)
+        clear(3, tile([P, T], F32, "page3", on="wgo_low"))
+        gw3 = {0: tile([P, CHUNK], F32, "gw3_0")}
+        nc.vector.tensor_tensor(gw3[0][:], gates[3][:].indirect(listed(0)), wgo_first[:], ALU.mult)
+        picked3 = tile([P, J - CHUNK], F32, "picked3")
+        nc.vector.tensor_copy(picked3[:], gates[3][:].indirect(listed(1, LAST)))
 
-        sign(1, 0, square_and_round(1, 0, rectified_root(1, 0)), nc.vector)
-        scale_and_round(1, squared(1, 1, rectified(1, 1)), laid_tile([P, PACK, CHUNK], F32, "scaled1", 0))
-        quantise(1)
-        clear_page(3, on="h1")
-        z = gate(0, 2, begun[0, 2][:, 0:CHUNK], nc.vector, laid_tile([P, CHUNK], F32, "z0_2", 0))
-        gather_gates(3, laid_tile([P, J], F32, "picked_g3", CHUNK_BYTES))
-        place(0, 2, z)
+        relu0 = tile([P, CHUNK * PACK], F32, "relu1_0")
+        relu1 = tile([P, PACK, CHUNK], F32, "relu1_1")
+        for c in range(LAST):
+            d = c + 1
+            rectified_interleaved(d, relu0)
+            rectified(d, relu1)
+            square0 = squared(d, 0, relu0)
+            if d < LAST:
+                square1 = squared(d, 1, relu1)
+            down_products(c)
+            for i in range(2):
+                copy_y(c, i)
+            if d == LAST:
+                square1 = squared(d, 1, relu1)
+            if c > 0:
+                place(c - 1, 2)
+                gate(c - 1, 3, tile([P, CHUNK], F32, f"z{c - 1}_3", on=f"y{c - 1}_0"), gw3[c - 1][:])
+                place(c - 1, 3)
+                count = 1 if d < LAST else 2
+                gw3[c] = tile([P, count * CHUNK], F32, f"gw3_{c}", on=f"y{c - 1}_3")
+                nc.gpsimd.tensor_tensor(gw3[c][:], picked3[:, tokens(c - 1, count)], wgo_sb[:, tokens(c, count)], ALU.mult)
+            for i in range(2):
+                dst = tile([P, CHUNK], F32, f"z{c}_{i}") if c > 0 else laid_tile([P, CHUNK], F32, f"z0_{i}", i * KIB)
+                gate(c, i, dst, gw[i][:, tokens(c)])
+                place(c, i)
+            h[d] = tile([P, R_PASSES, CHUNK * PACK], BF16, f"h{d}", on=f"y{c}_0")
+            times_pattern(nc.gpsimd, h[d][:, 0, :], square0[:], sm_run[:])
+            scaled = scale(d, square1)
+            if d < LAST:
+                copy_y(c, 2)
+            interleave(h[d][:, 1, :], scaled[:], ACT.Copy)
+            if d < LAST:
+                copy_y(c, 3)
+            quantise(d)
+            behind = laid_tile([P, CHUNK], F32, f"behind{d}", d * REGION + 4 * KIB)
+            if d < LAST:
+                gate(c, 2, behind, gw[2][:, tokens(c)])
+                relu0 = laid_tile([P, CHUNK * PACK], F32, f"relu{d + 1}_0", d * REGION)
+                relu1 = laid_tile([P, PACK, CHUNK], F32, f"relu{d + 1}_1", d * REGION + 5 * KIB)
+            else:
+                copy_y(c, 2, behind)
+                scatter(c, 1, 2, behind[:], gw[2][:, tokens(c)])
 
-        h_abs = square_and_round(2, 0, rectified_root(2, 0))
-        relu = rectified(2, 1, on="square1_1")
-        y = tile([P, 3, CHUNK], F32, "y1", on="relu2_0")
-        for k, (c, i) in enumerate(((1, 0), (0, 3), (1, 2))):
-            y_ps = begun[c, i] if (c, i) in begun else begin_down(c, i)
-            nc.scalar.copy(y[:, k, :], y_ps[:, 0:CHUNK])
-            place(c, i, gate(c, i, y[:, k, :], nc.gpsimd, tile([P, CHUNK], F32, f"z{c}_{i}")))
-        h[2] = tile([P, R_PASSES, CHUNK * PACK], BF16, "h2", on="relu2_0")
-        sign(2, 0, h_abs, nc.gpsimd)
-        square = squared(2, 1, relu)
-        y = tile([P, CHUNK], F32, "y1_3", on="square1_1")
-        down(begun[0, 3][:, CHUNK:], 1, 3)
-        nc.scalar.copy(y[:], begun[0, 3][:, CHUNK:])
-        place(1, 3, gate(1, 3, y[:], nc.gpsimd, tile([P, CHUNK], F32, "z1_3")))
-        h[3] = tile([P, R_PASSES, CHUNK * PACK], BF16, "h3", on="h_abs2_0")
-        sign(3, 0, square_and_round(3, 0, rectified_root(3, 0)), nc.gpsimd)
-        scale_and_round(2, square, tile([P, PACK, CHUNK], F32, "scaled2"))
-        quantise(2)
-        scatter([(1, 1, 1)], on="scaled2")
-
-        square = squared(3, 1, rectified(3, 1))
-        scatter([(2, 1, 0), (2, 1, 1)], on="relu3_1")
-        scale_and_round(3, square, tile([P, PACK, CHUNK], F32, "scaled3"))
-        quantise(3)
-        scatter([(2, 1, 2)], on="scaled3")
-        scatter([(3, 1, 0), (3, 1, 1), (3, 1, 2), (2, 2, 3)])
+        down_products(LAST, N_PAGES - 1)
+        for i in range(N_PAGES - 1):
+            copy_y(LAST, i)
+            scatter(LAST, 1, i, y[LAST, i][:], gw[i][:, tokens(LAST)])
+        both = y_ps[LAST - 1, N_PAGES - 1]
+        down8(both[:, CHUNK:], LAST, N_PAGES - 1)
+        down4(both[:, CHUNK:], LAST, N_PAGES - 1)
+        y_both = tile([P, BANK], F32, "y_both")
+        nc.scalar.copy(y_both[:], both[:])
+        scatter(LAST - 1, 2, N_PAGES - 1, y_both[:], gw3[LAST - 1][:])

@@ -120,7 +120,7 @@ def tile_list_modp_relu2_mix_gate_kernel(
 
         wgo_sb = tile([P, J], F32, "wgo_sb")
         wgo_low = tile([P, J // 2], F32, "wgo_low")
-        wgo_first = laid_tile([P, CHUNK], F32, "wgo_first", KIB // 2)
+        wgo_first = laid_tile([P, 2 * CHUNK], F32, "wgo_first", KIB // 2)[:, 0:CHUNK]
         for b in range(WGO_RUN // LINE):
             spread = bank([P, LINE, P], WGO_BANK + b, "spread")
             for k in range(LINE):
@@ -135,7 +135,7 @@ def tile_list_modp_relu2_mix_gate_kernel(
                 spread[:, :, 0 : P // 2].rearrange("p k m -> p m k"),
             )
             nc.scalar.copy(
-                wgo_first[:].rearrange("p (m i) -> p m i", i=WGO_RUN)[:, :, b * LINE : (b + 1) * LINE],
+                wgo_first.rearrange("p (m i) -> p m i", i=WGO_RUN)[:, :, b * LINE : (b + 1) * LINE],
                 spread[:, :, 0 : CHUNK // WGO_RUN].rearrange("p k m -> p m k"),
             )
 
@@ -188,7 +188,7 @@ def tile_list_modp_relu2_mix_gate_kernel(
         codes = {c: tile([P, R_PASSES * CHUNK], U32, f"h_w{c}") for c in range(1, N_CHUNKS)}
         planes = [tile([P, R_PASSES * CHUNK], U8, f"h_s{c}") for c in range(N_CHUNKS)]
         h_w = {c: [codes[c][:, tokens(g)] for g in range(R_PASSES)] for c in codes}
-        h_w[0] = [tile([P, CHUNK], U32, "h_w0_0")[:], laid_tile([P, CHUNK], U32, "h_w0_1", REGION + 3 * KIB)[:]]
+        h_w[0] = [tile([P, CHUNK], U32, f"h_w0_{g}")[:] for g in range(R_PASSES)]
         h_s = [[plane[:, tokens(g)] for g in range(R_PASSES)] for plane in planes]
         gw = {}
         y_ps = {}
@@ -340,7 +340,7 @@ def tile_list_modp_relu2_mix_gate_kernel(
         nc.vector.tensor_tensor(gw[2][:], gates[2][:].indirect(offsets[:]), wgo_sb[:], ALU.mult)
         clear(3, tile([P, T], F32, "page3", on="wgo_low"))
         gw3 = {0: tile([P, CHUNK], F32, "gw3_0")}
-        nc.vector.tensor_tensor(gw3[0][:], gates[3][:].indirect(listed(0)), wgo_first[:], ALU.mult)
+        nc.vector.tensor_tensor(gw3[0][:], gates[3][:].indirect(listed(0)), wgo_first, ALU.mult)
         picked3 = tile([P, J - CHUNK], F32, "picked3")
         nc.vector.tensor_copy(picked3[:], gates[3][:].indirect(listed(1, LAST)))
 
@@ -348,19 +348,22 @@ def tile_list_modp_relu2_mix_gate_kernel(
         relu1 = tile([P, PACK, CHUNK], F32, "relu1_1")
         for c in range(LAST):
             d = c + 1
-            rectified_interleaved(d, relu0)
             rectified(d, relu1)
-            square0 = squared(d, 0, relu0)
+            rectified_interleaved(d, relu0)
+            square1 = squared(d, 1, relu1)
             if d < LAST:
-                square1 = squared(d, 1, relu1)
+                square0 = squared(d, 0, relu0)
+            if c == 0:
+                scaled = scale(d, square1)
             down_products(c)
             for i in range(2):
                 copy_y(c, i)
             if d == LAST:
-                square1 = squared(d, 1, relu1)
+                square0 = squared(d, 0, relu0)
             if c > 0:
                 place(c - 1, 2)
-                gate(c - 1, 3, tile([P, CHUNK], F32, f"z{c - 1}_3", on=f"y{c - 1}_0"), gw3[c - 1][:])
+                dst = tile([P, CHUNK], F32, f"z{c - 1}_3", on=f"y{c - 1}_0") if c > 1 else laid_tile([P, CHUNK], F32, "z0_3", 3 * KIB)
+                gate(c - 1, 3, dst, gw3[c - 1][:])
                 place(c - 1, 3)
                 count = 1 if d < LAST else 2
                 gw3[c] = tile([P, count * CHUNK], F32, f"gw3_{c}", on=f"y{c - 1}_3")
@@ -369,9 +372,13 @@ def tile_list_modp_relu2_mix_gate_kernel(
                 dst = tile([P, CHUNK], F32, f"z{c}_{i}") if c > 0 else laid_tile([P, CHUNK], F32, f"z0_{i}", i * KIB)
                 gate(c, i, dst, gw[i][:, tokens(c)])
                 place(c, i)
-            h[d] = tile([P, R_PASSES, CHUNK * PACK], BF16, f"h{d}", on=f"y{c}_0")
+            if c == 0:
+                h[d] = laid_tile([P, R_PASSES, CHUNK * PACK], BF16, f"h{d}", 2 * KIB)
+            else:
+                h[d] = tile([P, R_PASSES, CHUNK * PACK], BF16, f"h{d}", on=f"y{c}_0")
             times_pattern(nc.gpsimd, h[d][:, 0, :], square0[:], sm_run[:])
-            scaled = scale(d, square1)
+            if c > 0:
+                scaled = scale(d, square1)
             if d < LAST:
                 copy_y(c, 2)
             interleave(h[d][:, 1, :], scaled[:], ACT.Copy)

@@ -83,12 +83,12 @@ def tile_list_modp_relu2_mix_gate_kernel(
         wu_raw_s = tile([P, PASS], U8, "wu_raw_s")
         wu_w = [tile([P, PASS], I32, f"wu_w{g}") for g in range(R_PASSES)]
         wu_s = tile([P, PASS], U8, "wu_s")
-        sm_sb = tile([P, R_PASSES, PACK], F32, "sm_sb")
+        sm_sb = tile([P, R_PASSES, 2 * PACK], F32, "sm_sb")[:, :, 0:PACK]
 
         nc.vector.memset(tab_s[:].bitcast(I32), 0)
         nc.vector.memset(wu_raw_s[:].bitcast(I32), 0)
         nc.sync.dma_start(offsets[:], offs)
-        nc.sync.dma_start(sm_sb[:], sm.rearrange("(g p t) -> p g t", g=R_PASSES, t=PACK))
+        nc.sync.dma_start(sm_sb, sm.rearrange("(g p t) -> p g t", g=R_PASSES, t=PACK))
         wgo_row = tile([P, WGO_RUN], F32, "wgo_row")
         nc.sync.dma_start(wgo_row[:], wgo[0].rearrange("(p i) -> p i", i=WGO_RUN))
         identity = tile([P, P], F32, "identity")
@@ -169,7 +169,7 @@ def tile_list_modp_relu2_mix_gate_kernel(
         clear(1, laid_tile([P, T], F32, "page1", HEAD_REGION + 3 * KIB))
         clear(2, tile([P, T], F32, "page2", on="first_w"))
 
-        gates = [tile([P, T], F32, f"gates{i}", on=name) for i, name in enumerate(("sm_abs1", "sm_abs0", "sm_sb"))]
+        gates = [tile([P, T], F32, f"gates{i}", on=name) for i, name in enumerate((None, None, "sm_sb"))]
         nc.sync.dma_start(gates[0][:], gT[0:P, :])
         nc.sync.dma_start(gates[1][:], gT[P : 2 * P, :])
         for q in range(QUADRANTS):

@@ -23,6 +23,7 @@ PASS = P * PACK
 QUADRANTS = 4
 QUAD = P // QUADRANTS
 SCALE_ROWS = 4
+TAB_ROW = 12
 GROUP = 16
 CHUNK = 256
 HALF = CHUNK // 2
@@ -44,6 +45,7 @@ WGO_BANK = 6
 FIRST_BANKS = (0, 1, 4, 5)
 REGION = 9 * KIB
 HEAD_REGION = N_CHUNKS * REGION
+H_AT = {1: 2 * KIB, 2: HEAD_REGION + 11 * KIB, 3: HEAD_REGION + 15 * KIB}
 
 
 def tile_list_modp_relu2_mix_gate_kernel(
@@ -94,7 +96,7 @@ def tile_list_modp_relu2_mix_gate_kernel(
         identity = tile([P, P], F32, "identity")
         make_identity(nc, identity[:])
         for r in range(SCALE_ROWS):
-            nc.sync.dma_start(tab_s[r:P:QUAD, :].bitcast(I32), tab_scales[0].bitcast(I32)[r::SCALE_ROWS, :])
+            nc.sync.dma_start(tab_s[TAB_ROW + r : P : QUAD, :].bitcast(I32), tab_scales[0].bitcast(I32)[r::SCALE_ROWS, :])
         nc.sync.dma_start(tab_w[:], tab_words[0].rearrange("p t i -> p (t i)").bitcast(I32))
         for q in range(QUADRANTS):
             nc.sync.dma_start(
@@ -152,15 +154,17 @@ def tile_list_modp_relu2_mix_gate_kernel(
             wu_s[:].rearrange("p (t m) -> p m t", t=PACK),
             wu_raw_s[:].rearrange("p (m t) -> p m t", t=PACK),
         )
-        for g in range(R_PASSES):
-            nc.vector.tensor_copy(
-                wu_w[g][:].rearrange("p (t m) -> p m t", t=PACK),
-                wu_raw_w[g][:].rearrange("p (m t) -> p m t", t=PACK),
+        second_w = tile([P, CHUNK], U32, "second_w")
+        nc.vector.tensor_copy(second_w[:], tab_w[:].bitcast(U32).indirect(listed(1)))
+        for g, (move, words) in enumerate(((nc.scalar.copy, U32), (nc.vector.tensor_copy, I32))):
+            move(
+                wu_w[g][:].bitcast(words).rearrange("p (t m) -> p m t", t=PACK),
+                wu_raw_w[g][:].bitcast(words).rearrange("p (m t) -> p m t", t=PACK),
             )
-        rest_w = laid_tile([P, J - CHUNK], U32, "rest_w", HEAD_REGION)
-        nc.vector.tensor_copy(rest_w[:], tab_w[:].bitcast(U32).indirect(listed(1, LAST)))
-        picked_w = [first_w[:]] + [rest_w[:, tokens(c)] for c in range(LAST)]
-        picked_s = [all_s[:, tokens(c)] for c in range(N_CHUNKS)]
+        rest_w = laid_tile([P, 2 * CHUNK], U32, "rest_w", HEAD_REGION + KIB)
+        nc.vector.tensor_copy(rest_w[:], tab_w[:].bitcast(U32).indirect(listed(2, 2)))
+        picked_w = [first_w[:], second_w[:]] + [rest_w[:, tokens(c)] for c in range(2)]
+        picked_s = [all_s[TAB_ROW:P, tokens(c)] for c in range(N_CHUNKS)]
 
         def clear(i, page):
             pages[i] = page
@@ -356,26 +360,22 @@ def tile_list_modp_relu2_mix_gate_kernel(
             if c == 0:
                 scaled = scale(d, square1)
             down_products(c)
-            for i in range(2):
-                copy_y(c, i)
+            copy_y(c, 0, laid_tile([P, CHUNK], F32, f"y{c}_0", H_AT[d]) if c > 0 else None)
+            copy_y(c, 1)
             if d == LAST:
                 square0 = squared(d, 0, relu0)
             if c > 0:
                 place(c - 1, 2)
-                dst = tile([P, CHUNK], F32, f"z{c - 1}_3", on=f"y{c - 1}_0") if c > 1 else laid_tile([P, CHUNK], F32, "z0_3", 3 * KIB)
-                gate(c - 1, 3, dst, gw3[c - 1][:])
+                gate(c - 1, 3, laid_tile([P, CHUNK], F32, f"z{c - 1}_3", H_AT[c] + KIB), gw3[c - 1][:])
                 place(c - 1, 3)
                 count = 1 if d < LAST else 2
-                gw3[c] = tile([P, count * CHUNK], F32, f"gw3_{c}", on=f"y{c - 1}_3")
+                gw3[c] = laid_tile([P, count * CHUNK], F32, f"gw3_{c}", H_AT[c] + 2 * KIB)
                 nc.gpsimd.tensor_tensor(gw3[c][:], picked3[:, tokens(c - 1, count)], wgo_sb[:, tokens(c, count)], ALU.mult)
             for i in range(2):
                 dst = tile([P, CHUNK], F32, f"z{c}_{i}") if c > 0 else laid_tile([P, CHUNK], F32, f"z0_{i}", i * KIB)
                 gate(c, i, dst, gw[i][:, tokens(c)])
                 place(c, i)
-            if c == 0:
-                h[d] = laid_tile([P, R_PASSES, CHUNK * PACK], BF16, f"h{d}", 2 * KIB)
-            else:
-                h[d] = tile([P, R_PASSES, CHUNK * PACK], BF16, f"h{d}", on=f"y{c}_0")
+            h[d] = laid_tile([P, R_PASSES, CHUNK * PACK], BF16, f"h{d}", H_AT[d])
             times_pattern(nc.gpsimd, h[d][:, 0, :], square0[:], sm_run[:])
             if c > 0:
                 scaled = scale(d, square1)

@@ -45,7 +45,8 @@ WGO_BANK = 6
 FIRST_BANKS = (0, 1, 4, 5)
 REGION = 9 * KIB
 HEAD_REGION = N_CHUNKS * REGION
-H_AT = {1: 2 * KIB, 2: HEAD_REGION + 11 * KIB, 3: HEAD_REGION + 15 * KIB}
+EARLY = CHUNK + HALF
+H_AT = {1: 2 * KIB, 2: HEAD_REGION + 16 * KIB, 3: HEAD_REGION + 20 * KIB}
 
 
 def tile_list_modp_relu2_mix_gate_kernel(
@@ -81,7 +82,7 @@ def tile_list_modp_relu2_mix_gate_kernel(
         offsets = keep.tile([P, J // GROUP], U16, name="offsets")
         tab_w = tile([P, T], I32, "tab_w")
         tab_s = tile([P, T], U8, "tab_s")
-        wu_raw_w = [tile([P, PASS], I32, "wu_raw_w0"), laid_tile([P, PASS], I32, "wu_raw_w1", HEAD_REGION + 2 * KIB)]
+        wu_raw_w = [tile([P, PASS], I32, "wu_raw_w0"), laid_tile([P, PASS], I32, "wu_raw_w1", HEAD_REGION + 7 * KIB)]
         wu_raw_s = tile([P, PASS], U8, "wu_raw_s")
         wu_w = [tile([P, PASS], I32, f"wu_w{g}") for g in range(R_PASSES)]
         wu_s = tile([P, PASS], U8, "wu_s")
@@ -148,30 +149,30 @@ def tile_list_modp_relu2_mix_gate_kernel(
 
         all_s = tile([P, J], U8, "all_s")
         nc.vector.tensor_copy(all_s[:], tab_s[:].indirect(offsets[:]))
-        first_w = tile([P, CHUNK], U32, "first_w")
-        nc.vector.tensor_copy(first_w[:], tab_w[:].bitcast(U32).indirect(listed(0)))
+        first_w = tile([P, EARLY], U32, "first_w")
+        nc.vector.tensor_copy(first_w[:], tab_w[:].bitcast(U32).indirect(offsets[:, 0 : EARLY // GROUP]))
         nc.vector.tensor_copy(
             wu_s[:].rearrange("p (t m) -> p m t", t=PACK),
             wu_raw_s[:].rearrange("p (m t) -> p m t", t=PACK),
         )
-        second_w = tile([P, CHUNK], U32, "second_w")
-        nc.vector.tensor_copy(second_w[:], tab_w[:].bitcast(U32).indirect(listed(1)))
-        for g, (move, words) in enumerate(((nc.scalar.copy, U32), (nc.vector.tensor_copy, I32))):
-            move(
-                wu_w[g][:].bitcast(words).rearrange("p (t m) -> p m t", t=PACK),
-                wu_raw_w[g][:].bitcast(words).rearrange("p (m t) -> p m t", t=PACK),
+        for first in range(0, PACK, PAIR):
+            nc.scalar.copy(
+                wu_w[0][:].bitcast(U32).rearrange("p (t m) -> p m t", t=PACK)[:, :, first : first + PAIR],
+                wu_raw_w[0][:].bitcast(U32).rearrange("p (m t) -> p m t", t=PACK)[:, :, first : first + PAIR],
             )
-        rest_w = laid_tile([P, 2 * CHUNK], U32, "rest_w", HEAD_REGION + KIB)
-        nc.vector.tensor_copy(rest_w[:], tab_w[:].bitcast(U32).indirect(listed(2, 2)))
-        picked_w = [first_w[:], second_w[:]] + [rest_w[:, tokens(c)] for c in range(2)]
-        picked_s = [all_s[TAB_ROW:P, tokens(c)] for c in range(N_CHUNKS)]
+        nc.vector.tensor_copy(
+            wu_w[1][:].rearrange("p (t m) -> p m t", t=PACK),
+            wu_raw_w[1][:].rearrange("p (m t) -> p m t", t=PACK),
+        )
+        rest_w = tile([P, J - EARLY], U32, "rest_w", on="wu_raw_w0")
+        nc.vector.tensor_copy(rest_w[:], tab_w[:].bitcast(U32).indirect(offsets[:, EARLY // GROUP :]))
 
         def clear(i, page):
             pages[i] = page
             nc.gpsimd.memset(page[:].bitcast(I32), 0)
 
-        clear(1, laid_tile([P, T], F32, "page1", HEAD_REGION + 3 * KIB))
-        clear(2, tile([P, T], F32, "page2", on="first_w"))
+        clear(1, laid_tile([P, T], F32, "page1", HEAD_REGION + 8 * KIB))
+        clear(2, laid_tile([P, T], F32, "page2", HEAD_REGION))
 
         gates = [tile([P, T], F32, f"gates{i}", on=name) for i, name in enumerate((None, None, "sm_sb"))]
         nc.sync.dma_start(gates[0][:], gT[0:P, :])
@@ -199,21 +200,24 @@ def tile_list_modp_relu2_mix_gate_kernel(
         y = {}
         z = {}
 
-        def up(a, c, g, t, columns):
+        def up(a, g, t, first, count):
+            words = first_w[:, first : first + count] if first < EARLY else rest_w[:, first - EARLY : first - EARLY + count]
             nc.tensor.matmul_mx(
                 out=a,
                 lhsT=wu_w[g][:, t * P : (t + 1) * P].bitcast(FP8X4),
                 lhsT_scale=wu_s[SCALE_ROWS * g : P, t * P : (t + 1) * P],
-                rhs=picked_w[c][:, columns].bitcast(FP8X4),
-                rhs_scale=picked_s[c][:, columns],
+                rhs=words.bitcast(FP8X4),
+                rhs_scale=all_s[TAB_ROW:P, first : first + count],
                 start=True,
                 stop=True,
             )
 
         def up_slices(c, g, first, count, index):
             a = bank([P, count, CHUNK], index, "a")
+            width = HALF if c * CHUNK < EARLY < (c + 1) * CHUNK else CHUNK
             for k in range(count):
-                up(a[:, k, :], c, g, first + k, slice(0, CHUNK))
+                for at in range(0, CHUNK, width):
+                    up(a[:, k, at : at + width], g, first + k, c * CHUNK + at, width)
             return a
 
         def interleave(dst, src, func):
@@ -251,7 +255,7 @@ def tile_list_modp_relu2_mix_gate_kernel(
             for b in range(CHUNK // HALF):
                 a = bank([P, PACK, HALF], b, "a")
                 for t in range(PACK):
-                    up(a[:, t, :], c, 0, t, slice(b * HALF, (b + 1) * HALF))
+                    up(a[:, t, :], 0, t, c * CHUNK + b * HALF, HALF)
                 nc.scalar.activation(
                     relu[:, b * BANK : (b + 1) * BANK].rearrange("p (j t) -> p j t", t=PACK),
                     a[:].rearrange("p t j -> p j t"),
@@ -270,11 +274,15 @@ def tile_list_modp_relu2_mix_gate_kernel(
             nc.scalar.activation(square[:], relu[:], ACT.Square)
             return square
 
-        def scale(c, square):
-            scaled = laid_tile([P, PACK, CHUNK], F32, f"scaled{c}", c * REGION + 3 * KIB)
-            for t in range(PACK):
-                nc.scalar.activation(scaled[:, t, :], square[:, t, :], ACT.Copy, scale=sm_pass1[:, t : t + 1])
-            return scaled
+        def scale(c, square, pieces=1):
+            width = CHUNK // pieces
+            scaled = laid_tile([P, pieces, PACK, width], F32, f"scaled{c}", c * REGION + 3 * KIB)
+            for k in range(pieces):
+                for t in range(PACK):
+                    nc.scalar.activation(
+                        scaled[:, k, t, :], square[:, t, k * width : (k + 1) * width], ACT.Copy, scale=sm_pass1[:, t : t + 1]
+                    )
+            return [scaled[:, k] for k in range(pieces)]
 
         def quantise(c):
             nc.vector.quantize_mx(
@@ -378,10 +386,12 @@ def tile_list_modp_relu2_mix_gate_kernel(
             h[d] = laid_tile([P, R_PASSES, CHUNK * PACK], BF16, f"h{d}", H_AT[d])
             times_pattern(nc.gpsimd, h[d][:, 0, :], square0[:], sm_run[:])
             if c > 0:
-                scaled = scale(d, square1)
+                scaled = scale(d, square1, 1 if d < LAST else 2)
             if d < LAST:
                 copy_y(c, 2)
-            interleave(h[d][:, 1, :], scaled[:], ACT.Copy)
+            width = CHUNK * PACK // len(scaled)
+            for k, piece in enumerate(scaled):
+                interleave(h[d][:, 1, k * width : (k + 1) * width], piece, ACT.Copy)
             if d < LAST:
                 copy_y(c, 3)
             quantise(d)

@@ -193,7 +193,7 @@ def tile_list_modp_relu2_mix_gate_kernel(
         codes = {c: tile([P, R_PASSES * CHUNK], U32, f"h_w{c}") for c in range(1, N_CHUNKS)}
         planes = [tile([P, R_PASSES * CHUNK], U8, f"h_s{c}") for c in range(N_CHUNKS)]
         h_w = {c: [codes[c][:, tokens(g)] for g in range(R_PASSES)] for c in codes}
-        h_w[0] = [tile([P, CHUNK], U32, f"h_w0_{g}")[:] for g in range(R_PASSES)]
+        h_w[0] = [tile([P, CHUNK], U32, "h_w0_0")[:], laid_tile([P, CHUNK], U32, "h_w0_1", REGION + 3 * KIB)[:]]
         h_s = [[plane[:, tokens(g)] for g in range(R_PASSES)] for plane in planes]
         gw = {}
         y_ps = {}
@@ -363,15 +363,15 @@ def tile_list_modp_relu2_mix_gate_kernel(
             rectified(d, relu1)
             rectified_interleaved(d, relu0)
             square1 = squared(d, 1, relu1)
-            if d < LAST:
-                square0 = squared(d, 0, relu0)
-            if c == 0:
-                scaled = scale(d, square1)
+            square0 = tile([P, CHUNK * PACK], F32, f"square{d}_0")
+            ahead = (LAST - d) * BANK
+            if ahead:
+                nc.scalar.activation(square0[:, 0:ahead], relu0[:, 0:ahead], ACT.Square)
             down_products(c)
             copy_y(c, 0, laid_tile([P, CHUNK], F32, f"y{c}_0", H_AT[d]) if c > 0 else None)
             copy_y(c, 1)
-            if d == LAST:
-                square0 = squared(d, 0, relu0)
+            if c > 0:
+                nc.scalar.activation(square0[:, ahead:], relu0[:, ahead:], ACT.Square)
             if c > 0:
                 place(c - 1, 2)
                 gate(c - 1, 3, laid_tile([P, CHUNK], F32, f"z{c - 1}_3", H_AT[c] + KIB), gw3[c - 1][:])
@@ -385,8 +385,7 @@ def tile_list_modp_relu2_mix_gate_kernel(
                 place(c, i)
             h[d] = laid_tile([P, R_PASSES, CHUNK * PACK], BF16, f"h{d}", H_AT[d])
             times_pattern(nc.gpsimd, h[d][:, 0, :], square0[:], sm_run[:])
-            if c > 0:
-                scaled = scale(d, square1, 1 if d < LAST else 2)
+            scaled = scale(d, square1, 1 if d < LAST else 2)
             if d < LAST:
                 copy_y(c, 2)
             width = CHUNK * PACK // len(scaled)

@@ -1,7 +1,6 @@
 from contextlib import ExitStack
 
 import concourse.mybir as mybir
-from concourse.masks import make_identity
 
 K, R, N, T, J = 512, 1024, 512, 2048, 1024
 FLOPS = 2 * K * R * J + 2 * R * N * J
@@ -45,8 +44,10 @@ WGO_BANK = 6
 FIRST_BANKS = (0, 1, 4, 5)
 REGION = 9 * KIB
 HEAD_REGION = N_CHUNKS * REGION
+PAGES_AT = HEAD_REGION + 17 * KIB
+WU_AT = PAGES_AT + 16 * KIB
 EARLY = CHUNK + HALF
-H_AT = {1: 2 * KIB, 2: HEAD_REGION + 16 * KIB, 3: HEAD_REGION + 20 * KIB}
+H_AT = {0: HEAD_REGION + 14 * KIB, 1: 3 * KIB, 2: HEAD_REGION, 3: HEAD_REGION + 4 * KIB}
 
 
 def tile_list_modp_relu2_mix_gate_kernel(
@@ -82,7 +83,7 @@ def tile_list_modp_relu2_mix_gate_kernel(
         offsets = keep.tile([P, J // GROUP], U16, name="offsets")
         tab_w = tile([P, T], I32, "tab_w")
         tab_s = tile([P, T], U8, "tab_s")
-        wu_raw_w = [tile([P, PASS], I32, "wu_raw_w0"), laid_tile([P, PASS], I32, "wu_raw_w1", HEAD_REGION + 7 * KIB)]
+        wu_raw_w = [tile([P, PASS], I32, "wu_raw_w0"), laid_tile([P, PASS], I32, "wu_raw_w1", WU_AT + 2 * KIB)]
         wu_raw_s = tile([P, PASS], U8, "wu_raw_s")
         wu_w = [tile([P, PASS], I32, f"wu_w{g}") for g in range(R_PASSES)]
         wu_s = tile([P, PASS], U8, "wu_s")
@@ -95,7 +96,13 @@ def tile_list_modp_relu2_mix_gate_kernel(
         wgo_row = tile([P, WGO_RUN], F32, "wgo_row")
         nc.sync.dma_start(wgo_row[:], wgo[0].rearrange("(p i) -> p i", i=WGO_RUN))
         identity = tile([P, P], F32, "identity")
-        make_identity(nc, identity[:])
+        zeros = laid_tile([P, P], F32, "zeros", PAGES_AT + 8 * KIB - KIB // 4)
+        wd_s32 = tile([P, WD_PLANE_WORDS], I32, "wd_s32")
+        nc.vector.memset(wd_s32[:], 0)
+        nc.vector.memset(zeros[:], 0.0)
+        nc.gpsimd.affine_select(
+            out=identity[:], in_=zeros[:], compare_op=ALU.not_equal, fill=1.0, base=0, pattern=[[-1, P]], channel_multiplier=1
+        )
         for r in range(SCALE_ROWS):
             nc.sync.dma_start(tab_s[TAB_ROW + r : P : QUAD, :].bitcast(I32), tab_scales[0].bitcast(I32)[r::SCALE_ROWS, :])
         nc.sync.dma_start(tab_w[:], tab_words[0].rearrange("p t i -> p (t i)").bitcast(I32))
@@ -108,44 +115,41 @@ def tile_list_modp_relu2_mix_gate_kernel(
         for g in range(R_PASSES):
             nc.sync.dma_start(wu_raw_w[g][:], wu_words32[:, g * PASS : (g + 1) * PASS])
 
-        root = tile([P, R_PASSES * PACK], F32, "root")
-        for g in range(R_PASSES):
-            sm_abs = tile([P, PACK], F32, f"sm_abs{g}")
-            nc.scalar.activation(sm_abs[:], sm_sb[:, g, :], ACT.Abs)
-            nc.scalar.activation(root[:, g * PACK : (g + 1) * PACK], sm_abs[:], ACT.Sqrt)
+        sm_abs = tile([P, PACK], F32, "sm_abs")
+        nc.scalar.activation(sm_abs[:], sm_sb[:, 1, :], ACT.Abs)
+        root = tile([P, PACK], F32, "root")
+        nc.scalar.activation(root[:], sm_abs[:], ACT.Sqrt)
         sm_pass1 = tile([P, PACK], F32, "sm_pass1")
         nc.scalar.copy(sm_pass1[:], sm_sb[:, 1, :])
         sm_run = tile([P, RUN, PACK], F32, "sm_run")
         nc.scalar.copy(sm_run[:], sm_sb[:, 0, :].unsqueeze(1).to_broadcast([P, RUN, PACK]))
-        signs = tile([P, R_PASSES, RUN, PACK], BF16, "signs")
-        for g in range(R_PASSES):
-            nc.scalar.activation(signs[:, g], sm_sb[:, g, :].unsqueeze(1).to_broadcast([P, RUN, PACK]), ACT.Sign)
+        signs = tile([P, RUN, PACK], BF16, "signs")
+        nc.scalar.activation(signs[:], sm_sb[:, 1, :].unsqueeze(1).to_broadcast([P, RUN, PACK]), ACT.Sign)
 
         wgo_sb = tile([P, J], F32, "wgo_sb")
-        wgo_low = tile([P, J // 2], F32, "wgo_low")
-        wgo_first = laid_tile([P, 2 * CHUNK], F32, "wgo_first", KIB // 2)[:, 0:CHUNK]
+        wgo_first = {
+            1: laid_tile([P, CHUNK], F32, "wgo_first1", H_AT[0] + 3 * KIB // 2)[:, 0:HALF],
+            3: laid_tile([P, 3 * CHUNK], F32, "wgo_first3", KIB // 2)[:, 0 : 2 * CHUNK],
+        }
         for b in range(WGO_RUN // LINE):
             spread = bank([P, LINE, P], WGO_BANK + b, "spread")
             for k in range(LINE):
                 i = b * LINE + k
                 nc.tensor.transpose(spread[:, k, :], wgo_row[:, i : i + 1].to_broadcast([P, P]), identity[:])
-            nc.scalar.copy(
-                wgo_sb[:].rearrange("p (m i) -> p m i", i=WGO_RUN)[:, :, b * LINE : (b + 1) * LINE],
-                spread[:].rearrange("p k m -> p m k"),
-            )
-            nc.scalar.copy(
-                wgo_low[:].rearrange("p (m i) -> p m i", i=WGO_RUN)[:, :, b * LINE : (b + 1) * LINE],
-                spread[:, :, 0 : P // 2].rearrange("p k m -> p m k"),
-            )
-            nc.scalar.copy(
-                wgo_first.rearrange("p (m i) -> p m i", i=WGO_RUN)[:, :, b * LINE : (b + 1) * LINE],
-                spread[:, :, 0 : CHUNK // WGO_RUN].rearrange("p k m -> p m k"),
-            )
+            for dst in [wgo_sb[:]] + list(wgo_first.values()):
+                nc.scalar.copy(
+                    dst.rearrange("p (m i) -> p m i", i=WGO_RUN)[:, :, b * LINE : (b + 1) * LINE],
+                    spread[:, :, 0 : dst.shape[1] // WGO_RUN].rearrange("p k m -> p m k"),
+                )
 
-        pages = {0: tile([P, T], F32, "page0")}
-        nc.vector.memset(pages[0][:].bitcast(I32), 0)
-        wd_s32 = tile([P, WD_PLANE_WORDS], I32, "wd_s32")
-        nc.vector.memset(wd_s32[:], 0)
+        pages = {}
+
+        def clear(i, page):
+            pages[i] = page
+            nc.gpsimd.memset(page[:].bitcast(I32), 0)
+
+        for i in range(2):
+            clear(i, laid_tile([P, T], F32, f"page{i}", PAGES_AT + 8 * i * KIB))
 
         all_s = tile([P, J], U8, "all_s")
         nc.vector.tensor_copy(all_s[:], tab_s[:].indirect(offsets[:]))
@@ -164,15 +168,10 @@ def tile_list_modp_relu2_mix_gate_kernel(
             wu_w[1][:].rearrange("p (t m) -> p m t", t=PACK),
             wu_raw_w[1][:].rearrange("p (m t) -> p m t", t=PACK),
         )
-        rest_w = tile([P, J - EARLY], U32, "rest_w", on="wu_raw_w0")
+        rest_w = laid_tile([P, J - EARLY], U32, "rest_w", WU_AT)
         nc.vector.tensor_copy(rest_w[:], tab_w[:].bitcast(U32).indirect(offsets[:, EARLY // GROUP :]))
 
-        def clear(i, page):
-            pages[i] = page
-            nc.gpsimd.memset(page[:].bitcast(I32), 0)
-
-        clear(1, laid_tile([P, T], F32, "page1", HEAD_REGION + 8 * KIB))
-        clear(2, laid_tile([P, T], F32, "page2", HEAD_REGION))
+        clear(2, laid_tile([P, T], F32, "page2", WU_AT + 3 * KIB))
 
         gates = [tile([P, T], F32, f"gates{i}", on=name) for i, name in enumerate((None, None, "sm_sb"))]
         nc.sync.dma_start(gates[0][:], gT[0:P, :])
@@ -180,22 +179,20 @@ def tile_list_modp_relu2_mix_gate_kernel(
         for q in range(QUADRANTS):
             nc.sync.dma_start(wd_s32[scale_rows(q, first=1), :], wd8_scales[0].bitcast(I32)[blocks(q), :])
         nc.sync.dma_start(gates[2][:], gT[2 * P : 3 * P, :])
-        wd = tile([P, WD8_WORDS + WD4_WORDS], I32, "wd", on="tab_s")
-        wd8_w = wd[:, 0:WD8_WORDS]
+        wd8_w = tile([P, WD8_WORDS], I32, "wd8", on="tab_s")[:]
         nc.sync.dma_start(wd8_w, wd8_words[0].rearrange("p n i -> p (n i)").bitcast(I32))
-        nc.sync.dma_start(wd[:, WD8_WORDS:], wd4_words[0].bitcast(I32))
-        wd4_w = wd[:, WD8_WORDS:].bitcast(U8)
         for q in range(QUADRANTS):
             nc.sync.dma_start(wd_s32[scale_rows(q), :], wd4_scales[0].bitcast(I32)[blocks(q), :])
         wd_s = wd_s32[:].bitcast(U8)
 
-        h = {0: tile([P, R_PASSES, CHUNK * PACK], BF16, "h0", on="wgo_low")}
+        h = {}
         codes = {c: tile([P, R_PASSES * CHUNK], U32, f"h_w{c}") for c in range(1, N_CHUNKS)}
         planes = [tile([P, R_PASSES * CHUNK], U8, f"h_s{c}") for c in range(N_CHUNKS)]
         h_w = {c: [codes[c][:, tokens(g)] for g in range(R_PASSES)] for c in codes}
-        h_w[0] = [tile([P, CHUNK], U32, "h_w0_0")[:], laid_tile([P, CHUNK], U32, "h_w0_1", REGION + 3 * KIB)[:]]
+        h_w[0] = [laid_tile([P, CHUNK], U32, "h_w0_0", H_AT[0] + 2 * KIB)[:], laid_tile([P, CHUNK], U32, "h_w0_1", REGION + 3 * KIB)[:]]
         h_s = [[plane[:, tokens(g)] for g in range(R_PASSES)] for plane in planes]
         gw = {}
+        picked = {}
         y_ps = {}
         y = {}
         z = {}
@@ -227,20 +224,14 @@ def tile_list_modp_relu2_mix_gate_kernel(
                 func,
             )
 
-        def rectified_root(g, banks):
-            relu = tile([P, PACK, CHUNK], F32, f"relu0_{g}")
-            count = PACK // len(banks)
-            for b, index in enumerate(banks):
-                a = up_slices(0, g, b * count, count, index)
-                for k in range(count):
-                    col = g * PACK + b * count + k
-                    nc.scalar.activation(relu[:, b * count + k, :], a[:, k, :], ACT.Relu, scale=root[:, col : col + 1])
+        def rectified_root():
+            relu = tile([P, PACK, CHUNK], F32, "relu0_1")
+            for b in range(PACK // PAIR):
+                a = up_slices(0, 1, b * PAIR, PAIR, PAIR + b)
+                for k in range(PAIR):
+                    t = b * PAIR + k
+                    nc.scalar.activation(relu[:, t, :], a[:, k, :], ACT.Relu, scale=root[:, t : t + 1])
             return relu
-
-        def square_and_round(g, relu):
-            h_abs = tile([P, CHUNK * PACK], BF16, f"h_abs0_{g}")
-            interleave(h_abs[:], relu[:], ACT.Square)
-            return h_abs
 
         def times_pattern(engine, dst, src, pattern):
             run = RUN * PACK
@@ -274,15 +265,13 @@ def tile_list_modp_relu2_mix_gate_kernel(
             nc.scalar.activation(square[:], relu[:], ACT.Square)
             return square
 
-        def scale(c, square, pieces=1):
-            width = CHUNK // pieces
-            scaled = laid_tile([P, pieces, PACK, width], F32, f"scaled{c}", c * REGION + 3 * KIB)
-            for k in range(pieces):
-                for t in range(PACK):
-                    nc.scalar.activation(
-                        scaled[:, k, t, :], square[:, t, k * width : (k + 1) * width], ACT.Copy, scale=sm_pass1[:, t : t + 1]
-                    )
-            return [scaled[:, k] for k in range(pieces)]
+        def scale(square, first, scaled):
+            width = scaled.shape[2]
+            for t in range(PACK):
+                nc.scalar.activation(
+                    scaled[:, t, :], square[:, t, first : first + width], ACT.Copy, scale=sm_pass1[:, t : t + 1]
+                )
+            return scaled
 
         def quantise(c):
             nc.vector.quantize_mx(
@@ -337,24 +326,89 @@ def tile_list_modp_relu2_mix_gate_kernel(
             if first + count == N_CHUNKS:
                 nc.sync.dma_start(out[i * P : (i + 1) * P, :], pages[i][:])
 
-        gw[0] = tile([P, J], F32, "gw0")
-        nc.vector.tensor_tensor(gw[0][:], gates[0][:].indirect(offsets[:]), wgo_sb[:], ALU.mult)
-        gw[1] = tile([P, J], F32, "gw1")
-        nc.vector.tensor_tensor(gw[1][:, tokens(0, 2)], gates[1][:].indirect(listed(0, 2)), wgo_low[:], ALU.mult)
-        nc.vector.tensor_tensor(gw[1][:, tokens(2, 2)], gates[1][:].indirect(listed(2, 2)), wgo_sb[:, tokens(2, 2)], ALU.mult)
-        times_pattern(nc.vector, h[0][:, 0, :], square_and_round(0, rectified_root(0, FIRST_BANKS))[:], signs[:, 0])
+        def gather_weighted(i, first, count, weights=None, on=None):
+            dst = tile([P, count * CHUNK], F32, f"gw{i}_{first}", on=on)
+            weights = wgo_sb[:, tokens(first, count)] if weights is None else weights
+            nc.vector.tensor_tensor(dst[:], gates[i][:].indirect(listed(first, count)), weights, ALU.mult)
+            for c in range(count):
+                gw[first + c, i] = dst[:, tokens(c)]
+
+        def gather_plain(i, first, dst):
+            picked[i] = dst
+            nc.vector.tensor_copy(dst, gates[i][:].indirect(listed(first, N_CHUNKS - first)))
+
+        def weigh(parts, values, dst):
+            first = parts[0][0]
+            weights = wgo_sb[:, tokens(first, len(parts))].rearrange("p (c j) -> p c j", j=CHUNK)
+            nc.gpsimd.tensor_tensor(dst[:], values, weights, ALU.mult)
+            for k, part in enumerate(parts):
+                gw[part] = dst[:, k, :]
+
+        def token_major(c, i, banks, flat=None):
+            sums = [bank([P, P], index, "sums") for index in banks]
+            if flat is None:
+                flat = tile([P, CHUNK // HALF, P], F32, f"flat{c}_{i}")
+            for b in range(CHUNK // HALF):
+                columns = slice(b * HALF, (b + 1) * HALF)
+                nc.tensor.matmul_mx(
+                    out=sums[b][:],
+                    lhsT=h_w[c][0][:, columns].bitcast(FP8X4),
+                    lhsT_scale=h_s[c][0][:, columns],
+                    rhs=wd8_w[:, i * P : (i + 1) * P].bitcast(FP8X4),
+                    rhs_scale=wd_s[SCALE_ROWS:P, i * P : (i + 1) * P],
+                    start=True,
+                    stop=False,
+                )
+                nc.tensor.matmul_mx(
+                    out=sums[b][:],
+                    lhsT=h_w[c][1][:, columns].bitcast(FP8X4),
+                    lhsT_scale=h_s[c][1][:, columns],
+                    rhs=wd4_w[:, 2 * i * P : 2 * (i + 1) * P].bitcast(FP4X4),
+                    rhs_scale=wd_s[:, i * P : (i + 1) * P],
+                    start=False,
+                    stop=True,
+                )
+                k = (c - 2) * (CHUNK // HALF) + b
+                nc.scalar.activation(flat[:, b, :], sums[b][:], ACT.Copy, scale=wgo_column[:, k : k + 1])
+            return flat
+
+        def turn_back(flat, index, dst):
+            back = bank([P, CHUNK // HALF, HALF], index, "back")
+            for b in range(CHUNK // HALF):
+                nc.tensor.transpose(back[:, b, :], flat[:, b, :], identity[:])
+            nc.scalar.copy(dst, back[:].rearrange("p b j -> p (b j)"))
+
+        early_flat = tile([P, J], F32, "early")
+        early = early_flat[:].rearrange("p (c j) -> p c j", j=CHUNK)
+        gather_weighted(0, 0, 3)
+        gather_plain(0, 3, early_flat[:, tokens(3)])
+        gather_plain(1, 1, early_flat[:, tokens(0, 3)])
+        gw[0, 1] = tile([P, CHUNK], F32, "gw1_0")[:]
+        for k, weights in enumerate((wgo_first[1], wgo_sb[:, HALF:CHUNK])):
+            entries = offsets[:, k * HALF // GROUP : (k + 1) * HALF // GROUP]
+            nc.vector.tensor_tensor(gw[0, 1][:, k * HALF : (k + 1) * HALF], gates[1][:].indirect(entries), weights, ALU.mult)
+        h0 = [tile([P, CHUNK * PACK], BF16, "h0_0"), laid_tile([P, CHUNK * PACK], BF16, "h0_1", H_AT[0])]
+        relu0 = tile([P, PACK, CHUNK], F32, "relu0_0")
+        for t, index in enumerate(FIRST_BANKS):
+            nc.scalar.activation(relu0[:, t : t + 1, :], up_slices(0, 0, t, 1, index)[:], ACT.Relu)
+        square0 = tile([P, CHUNK * PACK], F32, "square0_0")
+        interleave(square0[:], relu0[:], ACT.Square)
+        times_pattern(nc.gpsimd, h0[0][:], square0[:], sm_run[:])
         gates.append(tile([P, T], F32, "gates3", on="relu0_0"))
         nc.sync.dma_start(gates[3][:], gT[3 * P : 4 * P, :])
-        times_pattern(nc.vector, h[0][:, 1, :], square_and_round(1, rectified_root(1, (2, 3)))[:], signs[:, 1])
+        h_abs = tile([P, CHUNK * PACK], BF16, "h_abs")
+        interleave(h_abs[:], rectified_root()[:], ACT.Square)
+        wd4 = tile([P, WD4_WORDS], I32, "wd4", on="relu0_1")
+        nc.sync.dma_start(wd4[:], wd4_words[0].bitcast(I32))
+        wd4_w = wd4[:].bitcast(U8)
+        times_pattern(nc.vector, h0[1][:], h_abs[:], signs[:])
         for g in range(R_PASSES):
-            nc.vector.quantize_mx(out=h_w[0][g].bitcast(FP8X4), scales=h_s[0][g], in_=h[0][:, g, :])
-        gw[2] = tile([P, J], F32, "gw2", on="h_abs0_1")
-        nc.vector.tensor_tensor(gw[2][:], gates[2][:].indirect(offsets[:]), wgo_sb[:], ALU.mult)
-        clear(3, tile([P, T], F32, "page3", on="wgo_low"))
-        gw3 = {0: tile([P, CHUNK], F32, "gw3_0")}
-        nc.vector.tensor_tensor(gw3[0][:], gates[3][:].indirect(listed(0)), wgo_first, ALU.mult)
-        picked3 = tile([P, J - CHUNK], F32, "picked3")
-        nc.vector.tensor_copy(picked3[:], gates[3][:].indirect(listed(1, LAST)))
+            nc.vector.quantize_mx(out=h_w[0][g].bitcast(FP8X4), scales=h_s[0][g], in_=h0[g][:])
+        gather_weighted(2, 0, 3, on="h_abs")
+        clear(3, laid_tile([P, T], F32, "page3", H_AT[0] - 6 * KIB))
+        gather_weighted(3, 0, 2, wgo_first[3])
+        gather_plain(3, 2, tile([P, 2 * CHUNK], F32, "picked3")[:])
+        gather_plain(2, 3, laid_tile([P, CHUNK], F32, "picked2", 2 * KIB)[:])
 
         relu0 = tile([P, CHUNK * PACK], F32, "relu1_0")
         relu1 = tile([P, PACK, CHUNK], F32, "relu1_1")
@@ -367,49 +421,65 @@ def tile_list_modp_relu2_mix_gate_kernel(
             ahead = (LAST - d) * BANK
             if ahead:
                 nc.scalar.activation(square0[:, 0:ahead], relu0[:, 0:ahead], ACT.Square)
-            down_products(c)
-            copy_y(c, 0, laid_tile([P, CHUNK], F32, f"y{c}_0", H_AT[d]) if c > 0 else None)
+            if c == 0:
+                scaled = [scale(square1, 0, tile([P, PACK, HALF], F32, "scaled1_0"))]
+            down_products(c, N_PAGES if d < LAST else N_PAGES - 1)
+            copy_y(c, 0, laid_tile([P, CHUNK], F32, f"y{c}_0", H_AT[d] + KIB))
             copy_y(c, 1)
             if c > 0:
                 nc.scalar.activation(square0[:, ahead:], relu0[:, ahead:], ACT.Square)
             if c > 0:
                 place(c - 1, 2)
-                gate(c - 1, 3, laid_tile([P, CHUNK], F32, f"z{c - 1}_3", H_AT[c] + KIB), gw3[c - 1][:])
+                gate(c - 1, 3, laid_tile([P, CHUNK], F32, f"z{c - 1}_3", H_AT[c] + KIB), gw[c - 1, 3])
                 place(c - 1, 3)
-                count = 1 if d < LAST else 2
-                gw3[c] = laid_tile([P, count * CHUNK], F32, f"gw3_{c}", H_AT[c] + 2 * KIB)
-                nc.gpsimd.tensor_tensor(gw3[c][:], picked3[:, tokens(c - 1, count)], wgo_sb[:, tokens(c, count)], ALU.mult)
+                parts, values = ([(1, 1)], early[:, 0:1, :]) if c == 1 else ([(2, 1), (3, 0)], early[:, 1::2, :])
+                weigh(parts, values, laid_tile([P, c, CHUNK], F32, f"weighed{c}", H_AT[c] + 2 * KIB))
             for i in range(2):
                 dst = tile([P, CHUNK], F32, f"z{c}_{i}") if c > 0 else laid_tile([P, CHUNK], F32, f"z0_{i}", i * KIB)
-                gate(c, i, dst, gw[i][:, tokens(c)])
+                gate(c, i, dst, gw[c, i])
                 place(c, i)
             h[d] = laid_tile([P, R_PASSES, CHUNK * PACK], BF16, f"h{d}", H_AT[d])
             times_pattern(nc.gpsimd, h[d][:, 0, :], square0[:], sm_run[:])
-            scaled = scale(d, square1, 1 if d < LAST else 2)
+            at = d * REGION + 3 * KIB
+            if c == 0:
+                scaled.append(scale(square1, HALF, laid_tile([P, PACK, HALF], F32, "scaled1_1", at + KIB // 2)))
+            elif d < LAST:
+                scaled = [scale(square1, 0, laid_tile([P, PACK, CHUNK], F32, f"scaled{d}", at))]
+            else:
+                both = laid_tile([P, 2, PACK, HALF], F32, f"scaled{d}", at)
+                scaled = [scale(square1, k * HALF, both[:, k]) for k in range(2)]
             if d < LAST:
                 copy_y(c, 2)
             width = CHUNK * PACK // len(scaled)
             for k, piece in enumerate(scaled):
-                interleave(h[d][:, 1, k * width : (k + 1) * width], piece, ACT.Copy)
+                interleave(h[d][:, 1, k * width : (k + 1) * width], piece[:], ACT.Copy)
             if d < LAST:
                 copy_y(c, 3)
             quantise(d)
             behind = laid_tile([P, CHUNK], F32, f"behind{d}", d * REGION + 4 * KIB)
             if d < LAST:
-                gate(c, 2, behind, gw[2][:, tokens(c)])
+                gate(c, 2, behind, gw[c, 2])
                 relu0 = laid_tile([P, CHUNK * PACK], F32, f"relu{d + 1}_0", d * REGION)
                 relu1 = laid_tile([P, PACK, CHUNK], F32, f"relu{d + 1}_1", d * REGION + 5 * KIB)
             else:
                 copy_y(c, 2, behind)
-                scatter(c, 1, 2, behind[:], gw[2][:, tokens(c)])
+                scatter(c, 1, 2, behind[:], gw[c, 2])
 
-        down_products(LAST, N_PAGES - 1)
-        for i in range(N_PAGES - 1):
-            copy_y(LAST, i)
-            scatter(LAST, 1, i, y[LAST, i][:], gw[i][:, tokens(LAST)])
-        both = y_ps[LAST - 1, N_PAGES - 1]
-        down8(both[:, CHUNK:], LAST, N_PAGES - 1)
-        down4(both[:, CHUNK:], LAST, N_PAGES - 1)
-        y_both = tile([P, BANK], F32, "y_both")
-        nc.scalar.copy(y_both[:], both[:])
-        scatter(LAST - 1, 2, N_PAGES - 1, y_both[:], gw3[LAST - 1][:])
+        y_both = tile([P, 2 * CHUNK], F32, "y_both")
+        turned = bank([P, LINE, P], 0, "turned")
+        for b in range(LINE):
+            nc.tensor.transpose(turned[:, b, :], wgo_sb[:, J // 2 + b * P : J // 2 + (b + 1) * P], identity[:])
+        wgo_column = laid_tile([P, LINE], F32, "wgo_column", LAST * REGION + 6 * KIB)
+        nc.scalar.copy(wgo_column[:], turned[:, :, 0])
+        waiting = token_major(LAST - 1, 3, (7, 3), laid_tile([P, 2, P], F32, "flat2_3", LAST * REGION + 5 * KIB))
+        down_products(LAST, 1)
+        copy_y(LAST, 0)
+        scatter(LAST, 1, 0, y[LAST, 0][:], gw[LAST, 0])
+        weighted = [tile([P, CHUNK], F32, f"weighted{i}") for i in range(2)]
+        turn_back(token_major(LAST, 1, (0, 1)), 2, weighted[0][:])
+        scatter(LAST, 1, 1, weighted[0][:], picked[1][:, tokens(2)])
+        turn_back(token_major(LAST, 2, (5, 6)), 0, weighted[1][:])
+        scatter(LAST, 1, 2, weighted[1][:], picked[2])
+        turn_back(waiting, 2, y_both[:, tokens(0)])
+        turn_back(token_major(LAST, 3, (2, 0)), 1, y_both[:, tokens(1)])
+        scatter(LAST - 1, 2, 3, y_both[:], picked[3])

@@ -60,10 +60,10 @@ def tile_list_modp_relu2_mix_gate_kernel(
         psum = ctx.enter_context(tc.psum_pool(name="psum", bufs=1))
 
         def laid_tile(shape, dtype, name, offset):
-            return laid.tile(shape, dtype, name=name, align_bytes=64, offset=offset)
+            return laid.tile(shape, dtype, name=name, align_bytes=256, offset=offset)
 
         def tile(shape, dtype, name, on=None):
-            return keep.tile(shape, dtype, name=name, tag=on or name, align_bytes=64)
+            return keep.tile(shape, dtype, name=name, tag=on or name, align_bytes=256)
 
         def bank(shape, index, name):
             return psum.tile(shape, F32, name=name, tag=f"bank{index}")

from contextlib import ExitStack

import concourse.mybir as mybir

K, R, N, T, J = 512, 1024, 512, 2048, 1024
FLOPS = 2 * K * R * J + 2 * R * N * J

F32 = mybir.dt.float32
BF16 = mybir.dt.bfloat16
I32 = mybir.dt.int32
U32 = mybir.dt.uint32
U16 = mybir.dt.uint16
U8 = mybir.dt.uint8
FP8X4 = mybir.dt.float8_e4m3fn_x4
FP4X4 = mybir.dt.float4_e2m1fn_x4
ALU = mybir.AluOpType
ACT = mybir.ActivationFunctionType

P = 128
PACK = 4
PASS = P * PACK
QUADRANTS = 4
QUAD = P // QUADRANTS
SCALE_ROWS = 4
TAB_ROW = 12
GROUP = 16
CHUNK = 256
HALF = CHUNK // 2
COLS = CHUNK // GROUP
BANK = 512
PAIR = BANK // CHUNK
N_CHUNKS = J // CHUNK
LAST = N_CHUNKS - 1
N_PAGES = N // P
R_PASSES = R // PASS
LINE = 4
RUN = 16
WD8_WORDS = N
WD4_WORDS = N // 2
WD_PLANE_WORDS = N // 4
WGO_RUN = J // P
KIB = 1024
WGO_BANK = 6
FIRST_BANKS = (0, 1, 4, 5)
REGION = 9 * KIB
HEAD_REGION = N_CHUNKS * REGION
PAGES_AT = HEAD_REGION + 17 * KIB
WU_AT = PAGES_AT + 16 * KIB
EARLY = CHUNK + HALF
H_AT = {0: HEAD_REGION + 14 * KIB, 1: 3 * KIB, 2: HEAD_REGION, 3: HEAD_REGION + 4 * KIB}


def tile_list_modp_relu2_mix_gate_kernel(
    tc, tab_words, tab_scales, wu_words, wu_scales, sm, wd8_words, wd8_scales, wd4_words, wd4_scales, gT, wgo, offs, out
):
    nc = tc.nc
    with ExitStack() as ctx:
        keep = ctx.enter_context(tc.tile_pool(name="keep", bufs=1))
        laid = ctx.enter_context(tc.tile_pool(name="laid", bufs=1))
        psum = ctx.enter_context(tc.psum_pool(name="psum", bufs=1))

        def laid_tile(shape, dtype, name, offset):
            return laid.tile(shape, dtype, name=name, align_bytes=256, offset=offset)

        def tile(shape, dtype, name, on=None):
            return keep.tile(shape, dtype, name=name, tag=on or name, align_bytes=256)

        def bank(shape, index, name):
            return psum.tile(shape, F32, name=name, tag=f"bank{index}")

        def scale_rows(q, first=0, planes=1):
            return slice(QUAD * q + SCALE_ROWS * first, QUAD * q + SCALE_ROWS * (first + planes))

        def blocks(q):
            return slice(SCALE_ROWS * q, SCALE_ROWS * (q + 1))

        def listed(first, count=1):
            return offsets[:, first * COLS : (first + count) * COLS]

        def tokens(first, count=1):
            return slice(first * CHUNK, (first + count) * CHUNK)

        offsets = keep.tile([P, J // GROUP], U16, name="offsets")
        tab_w = tile([P, T], I32, "tab_w")
        tab_s = tile([P, T], U8, "tab_s")
        wu_raw_w = [tile([P, PASS], I32, "wu_raw_w0"), laid_tile([P, PASS], I32, "wu_raw_w1", WU_AT + 2 * KIB)]
        wu_raw_s = tile([P, PASS], U8, "wu_raw_s")
        wu_w = [tile([P, PASS], I32, f"wu_w{g}") for g in range(R_PASSES)]
        wu_s = tile([P, PASS], U8, "wu_s")
        sm_sb = tile([P, R_PASSES, 2 * PACK], F32, "sm_sb")[:, :, 0:PACK]

        nc.vector.memset(tab_s[:].bitcast(I32), 0)
        nc.vector.memset(wu_raw_s[:].bitcast(I32), 0)
        nc.sync.dma_start(offsets[:], offs)
        nc.sync.dma_start(sm_sb, sm.rearrange("(g p t) -> p g t", g=R_PASSES, t=PACK))
        wgo_row = tile([P, WGO_RUN], F32, "wgo_row")
        nc.sync.dma_start(wgo_row[:], wgo[0].rearrange("(p i) -> p i", i=WGO_RUN))
        identity = tile([P, P], F32, "identity")
        zeros = laid_tile([P, P], F32, "zeros", PAGES_AT + 8 * KIB - KIB // 4)
        wd_s32 = tile([P, WD_PLANE_WORDS], I32, "wd_s32")
        nc.vector.memset(wd_s32[:], 0)
        nc.vector.memset(zeros[:], 0.0)
        nc.gpsimd.affine_select(
            out=identity[:], in_=zeros[:], compare_op=ALU.not_equal, fill=1.0, base=0, pattern=[[-1, P]], channel_multiplier=1
        )
        for r in range(SCALE_ROWS):
            nc.sync.dma_start(tab_s[TAB_ROW + r : P : QUAD, :].bitcast(I32), tab_scales[0].bitcast(I32)[r::SCALE_ROWS, :])
        nc.sync.dma_start(tab_w[:], tab_words[0].rearrange("p t i -> p (t i)").bitcast(I32))
        for q in range(QUADRANTS):
            nc.sync.dma_start(
                wu_raw_s[scale_rows(q, planes=R_PASSES), :].bitcast(I32),
                wu_scales[0].bitcast(I32)[blocks(q), :].rearrange("q (g c) -> g q c", g=R_PASSES),
            )
        wu_words32 = wu_words[0].rearrange("p r i -> p (r i)").bitcast(I32)
        for g in range(R_PASSES):
            nc.sync.dma_start(wu_raw_w[g][:], wu_words32[:, g * PASS : (g + 1) * PASS])

        sm_abs = tile([P, PACK], F32, "sm_abs")
        nc.scalar.activation(sm_abs[:], sm_sb[:, 1, :], ACT.Abs)
        root = tile([P, PACK], F32, "root")
        nc.scalar.activation(root[:], sm_abs[:], ACT.Sqrt)
        sm_pass1 = tile([P, PACK], F32, "sm_pass1")
        nc.scalar.copy(sm_pass1[:], sm_sb[:, 1, :])
        sm_run = tile([P, RUN, PACK], F32, "sm_run")
        nc.scalar.copy(sm_run[:], sm_sb[:, 0, :].unsqueeze(1).to_broadcast([P, RUN, PACK]))
        signs = tile([P, RUN, PACK], BF16, "signs")
        nc.scalar.activation(signs[:], sm_sb[:, 1, :].unsqueeze(1).to_broadcast([P, RUN, PACK]), ACT.Sign)

        wgo_sb = tile([P, J], F32, "wgo_sb")
        wgo_first = {
            1: laid_tile([P, CHUNK], F32, "wgo_first1", H_AT[0] + 3 * KIB // 2)[:, 0:HALF],
            3: laid_tile([P, 3 * CHUNK], F32, "wgo_first3", KIB // 2)[:, 0 : 2 * CHUNK],
        }
        for b in range(WGO_RUN // LINE):
            spread = bank([P, LINE, P], WGO_BANK + b, "spread")
            for k in range(LINE):
                i = b * LINE + k
                nc.tensor.transpose(spread[:, k, :], wgo_row[:, i : i + 1].to_broadcast([P, P]), identity[:])
            for dst in [wgo_sb[:]] + list(wgo_first.values()):
                nc.scalar.copy(
                    dst.rearrange("p (m i) -> p m i", i=WGO_RUN)[:, :, b * LINE : (b + 1) * LINE],
                    spread[:, :, 0 : dst.shape[1] // WGO_RUN].rearrange("p k m -> p m k"),
                )

        pages = {}

        def clear(i, page):
            pages[i] = page
            nc.gpsimd.memset(page[:].bitcast(I32), 0)

        for i in range(2):
            clear(i, laid_tile([P, T], F32, f"page{i}", PAGES_AT + 8 * i * KIB))

        all_s = tile([P, J], U8, "all_s")
        nc.vector.tensor_copy(all_s[:], tab_s[:].indirect(offsets[:]))
        first_w = tile([P, EARLY], U32, "first_w")
        nc.vector.tensor_copy(first_w[:], tab_w[:].bitcast(U32).indirect(offsets[:, 0 : EARLY // GROUP]))
        nc.vector.tensor_copy(
            wu_s[:].rearrange("p (t m) -> p m t", t=PACK),
            wu_raw_s[:].rearrange("p (m t) -> p m t", t=PACK),
        )
        for first in range(0, PACK, PAIR):
            nc.scalar.copy(
                wu_w[0][:].bitcast(U32).rearrange("p (t m) -> p m t", t=PACK)[:, :, first : first + PAIR],
                wu_raw_w[0][:].bitcast(U32).rearrange("p (m t) -> p m t", t=PACK)[:, :, first : first + PAIR],
            )
        nc.vector.tensor_copy(
            wu_w[1][:].rearrange("p (t m) -> p m t", t=PACK),
            wu_raw_w[1][:].rearrange("p (m t) -> p m t", t=PACK),
        )
        rest_w = laid_tile([P, J - EARLY], U32, "rest_w", WU_AT)
        nc.vector.tensor_copy(rest_w[:], tab_w[:].bitcast(U32).indirect(offsets[:, EARLY // GROUP :]))

        clear(2, laid_tile([P, T], F32, "page2", WU_AT + 3 * KIB))

        gates = [tile([P, T], F32, f"gates{i}", on=name) for i, name in enumerate((None, None, "sm_sb"))]
        nc.sync.dma_start(gates[0][:], gT[0:P, :])
        nc.sync.dma_start(gates[1][:], gT[P : 2 * P, :])
        for q in range(QUADRANTS):
            nc.sync.dma_start(wd_s32[scale_rows(q, first=1), :], wd8_scales[0].bitcast(I32)[blocks(q), :])
        nc.sync.dma_start(gates[2][:], gT[2 * P : 3 * P, :])
        wd8_w = tile([P, WD8_WORDS], I32, "wd8", on="tab_s")[:]
        nc.sync.dma_start(wd8_w, wd8_words[0].rearrange("p n i -> p (n i)").bitcast(I32))
        for q in range(QUADRANTS):
            nc.sync.dma_start(wd_s32[scale_rows(q), :], wd4_scales[0].bitcast(I32)[blocks(q), :])
        wd_s = wd_s32[:].bitcast(U8)

        h = {}
        codes = {c: tile([P, R_PASSES * CHUNK], U32, f"h_w{c}") for c in range(1, N_CHUNKS)}
        planes = [tile([P, R_PASSES * CHUNK], U8, f"h_s{c}") for c in range(N_CHUNKS)]
        h_w = {c: [codes[c][:, tokens(g)] for g in range(R_PASSES)] for c in codes}
        h_w[0] = [laid_tile([P, CHUNK], U32, "h_w0_0", H_AT[0] + 2 * KIB)[:], laid_tile([P, CHUNK], U32, "h_w0_1", REGION + 3 * KIB)[:]]
        h_s = [[plane[:, tokens(g)] for g in range(R_PASSES)] for plane in planes]
        gw = {}
        picked = {}
        y_ps = {}
        y = {}
        z = {}

        def up(a, g, t, first, count):
            words = first_w[:, first : first + count] if first < EARLY else rest_w[:, first - EARLY : first - EARLY + count]
            nc.tensor.matmul_mx(
                out=a,
                lhsT=wu_w[g][:, t * P : (t + 1) * P].bitcast(FP8X4),
                lhsT_scale=wu_s[SCALE_ROWS * g : P, t * P : (t + 1) * P],
                rhs=words.bitcast(FP8X4),
                rhs_scale=all_s[TAB_ROW:P, first : first + count],
                start=True,
                stop=True,
            )

        def up_slices(c, g, first, count, index):
            a = bank([P, count, CHUNK], index, "a")
            width = HALF if c * CHUNK < EARLY < (c + 1) * CHUNK else CHUNK
            for k in range(count):
                for at in range(0, CHUNK, width):
                    up(a[:, k, at : at + width], g, first + k, c * CHUNK + at, width)
            return a

        def interleave(dst, src, func):
            nc.scalar.activation(
                dst.rearrange("p (c i t) -> p c t i", i=LINE, t=PACK),
                src.rearrange("p t (c i) -> p c t i", i=LINE),
                func,
            )

        def rectified_root():
            relu = tile([P, PACK, CHUNK], F32, "relu0_1")
            for b in range(PACK // PAIR):
                a = up_slices(0, 1, b * PAIR, PAIR, PAIR + b)
                for k in range(PAIR):
                    t = b * PAIR + k
                    nc.scalar.activation(relu[:, t, :], a[:, k, :], ACT.Relu, scale=root[:, t : t + 1])
            return relu

        def times_pattern(engine, dst, src, pattern):
            run = RUN * PACK
            engine.tensor_tensor(
                dst.rearrange("p (a b) -> p a b", b=run),
                src.rearrange("p (a b) -> p a b", b=run),
                pattern.rearrange("p j t -> p (j t)").unsqueeze(1).to_broadcast([P, CHUNK // RUN, run]),
                ALU.mult,
            )

        def rectified_interleaved(c, relu):
            for b in range(CHUNK // HALF):
                a = bank([P, PACK, HALF], b, "a")
                for t in range(PACK):
                    up(a[:, t, :], 0, t, c * CHUNK + b * HALF, HALF)
                nc.scalar.activation(
                    relu[:, b * BANK : (b + 1) * BANK].rearrange("p (j t) -> p j t", t=PACK),
                    a[:].rearrange("p t j -> p j t"),
                    ACT.Relu,
                )
            return relu

        def rectified(c, relu):
            for b in range(PACK // PAIR):
                a = up_slices(c, 1, b * PAIR, PAIR, PAIR + b)
                nc.scalar.activation(relu[:, b * PAIR : (b + 1) * PAIR, :], a[:], ACT.Relu)
            return relu

        def squared(c, g, relu):
            square = tile(relu.shape, F32, f"square{c}_{g}")
            nc.scalar.activation(square[:], relu[:], ACT.Square)
            return square

        def scale(square, first, scaled):
            width = scaled.shape[2]
            for t in range(PACK):
                nc.scalar.activation(
                    scaled[:, t, :], square[:, t, first : first + width], ACT.Copy, scale=sm_pass1[:, t : t + 1]
                )
            return scaled

        def quantise(c):
            nc.vector.quantize_mx(
                out=codes[c][:].bitcast(FP8X4), scales=planes[c][:], in_=h[c][:].rearrange("p g x -> p (g x)")
            )

        def down8(dst, c, i):
            nc.tensor.matmul_mx(
                out=dst,
                lhsT=wd8_w[:, i * P : (i + 1) * P].bitcast(FP8X4),
                lhsT_scale=wd_s[SCALE_ROWS:P, i * P : (i + 1) * P],
                rhs=h_w[c][0].bitcast(FP8X4),
                rhs_scale=h_s[c][0],
                start=True,
                stop=False,
            )

        def down4(dst, c, i):
            nc.tensor.matmul_mx(
                out=dst,
                lhsT=wd4_w[:, 2 * i * P : 2 * (i + 1) * P].bitcast(FP4X4),
                lhsT_scale=wd_s[:, i * P : (i + 1) * P],
                rhs=h_w[c][1].bitcast(FP8X4),
                rhs_scale=h_s[c][1],
                start=False,
                stop=True,
            )

        def down_products(c, count=N_PAGES):
            for i in range(count):
                y_ps[c, i] = bank([P, BANK], N_PAGES + i, "y_ps")
                down8(y_ps[c, i][:, 0:CHUNK], c, i)
                if c > 0:
                    down4(y_ps[c, i][:, 0:CHUNK], c, i)
            if c == 0:
                for i in range(count):
                    down4(y_ps[c, i][:, 0:CHUNK], c, i)

        def copy_y(c, i, dst=None):
            y[c, i] = dst if dst is not None else tile([P, CHUNK], F32, f"y{c}_{i}")
            nc.scalar.copy(y[c, i][:], y_ps[c, i][:, 0:CHUNK])

        def gate(c, i, dst, weights):
            z[c, i] = dst
            nc.gpsimd.tensor_tensor(dst[:], y[c, i][:], weights, ALU.mult)

        def place(c, i):
            nc.vector.tensor_copy(pages[i][:].indirect(listed(c)), z[c, i][:])

        def scatter(first, count, i, values, weights):
            nc.vector.tensor_tensor(pages[i][:].indirect(listed(first, count)), values, weights, ALU.mult)
            if first + count == N_CHUNKS:
                nc.sync.dma_start(out[i * P : (i + 1) * P, :], pages[i][:])

        def gather_weighted(i, first, count, weights=None, on=None):
            dst = tile([P, count * CHUNK], F32, f"gw{i}_{first}", on=on)
            weights = wgo_sb[:, tokens(first, count)] if weights is None else weights
            nc.vector.tensor_tensor(dst[:], gates[i][:].indirect(listed(first, count)), weights, ALU.mult)
            for c in range(count):
                gw[first + c, i] = dst[:, tokens(c)]

        def gather_plain(i, first, dst):
            picked[i] = dst
            nc.vector.tensor_copy(dst, gates[i][:].indirect(listed(first, N_CHUNKS - first)))

        def weigh(parts, values, dst):
            first = parts[0][0]
            weights = wgo_sb[:, tokens(first, len(parts))].rearrange("p (c j) -> p c j", j=CHUNK)
            nc.gpsimd.tensor_tensor(dst[:], values, weights, ALU.mult)
            for k, part in enumerate(parts):
                gw[part] = dst[:, k, :]

        def token_major(c, i, banks, flat=None):
            sums = [bank([P, P], index, "sums") for index in banks]
            if flat is None:
                flat = tile([P, CHUNK // HALF, P], F32, f"flat{c}_{i}")
            for b in range(CHUNK // HALF):
                columns = slice(b * HALF, (b + 1) * HALF)
                nc.tensor.matmul_mx(
                    out=sums[b][:],
                    lhsT=h_w[c][0][:, columns].bitcast(FP8X4),
                    lhsT_scale=h_s[c][0][:, columns],
                    rhs=wd8_w[:, i * P : (i + 1) * P].bitcast(FP8X4),
                    rhs_scale=wd_s[SCALE_ROWS:P, i * P : (i + 1) * P],
                    start=True,
                    stop=False,
                )
                nc.tensor.matmul_mx(
                    out=sums[b][:],
                    lhsT=h_w[c][1][:, columns].bitcast(FP8X4),
                    lhsT_scale=h_s[c][1][:, columns],
                    rhs=wd4_w[:, 2 * i * P : 2 * (i + 1) * P].bitcast(FP4X4),
                    rhs_scale=wd_s[:, i * P : (i + 1) * P],
                    start=False,
                    stop=True,
                )
                k = (c - 2) * (CHUNK // HALF) + b
                nc.scalar.activation(flat[:, b, :], sums[b][:], ACT.Copy, scale=wgo_column[:, k : k + 1])
            return flat

        def turn_back(flat, index, dst):
            back = bank([P, CHUNK // HALF, HALF], index, "back")
            for b in range(CHUNK // HALF):
                nc.tensor.transpose(back[:, b, :], flat[:, b, :], identity[:])
            nc.scalar.copy(dst, back[:].rearrange("p b j -> p (b j)"))

        early_flat = tile([P, J], F32, "early")
        early = early_flat[:].rearrange("p (c j) -> p c j", j=CHUNK)
        gather_weighted(0, 0, 3)
        gather_plain(0, 3, early_flat[:, tokens(3)])
        gather_plain(1, 1, early_flat[:, tokens(0, 3)])
        gw[0, 1] = tile([P, CHUNK], F32, "gw1_0")[:]
        for k, weights in enumerate((wgo_first[1], wgo_sb[:, HALF:CHUNK])):
            entries = offsets[:, k * HALF // GROUP : (k + 1) * HALF // GROUP]
            nc.vector.tensor_tensor(gw[0, 1][:, k * HALF : (k + 1) * HALF], gates[1][:].indirect(entries), weights, ALU.mult)
        h0 = [tile([P, CHUNK * PACK], BF16, "h0_0"), laid_tile([P, CHUNK * PACK], BF16, "h0_1", H_AT[0])]
        relu0 = tile([P, PACK, CHUNK], F32, "relu0_0")
        for t, index in enumerate(FIRST_BANKS):
            nc.scalar.activation(relu0[:, t : t + 1, :], up_slices(0, 0, t, 1, index)[:], ACT.Relu)
        square0 = tile([P, CHUNK * PACK], F32, "square0_0")
        interleave(square0[:], relu0[:], ACT.Square)
        times_pattern(nc.gpsimd, h0[0][:], square0[:], sm_run[:])
        gates.append(tile([P, T], F32, "gates3", on="relu0_0"))
        nc.sync.dma_start(gates[3][:], gT[3 * P : 4 * P, :])
        h_abs = tile([P, CHUNK * PACK], BF16, "h_abs")
        interleave(h_abs[:], rectified_root()[:], ACT.Square)
        wd4 = tile([P, WD4_WORDS], I32, "wd4", on="relu0_1")
        nc.sync.dma_start(wd4[:], wd4_words[0].bitcast(I32))
        wd4_w = wd4[:].bitcast(U8)
        times_pattern(nc.vector, h0[1][:], h_abs[:], signs[:])
        for g in range(R_PASSES):
            nc.vector.quantize_mx(out=h_w[0][g].bitcast(FP8X4), scales=h_s[0][g], in_=h0[g][:])
        gather_weighted(2, 0, 3, on="h_abs")
        clear(3, laid_tile([P, T], F32, "page3", H_AT[0] - 6 * KIB))
        gather_weighted(3, 0, 2, wgo_first[3])
        gather_plain(3, 2, tile([P, 2 * CHUNK], F32, "picked3")[:])
        gather_plain(2, 3, laid_tile([P, CHUNK], F32, "picked2", 2 * KIB)[:])

        relu0 = tile([P, CHUNK * PACK], F32, "relu1_0")
        relu1 = tile([P, PACK, CHUNK], F32, "relu1_1")
        for c in range(LAST):
            d = c + 1
            rectified(d, relu1)
            rectified_interleaved(d, relu0)
            square1 = squared(d, 1, relu1)
            square0 = tile([P, CHUNK * PACK], F32, f"square{d}_0")
            ahead = (LAST - d) * BANK
            if ahead:
                nc.scalar.activation(square0[:, 0:ahead], relu0[:, 0:ahead], ACT.Square)
            if c == 0:
                scaled = [scale(square1, 0, tile([P, PACK, HALF], F32, "scaled1_0"))]
            down_products(c, N_PAGES if d < LAST else N_PAGES - 1)
            copy_y(c, 0, laid_tile([P, CHUNK], F32, f"y{c}_0", H_AT[d] + KIB))
            copy_y(c, 1)
            if c > 0:
                nc.scalar.activation(square0[:, ahead:], relu0[:, ahead:], ACT.Square)
            if c > 0:
                place(c - 1, 2)
                gate(c - 1, 3, laid_tile([P, CHUNK], F32, f"z{c - 1}_3", H_AT[c] + KIB), gw[c - 1, 3])
                place(c - 1, 3)
                parts, values = ([(1, 1)], early[:, 0:1, :]) if c == 1 else ([(2, 1), (3, 0)], early[:, 1::2, :])
                weigh(parts, values, laid_tile([P, c, CHUNK], F32, f"weighed{c}", H_AT[c] + 2 * KIB))
            for i in range(2):
                dst = tile([P, CHUNK], F32, f"z{c}_{i}") if c > 0 else laid_tile([P, CHUNK], F32, f"z0_{i}", i * KIB)
                gate(c, i, dst, gw[c, i])
                place(c, i)
            h[d] = laid_tile([P, R_PASSES, CHUNK * PACK], BF16, f"h{d}", H_AT[d])
            times_pattern(nc.gpsimd, h[d][:, 0, :], square0[:], sm_run[:])
            at = d * REGION + 3 * KIB
            if c == 0:
                scaled.append(scale(square1, HALF, laid_tile([P, PACK, HALF], F32, "scaled1_1", at + KIB // 2)))
            elif d < LAST:
                scaled = [scale(square1, 0, laid_tile([P, PACK, CHUNK], F32, f"scaled{d}", at))]
            else:
                both = laid_tile([P, 2, PACK, HALF], F32, f"scaled{d}", at)
                scaled = [scale(square1, k * HALF, both[:, k]) for k in range(2)]
            if d < LAST:
                copy_y(c, 2)
            width = CHUNK * PACK // len(scaled)
            for k, piece in enumerate(scaled):
                interleave(h[d][:, 1, k * width : (k + 1) * width], piece[:], ACT.Copy)
            if d < LAST:
                copy_y(c, 3)
            quantise(d)
            behind = laid_tile([P, CHUNK], F32, f"behind{d}", d * REGION + 4 * KIB)
            if d < LAST:
                gate(c, 2, behind, gw[c, 2])
                relu0 = laid_tile([P, CHUNK * PACK], F32, f"relu{d + 1}_0", d * REGION)
                relu1 = laid_tile([P, PACK, CHUNK], F32, f"relu{d + 1}_1", d * REGION + 5 * KIB)
            else:
                copy_y(c, 2, behind)
                scatter(c, 1, 2, behind[:], gw[c, 2])

        y_both = tile([P, 2 * CHUNK], F32, "y_both")
        turned = bank([P, LINE, P], 0, "turned")
        for b in range(LINE):
            nc.tensor.transpose(turned[:, b, :], wgo_sb[:, J // 2 + b * P : J // 2 + (b + 1) * P], identity[:])
        wgo_column = laid_tile([P, LINE], F32, "wgo_column", LAST * REGION + 6 * KIB)
        nc.scalar.copy(wgo_column[:], turned[:, :, 0])
        waiting = token_major(LAST - 1, 3, (7, 3), laid_tile([P, 2, P], F32, "flat2_3", LAST * REGION + 5 * KIB))
        down_products(LAST, 1)
        copy_y(LAST, 0)
        scatter(LAST, 1, 0, y[LAST, 0][:], gw[LAST, 0])
        weighted = [tile([P, CHUNK], F32, f"weighted{i}") for i in range(2)]
        turn_back(token_major(LAST, 1, (0, 1)), 2, weighted[0][:])
        scatter(LAST, 1, 1, weighted[0][:], picked[1][:, tokens(2)])
        turn_back(token_major(LAST, 2, (5, 6)), 0, weighted[1][:])
        scatter(LAST, 1, 2, weighted[1][:], picked[2])
        turn_back(waiting, 2, y_both[:, tokens(0)])
        turn_back(token_major(LAST, 3, (2, 0)), 1, y_both[:, tokens(1)])
        scatter(LAST - 1, 2, 3, y_both[:], picked[3])
